import numpy as np
import ml_dtypes


def mxq(x, axis, fmt="e4m3"):
    dtype, down = {"e4m3": (ml_dtypes.float8_e4m3fn, 7), "e5m2": (ml_dtypes.float8_e5m2, 14)}[fmt]
    v = np.moveaxis(np.asarray(x, np.float32).astype(ml_dtypes.bfloat16).astype(np.float64), axis, -1)
    blocks = v.reshape(v.shape[:-1] + (-1, 32))
    amax = np.abs(blocks).max(-1, keepdims=True)
    byte = np.maximum(np.where(amax > 0, np.frexp(amax)[1] - 1 + 127, 0) - down, 1)
    scale = np.exp2(byte - 127.0)
    codes = (blocks / scale).astype(np.float32).astype(dtype).astype(np.float64)
    return np.moveaxis((codes * scale).reshape(v.shape), -1, axis)


WIDE = False


def mx_kscale(k):
    if not WIDE:
        return np.ones(k)
    levels = np.array([10, -10, 5, -5, 0])
    if k % 512:
        return np.exp2(np.random.permutation(np.resize(levels, k // 32))).repeat(32)
    a = np.empty((k // 512, 16))
    for p in range(k // 512):
        a[p, :8] = np.random.permutation(np.resize(levels, 8))
        for g in range(8):
            far = levels[np.abs(levels - a[p, g]) >= 10]
            a[p, g + 8] = far[np.random.randint(len(far))]
    return np.exp2(a.ravel()).repeat(32)


BF16 = ml_dtypes.bfloat16


def bf(x):
    return np.asarray(x, np.float32).astype(BF16)


def f64(x):
    return np.asarray(x).astype(np.float64)


E2M1 = np.array([0.0, 0.5, 1.0, 1.5, 2.0, 3.0, 4.0, 6.0, -0.0, -0.5, -1.0, -1.5, -2.0, -3.0, -4.0, -6.0])


def pack_weight(w, fmt):
    k, n = w.shape
    w = f64(bf(w)).reshape(k // 32, 32, n)
    amax = np.abs(w).max(1)
    if fmt == "e4m3":
        byte = np.frexp(amax)[1] - 1 + 127 - 7
    else:
        mant, ex = np.frexp(amax / 6.0)
        byte = np.where(mant > 0.5, ex, ex - 1) + 127
    byte = np.clip(np.where(amax > 0, byte, 1), 1, 254)
    scaled = (w * np.exp2(127.0 - byte)[:, None, :]).reshape(k, n).astype(np.float32)
    by_word = np.ascontiguousarray(scaled.reshape(k // 512, 128, 4, n).transpose(0, 1, 3, 2))
    if fmt == "e4m3":
        words = by_word.astype(ml_dtypes.float8_e4m3fn).view(np.uint8)
    else:
        c = by_word.astype(ml_dtypes.float4_e2m1fn).view(np.uint8) & 0xF
        words = c[..., 0::2] | (c[..., 1::2] << 4)
    return np.ascontiguousarray(words), np.ascontiguousarray(byte.astype(np.uint8).reshape(k // 512, 16, n))


def unpack_weight(words, scales, fmt):
    g, p, n, _ = words.shape
    if fmt == "e4m3":
        vals = np.ascontiguousarray(words).view(ml_dtypes.float8_e4m3fn).astype(np.float64)
    else:
        nib = np.empty((g, p, n, 4), np.uint8)
        nib[..., 0::2] = words & 0xF
        nib[..., 1::2] = words >> 4
        vals = E2M1[nib]
    vals = vals * np.repeat(np.exp2(scales.astype(np.float64) - 127.0), 8, axis=1)[..., None]
    return vals.transpose(0, 1, 3, 2).reshape(g * 512, n)
def pack4(w):
    words, scales = pack_weight(w, "e2m1")
    return words.reshape(words.shape[0], 128, -1), scales


def unpack4(words, scales):
    return unpack_weight(words.reshape(words.shape[0], 128, -1, 2), scales, "e2m1")


def planes(Y):
    n, m = Y.shape
    b = f64(bf(Y)).reshape(n // 32, 32, m)
    amax = np.abs(b).max(1)
    byte = np.clip(np.where(amax > 0, np.frexp(amax)[1] - 1 + 127 - 7, 1), 1, 254)
    codes = (b * np.exp2(127.0 - byte)[:, None, :]).reshape(n, m).astype(np.float32).astype(ml_dtypes.float8_e4m3fn).view(np.uint8)
    words = codes.reshape(n // 512, 128, 4, m).transpose(0, 1, 3, 2)
    return np.ascontiguousarray(words), np.ascontiguousarray(byte.astype(np.uint8).reshape(n // 512, 16, m))


R, C, S, D, F, N = 512, 256, 4, 4096, 1024, 1024

def setup_inputs():
    s = mx_kscale(D)
    t = mx_kscale(F)
    roi = bf(np.random.randn(R, D) * s[None, :]).reshape(R, C, S, S)
    w1 = np.random.randn(D, F) * np.sqrt(2.0 / D) / s[:, None] * t[None, :]
    b1 = bf(0.4 * np.random.randn(F) * t)
    w2 = np.random.randn(F, N) * np.sqrt(2.0 / F) / t[:, None]
    b2 = bf(0.4 * np.random.randn(N))
    shift = bf(0.5 * np.random.randn(N))
    gain = bf(np.exp(0.7 * np.random.randn(N)))
    w1_words, w1_scales = pack4(w1)
    w2_words, w2_scales = pack4(w2)
    return {"roi": roi, "w1_words": w1_words, "w1_scales": w1_scales, "b1": b1,
            "w2_words": w2_words, "w2_scales": w2_scales, "b2": b2,
            "shift": shift, "gain": gain}

def reference(roi, w1_words, w1_scales, b1, w2_words, w2_scales, b2, shift, gain):
    w1 = unpack4(w1_words, w1_scales)
    w2 = unpack4(w2_words, w2_scales)
    xq = mxq(f64(roi).reshape(R, D), 1, "e4m3")
    h = np.maximum((xq @ w1) + f64(b1), 0.0)
    hq = mxq(h, 1, "e4m3")
    a = np.maximum((hq @ w2) + f64(b2), 0.0)
    y = (a + f64(shift)) * f64(gain)
    words, scales = planes(y.T)
    return y, words, scales

@@ -1,0 +1,459 @@
+from contextlib import ExitStack
+
+import concourse.mybir as mybir
+from concourse.masks import make_identity
+
+R, D, F, N = 512, 4096, 1024, 1024
+FLOPS = 2 * R * D * F + 2 * R * F * N
+
+F32 = mybir.dt.float32
+BF16 = mybir.dt.bfloat16
+U32 = mybir.dt.uint32
+I32 = mybir.dt.int32
+U8 = mybir.dt.uint8
+FP8X4 = mybir.dt.float8_e4m3fn_x4
+FP4X4 = mybir.dt.float4_e2m1fn_x4
+ALU = mybir.AluOpType
+ACT = mybir.ActivationFunctionType
+
+P = 128
+SORTED = [(1, 0), (1, 1), (2, 0), (2, 1), (3, 0), (3, 1)]
+
+
+def tile_box_head_region_features_h1_kernel(
+    tc, roi, w1_words, w1_scales, b1, w2_words, w2_scales, b2, shift, gain, out_0, out_1, out_2
+):
+    nc = tc.nc
+    x = roi.rearrange("r c a b -> r (c a b)")
+    w1_i, s1_i = w1_words.bitcast(I32), w1_scales.bitcast(I32)
+    w2_i, s2_i = w2_words.bitcast(I32), w2_scales.bitcast(I32)
+    codes_out = out_1.rearrange("g p m t -> p g (m t)").bitcast(I32)
+    scales_out = out_2.bitcast(I32)
+
+    with ExitStack() as ctx:
+        sb = ctx.enter_context(tc.tile_pool(name="sb", bufs=1))
+        ps = ctx.enter_context(tc.psum_pool(name="ps", bufs=1))
+        ctx.enter_context(tc.manual_schedule())
+
+        def tile(name, shape, dtype):
+            return sb.tile(shape, dtype, name=name, align_bytes=64)
+
+        bank = [ps.tile([P, 512], F32, name="bank%d" % i) for i in range(8)]
+        ident = tile("ident", [P, P], F32)
+        warm = tile("warm", [P, 16], F32)
+        vec = {k: tile("vec_" + k, [P, 2, 4], BF16) for k in ("b1", "b2", "shift", "gain")}
+        b1_rows = tile("b1_rows", [P, 1024], BF16)
+        x_raw = {(gp, rt): tile("x_raw%d_%d" % (gp, rt), [P, 1024], BF16) for gp in range(1) for rt in range(2)}
+        x_pair = {(gp, tp): tile("x_pair%d_%d" % (gp, tp), [P, 2, 1024], BF16) for gp in range(4) for tp in range(2) if (gp, tp) != (0, 0)}
+        for (gp, tp), t in x_pair.items():
+            for j in range(2):
+                x_raw[gp, 2 * tp + j] = t[:, j, :]
+        x_perm = [tile("x_perm%d" % i, [P, 512], F32) for i in range(8)]
+        x_grp = [tile("x_grp%d" % i, [P, 1024], BF16) for i in range(4)]
+        x_codes = {(gp, rt): tile("x_codes%d_%d" % (gp, rt), [P, 256], U32) for gp in range(4) for rt in range(4)}
+        x_scales = {(gp, rt): tile("x_scales%d_%d" % (gp, rt), [P, 256], U8) for gp in range(4) for rt in range(4)}
+        w1 = {(h, gp): tile("w1_%d_%d" % (h, gp), [P, 2, 1024], U8) for h in range(2) for gp in range(4)}
+        s1_parts = [(0, 0, 2), (0, 2, 8), (1, 0, 8)]
+        s1_tiles = [tile("s1_%d" % i, [P, g1 - g0, 512], U8) for i, (h, g0, g1) in enumerate(s1_parts)]
+        s1 = {(h, g): s1_tiles[i][:, g - g0, :] for i, (h, g0, g1) in enumerate(s1_parts) for g in range(g0, g1)}
+        w2_raw = tile("w2_raw", [P, 2, 2048], U8)
+        s2_raw = tile("s2_raw", [P, 2, 1024], U8)
+        w2 = tile("w2", [P, 2, 2048], U8)
+        s2 = tile("s2", [P, 2, 1024], U8)
+        h_pre = {(rt, h): tile("h_pre%d_%d" % (rt, h), [P, 512], BF16) for rt in range(4) for h in range(2)}
+        h_grp = {(rt, h): tile("h_grp%d_%d" % (rt, h), [P, 512], BF16) for rt in range(4) for h in range(2)}
+        h_codes = {(rt, h): tile("h_codes%d_%d" % (rt, h), [P, P], U32) for rt in range(4) for h in range(2)}
+        h_scales = {(rt, h): tile("h_scales%d_%d" % (rt, h), [P, P], U8) for rt in range(4) for h in range(2)}
+        a_t = [tile("a_t%d" % g, [P, 4, R], F32) for g in range(2)]
+        y_t = [tile("y_t%d" % g, [P, 4, R], F32) for g in range(2)]
+        y_grp = [tile("y_grp%d" % g, [P, R, 4], BF16) for g in range(2)]
+        y_codes = tile("y_codes", [P, 2, R], U32)
+        y_scales = tile("y_scales", [P, 2, R], U8)
+        y_out = {(rt, g): tile("y_out%d_%d" % (rt, g), [P, 512], F32) for rt in range(4) for g in range(2)}
+
+        def load_vec(eng, key, src):
+            eng.dma_start(out=vec[key][:], in_=src.rearrange("(g p t) -> p g t", g=2, t=4))
+
+        def load_x(gp, tp):
+            cols = slice(1024 * gp, 1024 * (gp + 1))
+            if (gp, tp) == (0, 0):
+                for rt in range(2):
+                    nc.sync.dma_start(out=x_raw[gp, rt][:], in_=x[P * rt : P * (rt + 1), cols])
+            else:
+                rows = x[256 * tp : 256 * (tp + 1), cols]
+                nc.sync.dma_start(out=x_pair[gp, tp][:], in_=rows.rearrange("(j r) k -> r j k", j=2))
+
+        def load_w1(h, gp):
+            src = w1_i[2 * gp : 2 * gp + 2, :, 256 * h : 256 * (h + 1)]
+            nc.sync.dma_start(out=w1[h, gp][:].bitcast(I32), in_=src.rearrange("g p n -> p g n"))
+
+        def load_s1(i):
+            h, g0, g1 = s1_parts[i]
+            for q in (0, 2, 1, 3):
+                src = s1_i[g0:g1, 4 * q : 4 * q + 4, 128 * h : 128 * (h + 1)]
+                nc.sync.dma_start(out=s1_tiles[i][32 * q : 32 * q + 4].bitcast(I32), in_=src.rearrange("g r n -> r g n"))
+
+        def load_w2():
+            nc.sync.dma_start(out=w2_raw[:].bitcast(I32), in_=w2_i.rearrange("g p n -> p g n"))
+
+        def load_s2():
+            for q in (0, 2, 1, 3):
+                src = s2_i[:, 4 * q : 4 * q + 4, :]
+                nc.sync.dma_start(out=s2_raw[32 * q : 32 * q + 4].bitcast(I32), in_=src.rearrange("g r n -> r g n"))
+
+        def x_sort(gp, rt):
+            nc.vector.tensor_copy(
+                out=x_perm[(4 * gp + rt) % 8][:].rearrange("r (g u m) -> r g u m", g=2, u=2),
+                in_=x_raw[gp, rt][:].bitcast(F32).rearrange("r (g m u) -> r g u m", g=2, u=2),
+            )
+
+        def x_turn(gp, rt, b):
+            words = x_raw[gp, rt][:].bitcast(F32)
+            for gg in range(2):
+                for u in range(2):
+                    c = 2 * gg + u
+                    if (gp, rt // 2) in SORTED:
+                        src = x_perm[(4 * gp + rt) % 8][:, P * c : P * (c + 1)]
+                    else:
+                        src = words[:, 256 * gg + u : 256 * (gg + 1) : 2]
+                    nc.tensor.transpose(bank[b][:, P * c : P * (c + 1)], src, ident[:])
+
+        def x_out(b):
+            nc.scalar.copy(
+                out=x_grp[b - 4][:].bitcast(F32).rearrange("p (g r u) -> p g r u", g=2, u=2),
+                in_=bank[b][:].rearrange("p (g u r) -> p g r u", g=2, u=2),
+            )
+
+        def x_quant(gp, rt, b):
+            nc.vector.quantize_mx(out=x_codes[gp, rt][:].bitcast(FP8X4), scales=x_scales[gp, rt][:], in_=x_grp[b - 4][:])
+
+        def mm1(rt, h, g, b):
+            cols = slice(P * (g % 2), P * (g % 2 + 1))
+            nc.tensor.matmul_mx(
+                out=bank[b][:],
+                lhsT=x_codes[g // 2, rt][:, cols].bitcast(FP8X4),
+                lhsT_scale=x_scales[g // 2, rt][:, cols],
+                rhs=w1[h, g // 2][:, g % 2, :].bitcast(FP4X4),
+                rhs_scale=s1[h, g],
+                start=(g == 0),
+                stop=(g == 7),
+            )
+
+        def w2_words_perm(g2, g):
+            cols = slice(1024 * g, 1024 * (g + 1))
+            nc.vector.tensor_copy(
+                out=w2[:, g2, cols].rearrange("p (t m b) -> p t m b", t=4, b=2),
+                in_=w2_raw[:, g2, cols].rearrange("p (m t b) -> p t m b", t=4, b=2),
+            )
+
+        def w2_scales_perm(g2):
+            nc.vector.tensor_copy(
+                out=s2[:, g2, :].rearrange("p (g t m) -> p g t m", g=2, t=4),
+                in_=s2_raw[:, g2, :].rearrange("p (g m t) -> p g t m", g=2, t=4),
+            )
+
+        def h_add(rt, h, b):
+            nc.vector.tensor_tensor(
+                out=h_pre[rt, h][:].rearrange("p (u m e) -> p u m e", u=2, e=2),
+                in0=bank[b][:].rearrange("p (m u e) -> p u m e", u=2, e=2),
+                in1=b1_rows[:, 512 * h : 512 * (h + 1)].rearrange("p (u m e) -> p u m e", u=2, e=2),
+                op=ALU.add,
+            )
+
+        def h_turn(rt, h, b, c):
+            words = h_pre[rt, h][:].bitcast(F32)
+            for u in range(2):
+                nc.tensor.transpose(bank[b][:, 256 * c + P * u : 256 * c + P * (u + 1)], words[:, P * u : P * (u + 1)], ident[:])
+
+        def h_out(rt, h, b, c, eng):
+            src = bank[b][:, 256 * c : 256 * (c + 1)].bitcast(BF16).rearrange("p (u r e) -> p r u e", u=2, e=2)
+            dst = h_grp[rt, h][:].rearrange("p (r u e) -> p r u e", u=2, e=2)
+            if eng == "S":
+                nc.scalar.activation(out=dst, in_=src, func=ACT.Relu)
+            else:
+                nc.vector.tensor_scalar(out=dst, in0=src, scalar1=0.0, scalar2=None, op0=ALU.max)
+
+        def h_quant(rt, h):
+            nc.vector.quantize_mx(out=h_codes[rt, h][:].bitcast(FP8X4), scales=h_scales[rt, h][:], in_=h_grp[rt, h][:])
+
+        def mm2(rt, g, t, b, c):
+            for g2 in range(2):
+                col = 512 * g + P * t
+                nc.tensor.matmul_mx(
+                    out=bank[b][:, P * c : P * (c + 1)],
+                    lhsT=w2[:, g2, 2 * col : 2 * (col + P)].bitcast(FP4X4),
+                    lhsT_scale=s2[:, g2, col : col + P],
+                    rhs=h_codes[rt, g2][:].bitcast(FP8X4),
+                    rhs_scale=h_scales[rt, g2][:],
+                    start=(g2 == 0),
+                    stop=(g2 == 1),
+                )
+
+        def y_relu(r0, n, g, t, b, c, eng):
+            src = bank[b][:, P * c : P * (c + n)]
+            dst = a_t[g][:, t, P * r0 : P * (r0 + n)]
+            bias = vec["b2"][:, g, t : t + 1]
+            if eng == "S":
+                nc.scalar.activation(out=dst, in_=src, func=ACT.Relu, bias=bias)
+            else:
+                nc.vector.tensor_scalar(out=dst, in0=src, scalar1=bias, scalar2=0.0, op0=ALU.add, op1=ALU.max)
+
+        def y_affine(r0, n, g, t):
+            cols = slice(P * r0, P * (r0 + n))
+            nc.vector.tensor_scalar(
+                out=y_t[g][:, t, cols], in0=a_t[g][:, t, cols],
+                scalar1=vec["shift"][:, g, t : t + 1], scalar2=vec["gain"][:, g, t : t + 1],
+                op0=ALU.add, op1=ALU.mult,
+            )
+
+        def y_group(r0, n, g, eng):
+            cols = slice(P * r0, P * (r0 + n))
+            copy = nc.scalar.copy if eng == "S" else nc.vector.tensor_copy
+            copy(out=y_grp[g][:, cols, :], in_=y_t[g][:, :, cols].rearrange("p t r -> p r t"))
+
+        def y_quant(r0, n, g):
+            cols = slice(P * r0, P * (r0 + n))
+            nc.vector.quantize_mx(
+                out=y_codes[:, g, cols].bitcast(FP8X4), scales=y_scales[:, g, cols],
+                in_=y_grp[g][:, cols, :].rearrange("p r t -> p (r t)"),
+            )
+
+        def y_turn(rt, g, b):
+            for t in range(4):
+                nc.tensor.transpose(bank[b][:, P * t : P * (t + 1)], y_t[g][:, t, P * rt : P * (rt + 1)], ident[:])
+
+        def y_copy(rt, g, b, eng):
+            copy = nc.scalar.copy if eng == "S" else nc.vector.tensor_copy
+            copy(out=y_out[rt, g][:].rearrange("r (p t) -> r p t", t=4), in_=bank[b][:].rearrange("r (t p) -> r p t", t=4))
+
+        def y_store(rt, g, queue):
+            queue.dma_start(out=out_0[P * rt : P * (rt + 1), 512 * g : 512 * (g + 1)], in_=y_out[rt, g][:])
+
+        def store_codes(r0, n):
+            cols = slice(P * r0, P * (r0 + n))
+            nc.sync.dma_start(out=codes_out[:, :, cols], in_=y_codes[:, :, cols].bitcast(I32))
+
+        def store_scales(queue):
+            for q in range(4):
+                dst = scales_out[:, 4 * q : 4 * q + 4, :].rearrange("g r n -> r g n")
+                queue.dma_start(out=dst, in_=y_scales[32 * q : 32 * q + 4].bitcast(I32))
+
+        load_vec(nc.scalar, "b1", b1)
+        make_identity(nc, ident[:])
+        nc.vector.memset(s1_tiles[0][:].bitcast(I32), 0)
+        nc.vector.memset(warm[:, 0:8], 0.0)
+        for t in s1_tiles[1:] + [s2_raw]:
+            nc.vector.memset(t[:].bitcast(I32), 0)
+        nc.scalar.activation(out=warm[:, 8:16], in_=warm[:, 0:8], func=ACT.Relu)
+
+        load_x(0, 0)
+        load_x(0, 1)
+        load_s1(0)
+        load_w1(0, 0)
+        load_x(1, 0)
+        load_x(1, 1)
+        load_s1(1)
+        load_w1(0, 1)
+        load_x(2, 0)
+        load_x(2, 1)
+        load_w1(0, 2)
+        load_x(3, 0)
+        load_x(3, 1)
+        load_w1(0, 3)
+        load_w2()
+        load_s1(2)
+        load_w1(1, 0)
+        load_w1(1, 1)
+        load_w1(1, 2)
+        load_w1(1, 3)
+        load_s2()
+        load_vec(nc.sync, "b2", b2)
+        load_vec(nc.sync, "shift", shift)
+        load_vec(nc.sync, "gain", gain)
+
+        b1_words = vec["b1"][:].rearrange("p g t -> p (g t)").bitcast(F32)
+        for c in range(4):
+            nc.tensor.transpose(bank[7][:, P * c : P * (c + 1)], b1_words[:, c : c + 1].to_broadcast([P, P]), ident[:])
+        nc.vector.tensor_copy(out=b1_rows[:].bitcast(F32), in_=bank[7][:])
+
+        def sort(gp, tp):
+            if (gp, tp) in SORTED:
+                for j in range(2):
+                    x_sort(gp, 2 * tp + j)
+
+        def turn(gp, tp):
+            for j in range(2):
+                x_turn(gp, 2 * tp + j, 4 + 2 * tp + j)
+                x_out(4 + 2 * tp + j)
+
+        def quant(gp, tp):
+            for j in range(2):
+                x_quant(gp, 2 * tp + j, 4 + 2 * tp + j)
+
+        def mm_a(gp, tp):
+            for j in range(2):
+                for gg in range(2):
+                    mm1(2 * tp + j, 0, 2 * gp + gg, 2 * tp + j)
+
+        def mm_b(rt, b):
+            for g in range(8):
+                mm1(rt, 1, g, b)
+
+        def mm2_tile(rt, g, b):
+            for t in range(4):
+                mm2(rt, g, t, b, t)
+
+        def mm2_half(rt, g, tp, b):
+            for t in range(2):
+                mm2(rt, g, 2 * tp + t, b, t)
+
+        def y_act_half(rt, g, tp, b, eng):
+            for t in range(2):
+                y_relu(rt, 1, g, 2 * tp + t, b, t, eng)
+
+        def y_aff_half(rt, g, tp):
+            for t in range(2):
+                y_affine(rt, 1, g, 2 * tp + t)
+
+        def y_act(rt, g, b, eng):
+            for t in range(4):
+                y_relu(rt, 1, g, t, b, t, eng)
+
+        def y_aff(rt, g):
+            for t in range(4):
+                y_affine(rt, 1, g, t)
+
+        turn(0, 0)
+        quant(0, 0)
+        turn(0, 1)
+        mm_a(0, 0)
+        quant(0, 1)
+        sort(1, 0)
+        sort(1, 1)
+        for gp in range(1, 4):
+            turn(gp, 0)
+            turn(gp, 1)
+            quant(gp, 0)
+            if gp < 3:
+                sort(gp + 1, 0)
+            mm_a(gp - 1, 1)
+            mm_a(gp, 0)
+            quant(gp, 1)
+            if gp < 3:
+                sort(gp + 1, 1)
+            if gp == 2:
+                w2_words_perm(0, 0)
+        mm_a(3, 1)
+
+        w2_words_perm(1, 0)
+        h_add(0, 0, 0)
+        h_add(1, 0, 1)
+        h_add(2, 0, 2)
+        h_add(3, 0, 3)
+        mm_b(0, 4)
+        w2_words_perm(0, 1)
+        h_add(0, 1, 4)
+        h_turn(0, 0, 5, 0)
+        h_turn(1, 0, 5, 1)
+        h_turn(2, 0, 7, 0)
+        h_turn(3, 0, 7, 1)
+        h_turn(0, 1, 0, 0)
+        h_out(0, 0, 5, 0, "S")
+        h_out(0, 1, 0, 0, "S")
+        h_out(1, 0, 5, 1, "S")
+        h_out(2, 0, 7, 0, "S")
+        h_out(3, 0, 7, 1, "S")
+        w2_scales_perm(0)
+        h_quant(0, 0)
+        w2_scales_perm(1)
+        h_quant(0, 1)
+        mm_b(1, 6)
+        w2_words_perm(1, 1)
+        h_quant(1, 0)
+        h_add(1, 1, 6)
+        h_quant(2, 0)
+        h_quant(3, 0)
+        mm2_tile(0, 0, 1)
+        y_act(0, 0, 1, "S")
+        mm2_tile(0, 1, 2)
+        y_act(0, 1, 2, "S")
+        h_turn(1, 1, 3, 0)
+        y_aff(0, 0)
+        h_out(1, 1, 3, 0, "V")
+        y_aff(0, 1)
+        h_quant(1, 1)
+        mm_b(2, 4)
+        y_group(0, 1, 0, "V")
+        y_group(0, 1, 1, "V")
+        y_quant(0, 1, 0)
+        y_quant(0, 1, 1)
+        h_add(2, 1, 4)
+        y_turn(0, 0, 0)
+        y_turn(0, 1, 7)
+        h_turn(2, 1, 6, 0)
+        y_copy(0, 0, 0, "S")
+        y_store(0, 0, nc.sync)
+        y_copy(0, 1, 7, "S")
+        y_store(0, 1, nc.sync)
+        h_out(2, 1, 6, 0, "V")
+        mm2_tile(1, 0, 5)
+        y_act(1, 0, 5, "S")
+        mm2_tile(1, 1, 1)
+        y_act(1, 1, 1, "S")
+        h_quant(2, 1)
+        y_aff(1, 0)
+        y_aff(1, 1)
+        mm_b(3, 2)
+        y_group(1, 1, 0, "V")
+        y_group(1, 1, 1, "V")
+        y_quant(1, 1, 0)
+        y_quant(1, 1, 1)
+        store_codes(0, 2)
+        h_add(3, 1, 2)
+        y_turn(1, 0, 3)
+        y_turn(1, 1, 4)
+        h_turn(3, 1, 0, 0)
+        y_copy(1, 0, 3, "S")
+        y_store(1, 0, nc.sync)
+        y_copy(1, 1, 4, "S")
+        y_store(1, 1, nc.sync)
+        h_out(3, 1, 0, 0, "V")
+        mm2_tile(2, 0, 6)
+        mm2_tile(2, 1, 7)
+        h_quant(3, 1)
+        y_act(2, 0, 6, "S")
+        y_act(2, 1, 7, "V")
+        y_aff(2, 0)
+        y_aff(2, 1)
+        mm2_half(3, 0, 0, 5)
+        mm2_half(3, 0, 1, 1)
+        mm2_half(3, 1, 0, 2)
+        mm2_half(3, 1, 1, 3)
+        y_turn(2, 0, 4)
+        y_turn(2, 1, 0)
+        y_act_half(3, 0, 0, 5, "S")
+        y_act_half(3, 0, 1, 1, "S")
+        y_act_half(3, 1, 0, 2, "S")
+        y_act_half(3, 1, 1, 3, "S")
+        y_group(2, 1, 0, "V")
+        y_aff(3, 0)
+        y_group(2, 1, 1, "V")
+        y_aff(3, 1)
+        y_turn(3, 0, 6)
+        y_turn(3, 1, 7)
+        y_copy(2, 0, 4, "S")
+        y_store(2, 0, nc.sync)
+        y_copy(2, 1, 0, "S")
+        y_store(2, 1, nc.sync)
+        y_quant(2, 1, 0)
+        y_group(3, 1, 0, "V")
+        y_quant(2, 1, 1)
+        y_group(3, 1, 1, "V")
+        y_quant(3, 1, 0)
+        y_quant(3, 1, 1)
+        y_copy(3, 0, 6, "S")
+        y_store(3, 0, nc.sync)
+        y_copy(3, 1, 7, "S")
+        y_store(3, 1, nc.scalar)
+        store_codes(2, 2)
+        store_scales(nc.sync)

@@ -17,7 +17,6 @@ ALU = mybir.AluOpType
 ACT = mybir.ActivationFunctionType
 
 P = 128
-SORTED = [(1, 0), (1, 1), (2, 0), (2, 1), (3, 0), (3, 1)]
 
 
 def tile_box_head_region_features_h1_kernel(
@@ -43,13 +42,12 @@ def tile_box_head_region_features_h1_kernel(
         warm = tile("warm", [P, 16], F32)
         vec = {k: tile("vec_" + k, [P, 2, 4], BF16) for k in ("b1", "b2", "shift", "gain")}
         b1_rows = tile("b1_rows", [P, 1024], BF16)
-        x_raw = {(gp, rt): tile("x_raw%d_%d" % (gp, rt), [P, 1024], BF16) for gp in range(1) for rt in range(2)}
-        x_pair = {(gp, tp): tile("x_pair%d_%d" % (gp, tp), [P, 2, 1024], BF16) for gp in range(4) for tp in range(2) if (gp, tp) != (0, 0)}
-        for (gp, tp), t in x_pair.items():
-            for j in range(2):
-                x_raw[gp, 2 * tp + j] = t[:, j, :]
-        x_perm = [tile("x_perm%d" % i, [P, 512], F32) for i in range(8)]
-        x_grp = [tile("x_grp%d" % i, [P, 1024], BF16) for i in range(4)]
+        x_raw = {(gp, rt): tile("x_raw%d_%d" % (gp, rt), [P, 1024], BF16) for gp in range(4) for rt in range(4)}
+        x_perm = {(gp, rt): tile("x_perm%d_%d" % (gp, rt), [P, 512], F32) for gp in range(4) for rt in range(4)}
+        zero = tile("zero", [P, 2048], BF16)
+        zero_codes = tile("zero_codes", [P, 512], U32)
+        zero_scales = tile("zero_scales", [P, 512], U8)
+        w_warm = tile("w_warm", [P, 256], U8)
         x_codes = {(gp, rt): tile("x_codes%d_%d" % (gp, rt), [P, 256], U32) for gp in range(4) for rt in range(4)}
         x_scales = {(gp, rt): tile("x_scales%d_%d" % (gp, rt), [P, 256], U8) for gp in range(4) for rt in range(4)}
         w1 = {(h, gp): tile("w1_%d_%d" % (h, gp), [P, 2, 1024], U8) for h in range(2) for gp in range(4)}
@@ -69,19 +67,40 @@ def tile_box_head_region_features_h1_kernel(
         y_grp = [tile("y_grp%d" % g, [P, R, 4], BF16) for g in range(2)]
         y_codes = tile("y_codes", [P, 2, R], U32)
         y_scales = tile("y_scales", [P, 2, R], U8)
-        y_out = {(rt, g): tile("y_out%d_%d" % (rt, g), [P, 512], F32) for rt in range(4) for g in range(2)}
+        y_rows = [tile("y_rows%d" % rt, [P, 1024], F32) for rt in range(4)]
+        y_out = {(rt, g): y_rows[rt][:, 512 * g : 512 * (g + 1)] for rt in range(4) for g in range(2)}
 
         def load_vec(eng, key, src):
             eng.dma_start(out=vec[key][:], in_=src.rearrange("(g p t) -> p g t", g=2, t=4))
 
-        def load_x(gp, tp):
-            cols = slice(1024 * gp, 1024 * (gp + 1))
-            if (gp, tp) == (0, 0):
-                for rt in range(2):
-                    nc.sync.dma_start(out=x_raw[gp, rt][:], in_=x[P * rt : P * (rt + 1), cols])
-            else:
-                rows = x[256 * tp : 256 * (tp + 1), cols]
-                nc.sync.dma_start(out=x_pair[gp, tp][:], in_=rows.rearrange("(j r) k -> r j k", j=2))
+        def load_x(gp, rt):
+            nc.sync.dma_start(out=x_raw[gp, rt][:], in_=x[P * rt : P * (rt + 1), 1024 * gp : 1024 * (gp + 1)])
+
+        def load_vecs():
+            load_vec(nc.sync, "b2", b2)
+            load_vec(nc.sync, "shift", shift)
+            load_vec(nc.sync, "gain", gain)
+
+        def memset_plane(t):
+            nc.vector.memset(t[:].bitcast(I32), 0)
+
+        def copy_on(eng):
+            return nc.scalar.copy if eng == "S" else nc.vector.tensor_copy
+
+        def warm_up(b):
+            for i in range(2):
+                nc.tensor.matmul_mx(
+                    out=bank[b][:], lhsT=w_warm[:].bitcast(FP4X4), lhsT_scale=zero_scales[:, 0:P],
+                    rhs=zero_codes[:].bitcast(FP8X4), rhs_scale=zero_scales[:], start=True, stop=True,
+                )
+
+        def b1_turn(b):
+            b1_words = vec["b1"][:].rearrange("p g t -> p (g t)").bitcast(F32)
+            for c in range(4):
+                nc.tensor.transpose(bank[b][:, P * c : P * (c + 1)], b1_words[:, c : c + 1].to_broadcast([P, P]), ident[:])
+
+        def b1_out(b, eng):
+            copy_on(eng)(out=b1_rows[:].bitcast(F32), in_=bank[b][:])
 
         def load_w1(h, gp):
             src = w1_i[2 * gp : 2 * gp + 2, :, 256 * h : 256 * (h + 1)]
@@ -103,29 +122,33 @@ def tile_box_head_region_features_h1_kernel(
 
         def x_sort(gp, rt):
             nc.vector.tensor_copy(
-                out=x_perm[(4 * gp + rt) % 8][:].rearrange("r (g u m) -> r g u m", g=2, u=2),
+                out=x_perm[gp, rt][:].rearrange("r (g u m) -> r g u m", g=2, u=2),
                 in_=x_raw[gp, rt][:].bitcast(F32).rearrange("r (g m u) -> r g u m", g=2, u=2),
             )
 
-        def x_turn(gp, rt, b):
+        def x_turn(gp, rt, b, is_sorted):
             words = x_raw[gp, rt][:].bitcast(F32)
             for gg in range(2):
                 for u in range(2):
                     c = 2 * gg + u
-                    if (gp, rt // 2) in SORTED:
-                        src = x_perm[(4 * gp + rt) % 8][:, P * c : P * (c + 1)]
+                    if is_sorted:
+                        src = x_perm[gp, rt][:, P * c : P * (c + 1)]
                     else:
                         src = words[:, 256 * gg + u : 256 * (gg + 1) : 2]
                     nc.tensor.transpose(bank[b][:, P * c : P * (c + 1)], src, ident[:])
 
-        def x_out(b):
-            nc.scalar.copy(
-                out=x_grp[b - 4][:].bitcast(F32).rearrange("p (g r u) -> p g r u", g=2, u=2),
+        def x_out(gp, rt, b, eng):
+            copy_on(eng)(
+                out=x_raw[gp, rt][:].bitcast(F32).rearrange("p (g r u) -> p g r u", g=2, u=2),
                 in_=bank[b][:].rearrange("p (g u r) -> p g r u", g=2, u=2),
             )
 
-        def x_quant(gp, rt, b):
-            nc.vector.quantize_mx(out=x_codes[gp, rt][:].bitcast(FP8X4), scales=x_scales[gp, rt][:], in_=x_grp[b - 4][:])
+        def x_quant(gp, rt):
+            nc.vector.quantize_mx(out=x_codes[gp, rt][:].bitcast(FP8X4), scales=x_scales[gp, rt][:], in_=x_raw[gp, rt][:])
+
+        def mm1_pair(rt, h, gp, b):
+            mm1(rt, h, 2 * gp, b)
+            mm1(rt, h, 2 * gp + 1, b)
 
         def mm1(rt, h, g, b):
             cols = slice(P * (g % 2), P * (g % 2 + 1))
@@ -152,21 +175,20 @@ def tile_box_head_region_features_h1_kernel(
                 in_=s2_raw[:, g2, :].rearrange("p (g m t) -> p g t m", g=2, t=4),
             )
 
-        def h_add(rt, h, b):
+        def h_add(rt, h, u, b):
             nc.vector.tensor_tensor(
-                out=h_pre[rt, h][:].rearrange("p (u m e) -> p u m e", u=2, e=2),
-                in0=bank[b][:].rearrange("p (m u e) -> p u m e", u=2, e=2),
-                in1=b1_rows[:, 512 * h : 512 * (h + 1)].rearrange("p (u m e) -> p u m e", u=2, e=2),
+                out=h_pre[rt, h][:, 256 * u : 256 * (u + 1)].rearrange("p (m e) -> p m e", e=2),
+                in0=bank[b][:].rearrange("p (m u e) -> p u m e", u=2, e=2)[:, u],
+                in1=b1_rows[:, 512 * h + 256 * u : 512 * h + 256 * (u + 1)].rearrange("p (m e) -> p m e", e=2),
                 op=ALU.add,
             )
 
-        def h_turn(rt, h, b, c):
+        def h_turn(rt, h, u, b):
             words = h_pre[rt, h][:].bitcast(F32)
-            for u in range(2):
-                nc.tensor.transpose(bank[b][:, 256 * c + P * u : 256 * c + P * (u + 1)], words[:, P * u : P * (u + 1)], ident[:])
+            nc.tensor.transpose(bank[b][:, P * u : P * (u + 1)], words[:, P * u : P * (u + 1)], ident[:])
 
-        def h_out(rt, h, b, c, eng):
-            src = bank[b][:, 256 * c : 256 * (c + 1)].bitcast(BF16).rearrange("p (u r e) -> p r u e", u=2, e=2)
+        def h_out(rt, h, b, eng):
+            src = bank[b][:, 0:256].bitcast(BF16).rearrange("p (u r e) -> p r u e", u=2, e=2)
             dst = h_grp[rt, h][:].rearrange("p (r u e) -> p r u e", u=2, e=2)
             if eng == "S":
                 nc.scalar.activation(out=dst, in_=src, func=ACT.Relu)
@@ -229,6 +251,9 @@ def tile_box_head_region_features_h1_kernel(
         def y_store(rt, g, queue):
             queue.dma_start(out=out_0[P * rt : P * (rt + 1), 512 * g : 512 * (g + 1)], in_=y_out[rt, g][:])
 
+        def y_store_tile(rt):
+            nc.sync.dma_start(out=out_0[P * rt : P * (rt + 1), :], in_=y_rows[rt][:])
+
         def store_codes(r0, n):
             cols = slice(P * r0, P * (r0 + n))
             nc.sync.dma_start(out=codes_out[:, :, cols], in_=y_codes[:, :, cols].bitcast(I32))
@@ -237,71 +262,6 @@ def tile_box_head_region_features_h1_kernel(
             for q in range(4):
                 dst = scales_out[:, 4 * q : 4 * q + 4, :].rearrange("g r n -> r g n")
                 queue.dma_start(out=dst, in_=y_scales[32 * q : 32 * q + 4].bitcast(I32))
-
-        load_vec(nc.scalar, "b1", b1)
-        make_identity(nc, ident[:])
-        nc.vector.memset(s1_tiles[0][:].bitcast(I32), 0)
-        nc.vector.memset(warm[:, 0:8], 0.0)
-        for t in s1_tiles[1:] + [s2_raw]:
-            nc.vector.memset(t[:].bitcast(I32), 0)
-        nc.scalar.activation(out=warm[:, 8:16], in_=warm[:, 0:8], func=ACT.Relu)
-
-        load_x(0, 0)
-        load_x(0, 1)
-        load_s1(0)
-        load_w1(0, 0)
-        load_x(1, 0)
-        load_x(1, 1)
-        load_s1(1)
-        load_w1(0, 1)
-        load_x(2, 0)
-        load_x(2, 1)
-        load_w1(0, 2)
-        load_x(3, 0)
-        load_x(3, 1)
-        load_w1(0, 3)
-        load_w2()
-        load_s1(2)
-        load_w1(1, 0)
-        load_w1(1, 1)
-        load_w1(1, 2)
-        load_w1(1, 3)
-        load_s2()
-        load_vec(nc.sync, "b2", b2)
-        load_vec(nc.sync, "shift", shift)
-        load_vec(nc.sync, "gain", gain)
-
-        b1_words = vec["b1"][:].rearrange("p g t -> p (g t)").bitcast(F32)
-        for c in range(4):
-            nc.tensor.transpose(bank[7][:, P * c : P * (c + 1)], b1_words[:, c : c + 1].to_broadcast([P, P]), ident[:])
-        nc.vector.tensor_copy(out=b1_rows[:].bitcast(F32), in_=bank[7][:])
-
-        def sort(gp, tp):
-            if (gp, tp) in SORTED:
-                for j in range(2):
-                    x_sort(gp, 2 * tp + j)
-
-        def turn(gp, tp):
-            for j in range(2):
-                x_turn(gp, 2 * tp + j, 4 + 2 * tp + j)
-                x_out(4 + 2 * tp + j)
-
-        def quant(gp, tp):
-            for j in range(2):
-                x_quant(gp, 2 * tp + j, 4 + 2 * tp + j)
-
-        def mm_a(gp, tp):
-            for j in range(2):
-                for gg in range(2):
-                    mm1(2 * tp + j, 0, 2 * gp + gg, 2 * tp + j)
-
-        def mm_b(rt, b):
-            for g in range(8):
-                mm1(rt, 1, g, b)
-
-        def mm2_tile(rt, g, b):
-            for t in range(4):
-                mm2(rt, g, t, b, t)
 
         def mm2_half(rt, g, tp, b):
             for t in range(2):
@@ -315,145 +275,287 @@ def tile_box_head_region_features_h1_kernel(
             for t in range(2):
                 y_affine(rt, 1, g, 2 * tp + t)
 
-        def y_act(rt, g, b, eng):
-            for t in range(4):
-                y_relu(rt, 1, g, t, b, t, eng)
-
-        def y_aff(rt, g):
-            for t in range(4):
-                y_affine(rt, 1, g, t)
-
-        turn(0, 0)
-        quant(0, 0)
-        turn(0, 1)
-        mm_a(0, 0)
-        quant(0, 1)
-        sort(1, 0)
-        sort(1, 1)
-        for gp in range(1, 4):
-            turn(gp, 0)
-            turn(gp, 1)
-            quant(gp, 0)
-            if gp < 3:
-                sort(gp + 1, 0)
-            mm_a(gp - 1, 1)
-            mm_a(gp, 0)
-            quant(gp, 1)
-            if gp < 3:
-                sort(gp + 1, 1)
-            if gp == 2:
-                w2_words_perm(0, 0)
-        mm_a(3, 1)
-
+        nc.scalar.dma_start(out=w_warm[:].bitcast(I32), in_=w1_i[0, :, 0:64])
+        load_vec(nc.scalar, "b1", b1)
+        make_identity(nc, ident[:])
+        memset_plane(s1_tiles[0])
+        nc.vector.memset(warm[:, 0:8], 0.0)
+        nc.vector.memset(zero[:].bitcast(I32), 0)
+        nc.vector.quantize_mx(out=zero_codes[:].bitcast(FP8X4), scales=zero_scales[:], in_=zero[:])
+        nc.scalar.activation(out=warm[:, 8:16], in_=warm[:, 0:8], func=ACT.Relu)
+        load_x(0, 0)
+        load_x(0, 1)
+        load_x(0, 2)
+        load_x(0, 3)
+        load_x(1, 0)
+        load_x(1, 1)
+        memset_plane(s1_tiles[1])
+        memset_plane(s1_tiles[2])
+        x_sort(0, 0)
+        x_sort(0, 1)
+        x_sort(0, 2)
+        x_sort(0, 3)
+        x_sort(1, 0)
+        load_s1(0)
+        load_w1(0, 0)
+        load_x(1, 2)
+        load_x(1, 3)
+        load_x(2, 0)
+        load_x(2, 1)
+        load_s1(1)
+        load_w1(0, 1)
+        load_x(2, 2)
+        load_x(2, 3)
+        load_x(3, 0)
+        load_x(3, 1)
+        load_w1(0, 2)
+        load_x(3, 2)
+        load_x(3, 3)
+        load_w1(0, 3)
+        load_w2()
+        load_s1(2)
+        load_w1(1, 0)
+        load_w1(1, 1)
+        load_w1(1, 2)
+        load_w1(1, 3)
+        warm_up(0)
+        x_turn(0, 0, 1, True)
+        x_out(0, 0, 1, "S")
+        x_quant(0, 0)
+        x_sort(1, 1)
+        x_turn(0, 1, 2, True)
+        x_out(0, 1, 2, "S")
+        x_quant(0, 1)
+        x_turn(0, 2, 3, True)
+        x_out(0, 2, 3, "S")
+        x_quant(0, 2)
+        memset_plane(s2_raw)
+        x_sort(1, 2)
+        x_sort(1, 3)
+        load_s2()
+        load_vecs()
+        warm_up(4)
+        x_turn(0, 3, 5, True)
+        x_out(0, 3, 5, "S")
+        x_quant(0, 3)
+        x_sort(2, 0)
+        x_sort(2, 1)
+        x_turn(1, 0, 6, True)
+        x_out(1, 0, 6, "S")
+        x_quant(1, 0)
+        b1_turn(7)
+        x_turn(1, 1, 0, True)
+        x_out(1, 1, 0, "S")
+        b1_out(7, "S")
+        x_quant(1, 1)
+        x_sort(2, 2)
+        x_sort(2, 3)
+        mm1_pair(0, 0, 0, 1)
+        mm1_pair(1, 0, 0, 2)
+        mm1_pair(2, 0, 0, 3)
+        x_turn(1, 2, 4, True)
+        x_out(1, 2, 4, "S")
+        x_quant(1, 2)
+        x_sort(3, 0)
+        x_sort(3, 1)
+        x_turn(1, 3, 5, True)
+        x_out(1, 3, 5, "S")
+        x_quant(1, 3)
+        x_turn(2, 0, 6, True)
+        x_out(2, 0, 6, "S")
+        x_quant(2, 0)
+        x_turn(2, 1, 0, True)
+        x_out(2, 1, 0, "S")
+        x_quant(2, 1)
+        x_sort(3, 2)
+        x_sort(3, 3)
+        mm1_pair(3, 0, 0, 7)
+        mm1_pair(0, 0, 1, 1)
+        mm1_pair(1, 0, 1, 2)
+        x_turn(2, 2, 4, True)
+        x_out(2, 2, 4, "S")
+        x_quant(2, 2)
+        x_turn(2, 3, 5, True)
+        x_out(2, 3, 5, "S")
+        x_quant(2, 3)
+        x_turn(3, 0, 6, True)
+        x_out(3, 0, 6, "S")
+        x_quant(3, 0)
+        x_turn(3, 1, 0, True)
+        x_out(3, 1, 0, "S")
+        x_quant(3, 1)
+        w2_words_perm(0, 0)
         w2_words_perm(1, 0)
-        h_add(0, 0, 0)
-        h_add(1, 0, 1)
-        h_add(2, 0, 2)
-        h_add(3, 0, 3)
-        mm_b(0, 4)
         w2_words_perm(0, 1)
-        h_add(0, 1, 4)
-        h_turn(0, 0, 5, 0)
-        h_turn(1, 0, 5, 1)
-        h_turn(2, 0, 7, 0)
-        h_turn(3, 0, 7, 1)
-        h_turn(0, 1, 0, 0)
-        h_out(0, 0, 5, 0, "S")
-        h_out(0, 1, 0, 0, "S")
-        h_out(1, 0, 5, 1, "S")
-        h_out(2, 0, 7, 0, "S")
-        h_out(3, 0, 7, 1, "S")
-        w2_scales_perm(0)
-        h_quant(0, 0)
-        w2_scales_perm(1)
-        h_quant(0, 1)
-        mm_b(1, 6)
         w2_words_perm(1, 1)
+        mm1_pair(2, 0, 1, 3)
+        mm1_pair(3, 0, 1, 7)
+        mm1_pair(0, 0, 2, 1)
+        mm1_pair(1, 0, 2, 2)
+        mm1_pair(2, 0, 2, 3)
+        x_turn(3, 2, 4, True)
+        x_out(3, 2, 4, "S")
+        x_quant(3, 2)
+        x_turn(3, 3, 5, True)
+        x_out(3, 3, 5, "S")
+        x_quant(3, 3)
+        mm1_pair(3, 0, 2, 7)
+        mm1_pair(0, 0, 3, 1)
+        h_add(0, 0, 0, 1)
+        h_add(0, 0, 1, 1)
+        mm1_pair(1, 0, 3, 2)
+        h_add(1, 0, 0, 2)
+        h_add(1, 0, 1, 2)
+        w2_scales_perm(0)
+        mm1_pair(0, 1, 0, 6)
+        mm1_pair(0, 1, 1, 6)
+        mm1_pair(0, 1, 2, 6)
+        mm1_pair(0, 1, 3, 6)
+        h_add(0, 1, 0, 6)
+        h_add(0, 1, 1, 6)
+        w2_scales_perm(1)
+        mm1_pair(2, 0, 3, 3)
+        mm1_pair(3, 0, 3, 7)
+        h_turn(0, 0, 0, 0)
+        h_turn(0, 0, 1, 0)
+        h_out(0, 0, 0, "S")
+        h_quant(0, 0)
+        h_turn(1, 0, 0, 4)
+        h_turn(1, 0, 1, 4)
+        h_turn(0, 1, 0, 5)
+        h_turn(0, 1, 1, 5)
+        h_out(0, 1, 5, "S")
+        h_out(1, 0, 4, "S")
+        h_quant(0, 1)
+        h_add(2, 0, 0, 3)
+        h_add(2, 0, 1, 3)
+        h_add(3, 0, 0, 7)
+        h_add(3, 0, 1, 7)
         h_quant(1, 0)
-        h_add(1, 1, 6)
-        h_quant(2, 0)
-        h_quant(3, 0)
-        mm2_tile(0, 0, 1)
-        y_act(0, 0, 1, "S")
-        mm2_tile(0, 1, 2)
-        y_act(0, 1, 2, "S")
-        h_turn(1, 1, 3, 0)
-        y_aff(0, 0)
-        h_out(1, 1, 3, 0, "V")
-        y_aff(0, 1)
+        mm1_pair(1, 1, 0, 1)
+        mm1_pair(1, 1, 1, 1)
+        mm1_pair(1, 1, 2, 1)
+        mm1_pair(1, 1, 3, 1)
+        h_add(1, 1, 0, 1)
+        h_add(1, 1, 1, 1)
+        mm2_half(0, 0, 0, 2)
+        y_act_half(0, 0, 0, 2, "S")
+        y_aff_half(0, 0, 0)
+        mm2_half(0, 0, 1, 6)
+        y_act_half(0, 0, 1, 6, "S")
+        y_aff_half(0, 0, 1)
+        mm2_half(0, 1, 0, 0)
+        y_act_half(0, 1, 0, 0, "S")
+        mm2_half(0, 1, 1, 5)
+        y_act_half(0, 1, 1, 5, "S")
+        h_turn(1, 1, 0, 4)
+        h_turn(1, 1, 1, 4)
+        h_out(1, 1, 4, "V")
+        y_aff_half(0, 1, 0)
+        y_aff_half(0, 1, 1)
         h_quant(1, 1)
-        mm_b(2, 4)
         y_group(0, 1, 0, "V")
         y_group(0, 1, 1, "V")
         y_quant(0, 1, 0)
         y_quant(0, 1, 1)
-        h_add(2, 1, 4)
-        y_turn(0, 0, 0)
-        y_turn(0, 1, 7)
-        h_turn(2, 1, 6, 0)
-        y_copy(0, 0, 0, "S")
-        y_store(0, 0, nc.sync)
-        y_copy(0, 1, 7, "S")
-        y_store(0, 1, nc.sync)
-        h_out(2, 1, 6, 0, "V")
-        mm2_tile(1, 0, 5)
-        y_act(1, 0, 5, "S")
-        mm2_tile(1, 1, 1)
-        y_act(1, 1, 1, "S")
+        h_turn(2, 0, 0, 3)
+        h_turn(2, 0, 1, 3)
+        h_out(2, 0, 3, "S")
+        h_turn(3, 0, 0, 7)
+        h_turn(3, 0, 1, 7)
+        h_out(3, 0, 7, "S")
+        mm1_pair(2, 1, 0, 1)
+        mm1_pair(2, 1, 1, 1)
+        mm1_pair(2, 1, 2, 1)
+        mm1_pair(2, 1, 3, 1)
+        h_add(2, 1, 0, 1)
+        h_add(2, 1, 1, 1)
+        h_quant(2, 0)
+        h_quant(3, 0)
+        mm2_half(1, 0, 0, 2)
+        y_act_half(1, 0, 0, 2, "S")
+        y_aff_half(1, 0, 0)
+        mm2_half(1, 0, 1, 6)
+        y_act_half(1, 0, 1, 6, "S")
+        y_aff_half(1, 0, 1)
+        mm2_half(1, 1, 0, 0)
+        y_act_half(1, 1, 0, 0, "S")
+        mm2_half(1, 1, 1, 5)
+        y_act_half(1, 1, 1, 5, "S")
+        h_turn(2, 1, 0, 4)
+        h_turn(2, 1, 1, 4)
+        h_out(2, 1, 4, "V")
+        y_aff_half(1, 1, 0)
+        y_aff_half(1, 1, 1)
         h_quant(2, 1)
-        y_aff(1, 0)
-        y_aff(1, 1)
-        mm_b(3, 2)
         y_group(1, 1, 0, "V")
         y_group(1, 1, 1, "V")
         y_quant(1, 1, 0)
         y_quant(1, 1, 1)
+        y_turn(0, 0, 3)
+        y_copy(0, 0, 3, "S")
+        y_turn(0, 1, 7)
+        y_copy(0, 1, 7, "S")
+        y_store_tile(0)
         store_codes(0, 2)
-        h_add(3, 1, 2)
-        y_turn(1, 0, 3)
-        y_turn(1, 1, 4)
-        h_turn(3, 1, 0, 0)
-        y_copy(1, 0, 3, "S")
-        y_store(1, 0, nc.sync)
-        y_copy(1, 1, 4, "S")
-        y_store(1, 1, nc.sync)
-        h_out(3, 1, 0, 0, "V")
-        mm2_tile(2, 0, 6)
-        mm2_tile(2, 1, 7)
+        mm1_pair(3, 1, 0, 1)
+        mm1_pair(3, 1, 1, 1)
+        mm1_pair(3, 1, 2, 1)
+        mm1_pair(3, 1, 3, 1)
+        h_add(3, 1, 0, 1)
+        h_add(3, 1, 1, 1)
+        mm2_half(2, 0, 0, 2)
+        y_act_half(2, 0, 0, 2, "S")
+        y_aff_half(2, 0, 0)
+        mm2_half(2, 0, 1, 6)
+        y_act_half(2, 0, 1, 6, "S")
+        y_turn(1, 0, 0)
+        y_copy(1, 0, 0, "S")
+        h_turn(3, 1, 0, 5)
+        h_turn(3, 1, 1, 5)
+        h_out(3, 1, 5, "V")
+        y_aff_half(2, 0, 1)
         h_quant(3, 1)
-        y_act(2, 0, 6, "S")
-        y_act(2, 1, 7, "V")
-        y_aff(2, 0)
-        y_aff(2, 1)
-        mm2_half(3, 0, 0, 5)
-        mm2_half(3, 0, 1, 1)
-        mm2_half(3, 1, 0, 2)
-        mm2_half(3, 1, 1, 3)
-        y_turn(2, 0, 4)
-        y_turn(2, 1, 0)
-        y_act_half(3, 0, 0, 5, "S")
-        y_act_half(3, 0, 1, 1, "S")
-        y_act_half(3, 1, 0, 2, "S")
-        y_act_half(3, 1, 1, 3, "S")
         y_group(2, 1, 0, "V")
-        y_aff(3, 0)
-        y_group(2, 1, 1, "V")
-        y_aff(3, 1)
-        y_turn(3, 0, 6)
-        y_turn(3, 1, 7)
-        y_copy(2, 0, 4, "S")
-        y_store(2, 0, nc.sync)
-        y_copy(2, 1, 0, "S")
-        y_store(2, 1, nc.sync)
+        y_turn(1, 1, 4)
+        y_copy(1, 1, 4, "S")
+        y_store_tile(1)
+        mm2_half(2, 1, 0, 3)
+        y_act_half(2, 1, 0, 3, "S")
+        y_aff_half(2, 1, 0)
+        mm2_half(2, 1, 1, 7)
+        y_act_half(2, 1, 1, 7, "S")
+        y_aff_half(2, 1, 1)
+        mm2_half(3, 0, 0, 1)
+        y_act_half(3, 0, 0, 1, "S")
+        mm2_half(3, 0, 1, 2)
+        y_act_half(3, 0, 1, 2, "V")
         y_quant(2, 1, 0)
+        y_aff_half(3, 0, 0)
+        y_aff_half(3, 0, 1)
+        y_group(2, 1, 1, "V")
+        mm2_half(3, 1, 0, 6)
+        y_act_half(3, 1, 0, 6, "S")
+        y_aff_half(3, 1, 0)
+        mm2_half(3, 1, 1, 0)
+        y_act_half(3, 1, 1, 0, "S")
+        y_aff_half(3, 1, 1)
         y_group(3, 1, 0, "V")
         y_quant(2, 1, 1)
         y_group(3, 1, 1, "V")
         y_quant(3, 1, 0)
         y_quant(3, 1, 1)
-        y_copy(3, 0, 6, "S")
+        y_turn(2, 0, 5)
+        y_copy(2, 0, 5, "S")
+        y_store(2, 0, nc.sync)
+        y_turn(2, 1, 4)
+        y_copy(2, 1, 4, "S")
+        y_store(2, 1, nc.sync)
+        y_turn(3, 0, 3)
+        y_copy(3, 0, 3, "S")
         y_store(3, 0, nc.sync)
+        y_turn(3, 1, 7)
         y_copy(3, 1, 7, "S")
-        y_store(3, 1, nc.scalar)
+        y_store(3, 1, nc.sync)
         store_codes(2, 2)
         store_scales(nc.sync)

@@ -108,17 +108,17 @@ def tile_box_head_region_features_h1_kernel(
 
         def load_s1(i):
             h, g0, g1 = s1_parts[i]
-            for q in (0, 2, 1, 3):
-                src = s1_i[g0:g1, 4 * q : 4 * q + 4, 128 * h : 128 * (h + 1)]
-                nc.sync.dma_start(out=s1_tiles[i][32 * q : 32 * q + 4].bitcast(I32), in_=src.rearrange("g r n -> r g n"))
+            for r in range(4):
+                src = s1_i[g0:g1, r:16:4, 128 * h : 128 * (h + 1)]
+                nc.sync.dma_start(out=s1_tiles[i][r:P:32].bitcast(I32), in_=src.rearrange("g q n -> q g n"))
 
         def load_w2():
             nc.sync.dma_start(out=w2_raw[:].bitcast(I32), in_=w2_i.rearrange("g p n -> p g n"))
 
         def load_s2():
-            for q in (0, 2, 1, 3):
-                src = s2_i[:, 4 * q : 4 * q + 4, :]
-                nc.sync.dma_start(out=s2_raw[32 * q : 32 * q + 4].bitcast(I32), in_=src.rearrange("g r n -> r g n"))
+            for r in range(4):
+                src = s2_i[:, r:16:4, :]
+                nc.sync.dma_start(out=s2_raw[r:P:32].bitcast(I32), in_=src.rearrange("g q n -> q g n"))
 
         def x_sort(gp, rt):
             nc.vector.tensor_copy(
@@ -259,9 +259,9 @@ def tile_box_head_region_features_h1_kernel(
             nc.sync.dma_start(out=codes_out[:, :, cols], in_=y_codes[:, :, cols].bitcast(I32))
 
         def store_scales(queue):
-            for q in range(4):
-                dst = scales_out[:, 4 * q : 4 * q + 4, :].rearrange("g r n -> r g n")
-                queue.dma_start(out=dst, in_=y_scales[32 * q : 32 * q + 4].bitcast(I32))
+            for r in range(4):
+                dst = scales_out[:, r:16:4, :].rearrange("g q n -> q g n")
+                queue.dma_start(out=dst, in_=y_scales[r:P:32].bitcast(I32))
 
         def mm2_half(rt, g, tp, b):
             for t in range(2):
@@ -289,30 +289,29 @@ def tile_box_head_region_features_h1_kernel(
         load_x(0, 3)
         load_x(1, 0)
         load_x(1, 1)
+        load_x(1, 2)
+        load_w1(0, 0)
         memset_plane(s1_tiles[1])
         memset_plane(s1_tiles[2])
         x_sort(0, 0)
         x_sort(0, 1)
         x_sort(0, 2)
         x_sort(0, 3)
-        x_sort(1, 0)
         load_s1(0)
-        load_w1(0, 0)
-        load_x(1, 2)
         load_x(1, 3)
         load_x(2, 0)
         load_x(2, 1)
-        load_s1(1)
-        load_w1(0, 1)
         load_x(2, 2)
+        load_w1(0, 1)
+        load_s1(1)
         load_x(2, 3)
         load_x(3, 0)
         load_x(3, 1)
-        load_w1(0, 2)
         load_x(3, 2)
         load_x(3, 3)
-        load_w1(0, 3)
+        load_w1(0, 2)
         load_w2()
+        load_w1(0, 3)
         load_s1(2)
         load_w1(1, 0)
         load_w1(1, 1)
@@ -322,90 +321,96 @@ def tile_box_head_region_features_h1_kernel(
         x_turn(0, 0, 1, True)
         x_out(0, 0, 1, "S")
         x_quant(0, 0)
+        x_sort(1, 0)
         x_sort(1, 1)
+        x_sort(1, 2)
         x_turn(0, 1, 2, True)
         x_out(0, 1, 2, "S")
         x_quant(0, 1)
-        x_turn(0, 2, 3, True)
-        x_out(0, 2, 3, "S")
+        warm_up(3)
+        x_turn(0, 2, 4, True)
+        x_out(0, 2, 4, "S")
         x_quant(0, 2)
-        memset_plane(s2_raw)
-        x_sort(1, 2)
         x_sort(1, 3)
-        load_s2()
-        load_vecs()
-        warm_up(4)
+        x_sort(2, 0)
+        x_sort(2, 1)
         x_turn(0, 3, 5, True)
         x_out(0, 3, 5, "S")
         x_quant(0, 3)
-        x_sort(2, 0)
-        x_sort(2, 1)
+        x_sort(2, 2)
         x_turn(1, 0, 6, True)
         x_out(1, 0, 6, "S")
         x_quant(1, 0)
         b1_turn(7)
+        b1_out(7, "S")
         x_turn(1, 1, 0, True)
         x_out(1, 1, 0, "S")
-        b1_out(7, "S")
         x_quant(1, 1)
-        x_sort(2, 2)
-        x_sort(2, 3)
-        mm1_pair(0, 0, 0, 1)
-        mm1_pair(1, 0, 0, 2)
-        mm1_pair(2, 0, 0, 3)
-        x_turn(1, 2, 4, True)
-        x_out(1, 2, 4, "S")
+        x_turn(1, 2, 1, True)
+        x_out(1, 2, 1, "S")
         x_quant(1, 2)
-        x_sort(3, 0)
-        x_sort(3, 1)
+        memset_plane(s2_raw)
+        load_s2()
+        load_vecs()
+        mm1_pair(0, 0, 0, 2)
+        mm1_pair(1, 0, 0, 3)
+        mm1_pair(2, 0, 0, 4)
         x_turn(1, 3, 5, True)
         x_out(1, 3, 5, "S")
         x_quant(1, 3)
+        x_sort(2, 3)
         x_turn(2, 0, 6, True)
         x_out(2, 0, 6, "S")
         x_quant(2, 0)
-        x_turn(2, 1, 0, True)
-        x_out(2, 1, 0, "S")
+        x_sort(3, 0)
+        x_turn(2, 1, 7, True)
+        x_out(2, 1, 7, "S")
         x_quant(2, 1)
+        x_turn(2, 2, 0, True)
+        x_out(2, 2, 0, "S")
+        x_quant(2, 2)
+        x_sort(3, 1)
         x_sort(3, 2)
         x_sort(3, 3)
-        mm1_pair(3, 0, 0, 7)
-        mm1_pair(0, 0, 1, 1)
-        mm1_pair(1, 0, 1, 2)
-        x_turn(2, 2, 4, True)
-        x_out(2, 2, 4, "S")
-        x_quant(2, 2)
+        mm1_pair(3, 0, 0, 1)
+        mm1_pair(0, 0, 1, 2)
+        mm1_pair(1, 0, 1, 3)
+        mm1_pair(2, 0, 1, 4)
         x_turn(2, 3, 5, True)
         x_out(2, 3, 5, "S")
         x_quant(2, 3)
         x_turn(3, 0, 6, True)
         x_out(3, 0, 6, "S")
         x_quant(3, 0)
-        x_turn(3, 1, 0, True)
-        x_out(3, 1, 0, "S")
-        x_quant(3, 1)
         w2_words_perm(0, 0)
-        w2_words_perm(1, 0)
-        w2_words_perm(0, 1)
-        w2_words_perm(1, 1)
-        mm1_pair(2, 0, 1, 3)
-        mm1_pair(3, 0, 1, 7)
-        mm1_pair(0, 0, 2, 1)
-        mm1_pair(1, 0, 2, 2)
-        mm1_pair(2, 0, 2, 3)
-        x_turn(3, 2, 4, True)
-        x_out(3, 2, 4, "S")
+        x_turn(3, 1, 7, True)
+        x_out(3, 1, 7, "S")
+        x_quant(3, 1)
+        x_turn(3, 2, 0, True)
+        x_out(3, 2, 0, "S")
         x_quant(3, 2)
         x_turn(3, 3, 5, True)
         x_out(3, 3, 5, "S")
         x_quant(3, 3)
-        mm1_pair(3, 0, 2, 7)
-        mm1_pair(0, 0, 3, 1)
-        h_add(0, 0, 0, 1)
-        h_add(0, 0, 1, 1)
-        mm1_pair(1, 0, 3, 2)
-        h_add(1, 0, 0, 2)
-        h_add(1, 0, 1, 2)
+        w2_words_perm(1, 0)
+        w2_words_perm(0, 1)
+        mm1_pair(3, 0, 1, 1)
+        mm1_pair(0, 0, 2, 2)
+        mm1_pair(1, 0, 2, 3)
+        mm1_pair(2, 0, 2, 4)
+        mm1_pair(3, 0, 2, 1)
+        mm1_pair(0, 0, 3, 2)
+        h_add(0, 0, 0, 2)
+        h_add(0, 0, 1, 2)
+        mm1_pair(1, 0, 3, 3)
+        h_add(1, 0, 0, 3)
+        h_add(1, 0, 1, 3)
+        mm1_pair(2, 0, 3, 4)
+        h_add(2, 0, 0, 4)
+        h_add(2, 0, 1, 4)
+        mm1_pair(3, 0, 3, 1)
+        h_add(3, 0, 0, 1)
+        h_add(3, 0, 1, 1)
         w2_scales_perm(0)
         mm1_pair(0, 1, 0, 6)
         mm1_pair(0, 1, 1, 6)
@@ -414,43 +419,46 @@ def tile_box_head_region_features_h1_kernel(
         h_add(0, 1, 0, 6)
         h_add(0, 1, 1, 6)
         w2_scales_perm(1)
-        mm1_pair(2, 0, 3, 3)
-        mm1_pair(3, 0, 3, 7)
+        mm1_pair(1, 1, 0, 7)
         h_turn(0, 0, 0, 0)
         h_turn(0, 0, 1, 0)
         h_out(0, 0, 0, "S")
         h_quant(0, 0)
-        h_turn(1, 0, 0, 4)
-        h_turn(1, 0, 1, 4)
-        h_turn(0, 1, 0, 5)
-        h_turn(0, 1, 1, 5)
-        h_out(0, 1, 5, "S")
-        h_out(1, 0, 4, "S")
+        h_turn(1, 0, 0, 5)
+        h_turn(1, 0, 1, 5)
+        h_turn(2, 0, 0, 2)
+        h_turn(2, 0, 1, 2)
+        h_turn(3, 0, 0, 3)
+        h_turn(3, 0, 1, 3)
+        h_turn(0, 1, 0, 4)
+        h_turn(0, 1, 1, 4)
+        h_out(0, 1, 4, "S")
+        h_out(1, 0, 5, "S")
+        h_out(2, 0, 2, "S")
+        h_out(3, 0, 3, "S")
         h_quant(0, 1)
-        h_add(2, 0, 0, 3)
-        h_add(2, 0, 1, 3)
-        h_add(3, 0, 0, 7)
-        h_add(3, 0, 1, 7)
+        w2_words_perm(1, 1)
+        mm1_pair(1, 1, 1, 7)
+        mm1_pair(1, 1, 2, 7)
+        mm1_pair(1, 1, 3, 7)
+        h_add(1, 1, 0, 7)
+        h_add(1, 1, 1, 7)
         h_quant(1, 0)
-        mm1_pair(1, 1, 0, 1)
-        mm1_pair(1, 1, 1, 1)
-        mm1_pair(1, 1, 2, 1)
-        mm1_pair(1, 1, 3, 1)
-        h_add(1, 1, 0, 1)
-        h_add(1, 1, 1, 1)
-        mm2_half(0, 0, 0, 2)
-        y_act_half(0, 0, 0, 2, "S")
+        h_quant(2, 0)
+        h_quant(3, 0)
+        mm2_half(0, 0, 0, 1)
+        y_act_half(0, 0, 0, 1, "S")
         y_aff_half(0, 0, 0)
         mm2_half(0, 0, 1, 6)
         y_act_half(0, 0, 1, 6, "S")
         y_aff_half(0, 0, 1)
         mm2_half(0, 1, 0, 0)
         y_act_half(0, 1, 0, 0, "S")
-        mm2_half(0, 1, 1, 5)
-        y_act_half(0, 1, 1, 5, "S")
-        h_turn(1, 1, 0, 4)
-        h_turn(1, 1, 1, 4)
-        h_out(1, 1, 4, "V")
+        mm2_half(0, 1, 1, 4)
+        y_act_half(0, 1, 1, 4, "S")
+        h_turn(1, 1, 0, 5)
+        h_turn(1, 1, 1, 5)
+        h_out(1, 1, 5, "V")
         y_aff_half(0, 1, 0)
         y_aff_half(0, 1, 1)
         h_quant(1, 1)
@@ -458,33 +466,25 @@ def tile_box_head_region_features_h1_kernel(
         y_group(0, 1, 1, "V")
         y_quant(0, 1, 0)
         y_quant(0, 1, 1)
-        h_turn(2, 0, 0, 3)
-        h_turn(2, 0, 1, 3)
-        h_out(2, 0, 3, "S")
-        h_turn(3, 0, 0, 7)
-        h_turn(3, 0, 1, 7)
-        h_out(3, 0, 7, "S")
-        mm1_pair(2, 1, 0, 1)
-        mm1_pair(2, 1, 1, 1)
-        mm1_pair(2, 1, 2, 1)
-        mm1_pair(2, 1, 3, 1)
-        h_add(2, 1, 0, 1)
-        h_add(2, 1, 1, 1)
-        h_quant(2, 0)
-        h_quant(3, 0)
-        mm2_half(1, 0, 0, 2)
-        y_act_half(1, 0, 0, 2, "S")
+        mm1_pair(2, 1, 0, 2)
+        mm1_pair(2, 1, 1, 2)
+        mm1_pair(2, 1, 2, 2)
+        mm1_pair(2, 1, 3, 2)
+        h_add(2, 1, 0, 2)
+        h_add(2, 1, 1, 2)
+        mm2_half(1, 0, 0, 3)
+        y_act_half(1, 0, 0, 3, "S")
         y_aff_half(1, 0, 0)
-        mm2_half(1, 0, 1, 6)
-        y_act_half(1, 0, 1, 6, "S")
+        mm2_half(1, 0, 1, 7)
+        y_act_half(1, 0, 1, 7, "S")
         y_aff_half(1, 0, 1)
-        mm2_half(1, 1, 0, 0)
-        y_act_half(1, 1, 0, 0, "S")
-        mm2_half(1, 1, 1, 5)
-        y_act_half(1, 1, 1, 5, "S")
-        h_turn(2, 1, 0, 4)
-        h_turn(2, 1, 1, 4)
-        h_out(2, 1, 4, "V")
+        mm2_half(1, 1, 0, 1)
+        y_act_half(1, 1, 0, 1, "S")
+        mm2_half(1, 1, 1, 6)
+        y_act_half(1, 1, 1, 6, "S")
+        h_turn(2, 1, 0, 0)
+        h_turn(2, 1, 1, 0)
+        h_out(2, 1, 0, "V")
         y_aff_half(1, 1, 0)
         y_aff_half(1, 1, 1)
         h_quant(2, 1)
@@ -492,70 +492,70 @@ def tile_box_head_region_features_h1_kernel(
         y_group(1, 1, 1, "V")
         y_quant(1, 1, 0)
         y_quant(1, 1, 1)
-        y_turn(0, 0, 3)
-        y_copy(0, 0, 3, "S")
-        y_turn(0, 1, 7)
-        y_copy(0, 1, 7, "S")
+        y_turn(0, 0, 4)
+        y_copy(0, 0, 4, "S")
+        y_turn(0, 1, 5)
+        y_copy(0, 1, 5, "S")
         y_store_tile(0)
         store_codes(0, 2)
-        mm1_pair(3, 1, 0, 1)
-        mm1_pair(3, 1, 1, 1)
-        mm1_pair(3, 1, 2, 1)
-        mm1_pair(3, 1, 3, 1)
-        h_add(3, 1, 0, 1)
-        h_add(3, 1, 1, 1)
-        mm2_half(2, 0, 0, 2)
-        y_act_half(2, 0, 0, 2, "S")
+        mm1_pair(3, 1, 0, 2)
+        mm1_pair(3, 1, 1, 2)
+        mm1_pair(3, 1, 2, 2)
+        mm1_pair(3, 1, 3, 2)
+        h_add(3, 1, 0, 2)
+        h_add(3, 1, 1, 2)
+        mm2_half(2, 0, 0, 3)
+        y_act_half(2, 0, 0, 3, "S")
         y_aff_half(2, 0, 0)
-        mm2_half(2, 0, 1, 6)
-        y_act_half(2, 0, 1, 6, "S")
-        y_turn(1, 0, 0)
-        y_copy(1, 0, 0, "S")
-        h_turn(3, 1, 0, 5)
-        h_turn(3, 1, 1, 5)
-        h_out(3, 1, 5, "V")
+        mm2_half(2, 0, 1, 7)
+        y_act_half(2, 0, 1, 7, "S")
+        y_turn(1, 0, 1)
+        y_copy(1, 0, 1, "S")
+        h_turn(3, 1, 0, 6)
+        h_turn(3, 1, 1, 6)
+        h_out(3, 1, 6, "V")
         y_aff_half(2, 0, 1)
         h_quant(3, 1)
         y_group(2, 1, 0, "V")
-        y_turn(1, 1, 4)
-        y_copy(1, 1, 4, "S")
+        y_turn(1, 1, 0)
+        y_copy(1, 1, 0, "S")
         y_store_tile(1)
-        mm2_half(2, 1, 0, 3)
-        y_act_half(2, 1, 0, 3, "S")
+        mm2_half(2, 1, 0, 4)
+        y_act_half(2, 1, 0, 4, "S")
         y_aff_half(2, 1, 0)
-        mm2_half(2, 1, 1, 7)
-        y_act_half(2, 1, 1, 7, "S")
+        mm2_half(2, 1, 1, 5)
+        y_act_half(2, 1, 1, 5, "S")
         y_aff_half(2, 1, 1)
-        mm2_half(3, 0, 0, 1)
-        y_act_half(3, 0, 0, 1, "S")
-        mm2_half(3, 0, 1, 2)
-        y_act_half(3, 0, 1, 2, "V")
+        mm2_half(3, 0, 0, 2)
+        y_act_half(3, 0, 0, 2, "S")
+        mm2_half(3, 0, 1, 3)
+        y_act_half(3, 0, 1, 3, "V")
         y_quant(2, 1, 0)
         y_aff_half(3, 0, 0)
         y_aff_half(3, 0, 1)
         y_group(2, 1, 1, "V")
-        mm2_half(3, 1, 0, 6)
-        y_act_half(3, 1, 0, 6, "S")
+        mm2_half(3, 1, 0, 7)
+        y_act_half(3, 1, 0, 7, "S")
         y_aff_half(3, 1, 0)
-        mm2_half(3, 1, 1, 0)
-        y_act_half(3, 1, 1, 0, "S")
+        mm2_half(3, 1, 1, 1)
+        y_act_half(3, 1, 1, 1, "S")
         y_aff_half(3, 1, 1)
         y_group(3, 1, 0, "V")
         y_quant(2, 1, 1)
         y_group(3, 1, 1, "V")
         y_quant(3, 1, 0)
         y_quant(3, 1, 1)
-        y_turn(2, 0, 5)
-        y_copy(2, 0, 5, "S")
+        y_turn(2, 0, 6)
+        y_copy(2, 0, 6, "S")
         y_store(2, 0, nc.sync)
-        y_turn(2, 1, 4)
-        y_copy(2, 1, 4, "S")
+        y_turn(2, 1, 0)
+        y_copy(2, 1, 0, "S")
         y_store(2, 1, nc.sync)
-        y_turn(3, 0, 3)
-        y_copy(3, 0, 3, "S")
+        y_turn(3, 0, 4)
+        y_copy(3, 0, 4, "S")
         y_store(3, 0, nc.sync)
-        y_turn(3, 1, 7)
-        y_copy(3, 1, 7, "S")
+        y_turn(3, 1, 5)
+        y_copy(3, 1, 5, "S")
         y_store(3, 1, nc.sync)
         store_codes(2, 2)
         store_scales(nc.sync)

@@ -17,6 +17,14 @@ ALU = mybir.AluOpType
 ACT = mybir.ActivationFunctionType
 
 P = 128
+GROUP = 512
+TILES = R // P
+CHUNK = 2 * GROUP
+BLOCKS = TILES * D // CHUNK
+SCALAR, VECTOR = "scalar", "vector"
+
+W1_SCALE_PARTS = [(0, 0, 2), (0, 2, 4), (0, 4, 8), (1, 0, 8)]
+SORT_AFTER_QUANT = {0: [4, 5, 6], 2: [7, 8, 9], 3: [10], 7: [11], 8: [12], 10: [13, 14, 15]}
 
 
 def tile_box_head_region_features_h1_kernel(
@@ -24,10 +32,10 @@ def tile_box_head_region_features_h1_kernel(
 ):
     nc = tc.nc
     x = roi.rearrange("r c a b -> r (c a b)")
-    w1_i, s1_i = w1_words.bitcast(I32), w1_scales.bitcast(I32)
-    w2_i, s2_i = w2_words.bitcast(I32), w2_scales.bitcast(I32)
-    codes_out = out_1.rearrange("g p m t -> p g (m t)").bitcast(I32)
-    scales_out = out_2.bitcast(I32)
+    w1_hbm, s1_hbm = w1_words.bitcast(I32), w1_scales.bitcast(I32)
+    w2_hbm, s2_hbm = w2_words.bitcast(I32), w2_scales.bitcast(I32)
+    codes_hbm = out_1.rearrange("g p m t -> p g (m t)").bitcast(I32)
+    scales_hbm = out_2.bitcast(I32)
 
     with ExitStack() as ctx:
         sb = ctx.enter_context(tc.tile_pool(name="sb", bufs=1))
@@ -37,525 +45,436 @@ def tile_box_head_region_features_h1_kernel(
         def tile(name, shape, dtype):
             return sb.tile(shape, dtype, name=name, align_bytes=64)
 
-        bank = [ps.tile([P, 512], F32, name="bank%d" % i) for i in range(8)]
+        halves = [(rt, h) for rt in range(TILES) for h in range(2)]
+
+        banks = [ps.tile([P, GROUP], F32, name="bank%d" % i) for i in range(8)]
         ident = tile("ident", [P, P], F32)
-        warm = tile("warm", [P, 16], F32)
-        vec = {k: tile("vec_" + k, [P, 2, 4], BF16) for k in ("b1", "b2", "shift", "gain")}
-        b1_rows = tile("b1_rows", [P, 1024], BF16)
-        x_raw = {(gp, rt): tile("x_raw%d_%d" % (gp, rt), [P, 1024], BF16) for gp in range(4) for rt in range(4)}
-        x_perm = {(gp, rt): tile("x_perm%d_%d" % (gp, rt), [P, 512], F32) for gp in range(4) for rt in range(4)}
-        zero = tile("zero", [P, 2048], BF16)
-        zero_codes = tile("zero_codes", [P, 512], U32)
-        zero_scales = tile("zero_scales", [P, 512], U8)
-        w_warm = tile("w_warm", [P, 256], U8)
-        x_codes = {(gp, rt): tile("x_codes%d_%d" % (gp, rt), [P, 256], U32) for gp in range(4) for rt in range(4)}
-        x_scales = {(gp, rt): tile("x_scales%d_%d" % (gp, rt), [P, 256], U8) for gp in range(4) for rt in range(4)}
-        w1 = {(h, gp): tile("w1_%d_%d" % (h, gp), [P, 2, 1024], U8) for h in range(2) for gp in range(4)}
-        s1_parts = [(0, 0, 2), (0, 2, 8), (1, 0, 8)]
-        s1_tiles = [tile("s1_%d" % i, [P, g1 - g0, 512], U8) for i, (h, g0, g1) in enumerate(s1_parts)]
-        s1 = {(h, g): s1_tiles[i][:, g - g0, :] for i, (h, g0, g1) in enumerate(s1_parts) for g in range(g0, g1)}
-        w2_raw = tile("w2_raw", [P, 2, 2048], U8)
-        s2_raw = tile("s2_raw", [P, 2, 1024], U8)
-        w2 = tile("w2", [P, 2, 2048], U8)
-        s2 = tile("s2", [P, 2, 1024], U8)
-        h_pre = {(rt, h): tile("h_pre%d_%d" % (rt, h), [P, 512], BF16) for rt in range(4) for h in range(2)}
-        h_grp = {(rt, h): tile("h_grp%d_%d" % (rt, h), [P, 512], BF16) for rt in range(4) for h in range(2)}
-        h_codes = {(rt, h): tile("h_codes%d_%d" % (rt, h), [P, P], U32) for rt in range(4) for h in range(2)}
-        h_scales = {(rt, h): tile("h_scales%d_%d" % (rt, h), [P, P], U8) for rt in range(4) for h in range(2)}
+        table_warm = tile("table_warm", [P, 16], F32)
+        vec = {key: tile("vec_" + key, [P, 2, 4], BF16) for key in ("b1", "b2", "shift", "gain")}
+        b1_rows = tile("b1_rows", [P, F], BF16)
+        x_raw = [tile("x_raw%d" % i, [P, CHUNK], BF16) for i in range(BLOCKS)]
+        x_sorted = [tile("x_sorted%d" % i, [P, CHUNK // 2], F32) for i in range(BLOCKS)]
+        zeros = tile("zeros", [P, 4 * GROUP], BF16)
+        zero_codes = tile("zero_codes", [P, GROUP], U32)
+        zero_scales = tile("zero_scales", [P, GROUP], U8)
+        w_warm = tile("w_warm", [P, 2 * P], U8)
+        x_codes = [tile("x_codes%d" % i, [P, 2 * P], U32) for i in range(BLOCKS)]
+        x_scales = [tile("x_scales%d" % i, [P, 2 * P], U8) for i in range(BLOCKS)]
+        w1 = {(h, c): tile("w1_%d_%d" % (h, c), [P, 2, 2 * GROUP], U8) for h in range(2) for c in range(4)}
+        s1_parts = [tile("s1_%d" % i, [P, g1 - g0, GROUP], U8) for i, (h, g0, g1) in enumerate(W1_SCALE_PARTS)]
+        s1 = {
+            (h, g): s1_parts[i][:, g - g0, :] for i, (h, g0, g1) in enumerate(W1_SCALE_PARTS) for g in range(g0, g1)
+        }
+        w2_raw = [tile("w2_raw%d" % g, [P, 2, 2 * GROUP], U8) for g in range(2)]
+        s2_raw = tile("s2_raw", [P, 2, N], U8)
+        w2 = tile("w2", [P, 2, 2 * N], U8)
+        s2 = tile("s2", [P, 2, N], U8)
+        h_biased = {key: tile("h_biased%d_%d" % key, [P, GROUP], BF16) for key in halves}
+        h_turned = {key: tile("h_turned%d_%d" % key, [P, GROUP], BF16) for key in halves}
+        h_codes = {key: tile("h_codes%d_%d" % key, [P, P], U32) for key in halves}
+        h_scales = {key: tile("h_scales%d_%d" % key, [P, P], U8) for key in halves}
         a_t = [tile("a_t%d" % g, [P, 4, R], F32) for g in range(2)]
         y_t = [tile("y_t%d" % g, [P, 4, R], F32) for g in range(2)]
-        y_grp = [tile("y_grp%d" % g, [P, R, 4], BF16) for g in range(2)]
+        y_bf16 = [tile("y_bf16_%d" % g, [P, R, 4], BF16) for g in range(2)]
         y_codes = tile("y_codes", [P, 2, R], U32)
         y_scales = tile("y_scales", [P, 2, R], U8)
-        y_rows = [tile("y_rows%d" % rt, [P, 1024], F32) for rt in range(4)]
-        y_out = {(rt, g): y_rows[rt][:, 512 * g : 512 * (g + 1)] for rt in range(4) for g in range(2)}
+        y_rows = [tile("y_rows%d" % rt, [P, N], F32) for rt in range(TILES)]
 
-        def load_vec(eng, key, src):
-            eng.dma_start(out=vec[key][:], in_=src.rearrange("(g p t) -> p g t", g=2, t=4))
+        free_banks = list(range(len(banks)))
+        held = {}
 
-        def load_x(gp, rt):
-            nc.sync.dma_start(out=x_raw[gp, rt][:], in_=x[P * rt : P * (rt + 1), 1024 * gp : 1024 * (gp + 1)])
+        def take(use):
+            held[use] = free_banks[0]
+            free_banks.remove(held[use])
+            return banks[held[use]]
 
-        def load_vecs():
-            load_vec(nc.sync, "b2", b2)
-            load_vec(nc.sync, "shift", shift)
-            load_vec(nc.sync, "gain", gain)
+        def bank_of(use):
+            return banks[held[use]]
 
-        def memset_plane(t):
+        def give_back(use):
+            free_banks.append(held[use])
+
+        def regions(rt, count=1):
+            return slice(P * rt, P * (rt + count))
+
+        def copy_on(engine):
+            return nc.scalar.copy if engine == SCALAR else nc.vector.tensor_copy
+
+        def load_vec(queue, key, src):
+            queue.dma_start(out=vec[key][:], in_=src.rearrange("(g p t) -> p g t", g=2, t=4))
+
+        def load_x(blocks):
+            for i in blocks:
+                c, rt = divmod(i, TILES)
+                nc.sync.dma_start(out=x_raw[i][:], in_=x[regions(rt), CHUNK * c : CHUNK * (c + 1)])
+
+        def load_w1(h, c):
+            src = w1_hbm[2 * c : 2 * c + 2, :, 256 * h : 256 * (h + 1)]
+            nc.sync.dma_start(out=w1[h, c][:].bitcast(I32), in_=src.rearrange("g p n -> p g n"))
+
+        def load_w2(g):
+            src = w2_hbm[:, :, 256 * g : 256 * (g + 1)]
+            nc.sync.dma_start(out=w2_raw[g][:].bitcast(I32), in_=src.rearrange("h p n -> p h n"))
+
+        def load_scale_rows(plane, src):
+            for r in range(4):
+                nc.sync.dma_start(out=plane[r:P:32].bitcast(I32), in_=src[:, r:16:4, :].rearrange("g q n -> q g n"))
+
+        def load_s1(part):
+            h, g0, g1 = W1_SCALE_PARTS[part]
+            load_scale_rows(s1_parts[part], s1_hbm[g0:g1, :, 128 * h : 128 * (h + 1)])
+
+        def clear(t):
             nc.vector.memset(t[:].bitcast(I32), 0)
 
-        def copy_on(eng):
-            return nc.scalar.copy if eng == "S" else nc.vector.tensor_copy
-
-        def warm_up(b):
-            for i in range(2):
+        def warm_up():
+            bank = take("warm")
+            for repeat in range(2):
                 nc.tensor.matmul_mx(
-                    out=bank[b][:], lhsT=w_warm[:].bitcast(FP4X4), lhsT_scale=zero_scales[:, 0:P],
-                    rhs=zero_codes[:].bitcast(FP8X4), rhs_scale=zero_scales[:], start=True, stop=True,
+                    out=bank[:],
+                    lhsT=w_warm[:].bitcast(FP4X4),
+                    lhsT_scale=zero_scales[:, 0:P],
+                    rhs=zero_codes[:].bitcast(FP8X4),
+                    rhs_scale=zero_scales[:],
+                    start=True,
+                    stop=True,
+                )
+            give_back("warm")
+
+        def spread_b1():
+            bank = take("b1")
+            words = vec["b1"][:].rearrange("p g t -> p (g t)").bitcast(F32)
+            for j in range(4):
+                nc.tensor.transpose(bank[:, P * j : P * (j + 1)], words[:, j : j + 1].to_broadcast([P, P]), ident[:])
+            nc.scalar.copy(out=b1_rows[:].bitcast(F32), in_=bank[:])
+            give_back("b1")
+
+        def x_sort(blocks):
+            for i in blocks:
+                nc.vector.tensor_copy(
+                    out=x_sorted[i][:].rearrange("r (g u m) -> r g u m", g=2, u=2),
+                    in_=x_raw[i][:].bitcast(F32).rearrange("r (g m u) -> r g u m", g=2, u=2),
                 )
 
-        def b1_turn(b):
-            b1_words = vec["b1"][:].rearrange("p g t -> p (g t)").bitcast(F32)
-            for c in range(4):
-                nc.tensor.transpose(bank[b][:, P * c : P * (c + 1)], b1_words[:, c : c + 1].to_broadcast([P, P]), ident[:])
-
-        def b1_out(b, eng):
-            copy_on(eng)(out=b1_rows[:].bitcast(F32), in_=bank[b][:])
-
-        def load_w1(h, gp):
-            src = w1_i[2 * gp : 2 * gp + 2, :, 256 * h : 256 * (h + 1)]
-            nc.sync.dma_start(out=w1[h, gp][:].bitcast(I32), in_=src.rearrange("g p n -> p g n"))
-
-        def load_s1(i):
-            h, g0, g1 = s1_parts[i]
-            for r in range(4):
-                src = s1_i[g0:g1, r:16:4, 128 * h : 128 * (h + 1)]
-                nc.sync.dma_start(out=s1_tiles[i][r:P:32].bitcast(I32), in_=src.rearrange("g q n -> q g n"))
-
-        def load_w2():
-            nc.sync.dma_start(out=w2_raw[:].bitcast(I32), in_=w2_i.rearrange("g p n -> p g n"))
-
-        def load_s2():
-            for r in range(4):
-                src = s2_i[:, r:16:4, :]
-                nc.sync.dma_start(out=s2_raw[r:P:32].bitcast(I32), in_=src.rearrange("g q n -> q g n"))
-
-        def x_sort(gp, rt):
-            nc.vector.tensor_copy(
-                out=x_perm[gp, rt][:].rearrange("r (g u m) -> r g u m", g=2, u=2),
-                in_=x_raw[gp, rt][:].bitcast(F32).rearrange("r (g m u) -> r g u m", g=2, u=2),
+        def x_turn(i):
+            bank = take(("x", i))
+            for j in range(4):
+                nc.tensor.transpose(bank[:, P * j : P * (j + 1)], x_sorted[i][:, P * j : P * (j + 1)], ident[:])
+            nc.scalar.copy(
+                out=x_raw[i][:].bitcast(F32).rearrange("p (g r u) -> p g r u", g=2, u=2),
+                in_=bank[:].rearrange("p (g u r) -> p g r u", g=2, u=2),
             )
+            give_back(("x", i))
+            nc.vector.quantize_mx(out=x_codes[i][:].bitcast(FP8X4), scales=x_scales[i][:], in_=x_raw[i][:])
+            x_sort(SORT_AFTER_QUANT.get(i, []))
 
-        def x_turn(gp, rt, b, is_sorted):
-            words = x_raw[gp, rt][:].bitcast(F32)
-            for gg in range(2):
-                for u in range(2):
-                    c = 2 * gg + u
-                    if is_sorted:
-                        src = x_perm[gp, rt][:, P * c : P * (c + 1)]
-                    else:
-                        src = words[:, 256 * gg + u : 256 * (gg + 1) : 2]
-                    nc.tensor.transpose(bank[b][:, P * c : P * (c + 1)], src, ident[:])
+        def mm1(i, h):
+            c, rt = divmod(i, TILES)
+            bank = take(("h", rt, h)) if c == 0 else bank_of(("h", rt, h))
+            for j in range(2):
+                g = 2 * c + j
+                nc.tensor.matmul_mx(
+                    out=bank[:],
+                    lhsT=x_codes[i][:, P * j : P * (j + 1)].bitcast(FP8X4),
+                    lhsT_scale=x_scales[i][:, P * j : P * (j + 1)],
+                    rhs=w1[h, c][:, j, :].bitcast(FP4X4),
+                    rhs_scale=s1[h, g],
+                    start=(g == 0),
+                    stop=(g == D // GROUP - 1),
+                )
 
-        def x_out(gp, rt, b, eng):
-            copy_on(eng)(
-                out=x_raw[gp, rt][:].bitcast(F32).rearrange("p (g r u) -> p g r u", g=2, u=2),
-                in_=bank[b][:].rearrange("p (g u r) -> p g r u", g=2, u=2),
-            )
+        def mm1_second_half(rt, chunks=range(4)):
+            for c in chunks:
+                mm1(TILES * c + rt, 1)
 
-        def x_quant(gp, rt):
-            nc.vector.quantize_mx(out=x_codes[gp, rt][:].bitcast(FP8X4), scales=x_scales[gp, rt][:], in_=x_raw[gp, rt][:])
-
-        def mm1_pair(rt, h, gp, b):
-            mm1(rt, h, 2 * gp, b)
-            mm1(rt, h, 2 * gp + 1, b)
-
-        def mm1(rt, h, g, b):
-            cols = slice(P * (g % 2), P * (g % 2 + 1))
-            nc.tensor.matmul_mx(
-                out=bank[b][:],
-                lhsT=x_codes[g // 2, rt][:, cols].bitcast(FP8X4),
-                lhsT_scale=x_scales[g // 2, rt][:, cols],
-                rhs=w1[h, g // 2][:, g % 2, :].bitcast(FP4X4),
-                rhs_scale=s1[h, g],
-                start=(g == 0),
-                stop=(g == 7),
-            )
-
-        def w2_words_perm(g2, g):
-            cols = slice(1024 * g, 1024 * (g + 1))
-            nc.vector.tensor_copy(
-                out=w2[:, g2, cols].rearrange("p (t m b) -> p t m b", t=4, b=2),
-                in_=w2_raw[:, g2, cols].rearrange("p (m t b) -> p t m b", t=4, b=2),
-            )
-
-        def w2_scales_perm(g2):
-            nc.vector.tensor_copy(
-                out=s2[:, g2, :].rearrange("p (g t m) -> p g t m", g=2, t=4),
-                in_=s2_raw[:, g2, :].rearrange("p (g m t) -> p g t m", g=2, t=4),
-            )
-
-        def h_add(rt, h, u, b):
+        def h_add_part(rt, h, u):
+            cols = slice(256 * u, 256 * (u + 1))
             nc.vector.tensor_tensor(
-                out=h_pre[rt, h][:, 256 * u : 256 * (u + 1)].rearrange("p (m e) -> p m e", e=2),
-                in0=bank[b][:].rearrange("p (m u e) -> p u m e", u=2, e=2)[:, u],
-                in1=b1_rows[:, 512 * h + 256 * u : 512 * h + 256 * (u + 1)].rearrange("p (m e) -> p m e", e=2),
+                out=h_biased[rt, h][:, cols].rearrange("r (m e) -> r m e", e=2),
+                in0=bank_of(("h", rt, h))[:].rearrange("r (m u e) -> r u m e", u=2, e=2)[:, u],
+                in1=b1_rows[:, GROUP * h : GROUP * (h + 1)][:, cols].rearrange("r (m e) -> r m e", e=2),
                 op=ALU.add,
             )
+            if u == 1:
+                give_back(("h", rt, h))
 
-        def h_turn(rt, h, u, b):
-            words = h_pre[rt, h][:].bitcast(F32)
-            nc.tensor.transpose(bank[b][:, P * u : P * (u + 1)], words[:, P * u : P * (u + 1)], ident[:])
+        def h_add(rt, h):
+            h_add_part(rt, h, 0)
+            h_add_part(rt, h, 1)
 
-        def h_out(rt, h, b, eng):
-            src = bank[b][:, 0:256].bitcast(BF16).rearrange("p (u r e) -> p r u e", u=2, e=2)
-            dst = h_grp[rt, h][:].rearrange("p (r u e) -> p r u e", u=2, e=2)
-            if eng == "S":
+        def h_turn_part(rt, h, u):
+            bank = take(("ht", rt, h)) if u == 0 else bank_of(("ht", rt, h))
+            words = h_biased[rt, h][:].bitcast(F32)
+            nc.tensor.transpose(bank[:, P * u : P * (u + 1)], words[:, P * u : P * (u + 1)], ident[:])
+
+        def h_turn(rt, h):
+            h_turn_part(rt, h, 0)
+            h_turn_part(rt, h, 1)
+
+        def h_relu(rt, h, engine):
+            src = bank_of(("ht", rt, h))[:, 0 : 2 * P].bitcast(BF16).rearrange("p (u r e) -> p r u e", u=2, e=2)
+            dst = h_turned[rt, h][:].rearrange("p (r u e) -> p r u e", u=2, e=2)
+            if engine == SCALAR:
                 nc.scalar.activation(out=dst, in_=src, func=ACT.Relu)
             else:
                 nc.vector.tensor_scalar(out=dst, in0=src, scalar1=0.0, scalar2=None, op0=ALU.max)
+            give_back(("ht", rt, h))
 
         def h_quant(rt, h):
-            nc.vector.quantize_mx(out=h_codes[rt, h][:].bitcast(FP8X4), scales=h_scales[rt, h][:], in_=h_grp[rt, h][:])
+            nc.vector.quantize_mx(out=h_codes[rt, h][:].bitcast(FP8X4), scales=h_scales[rt, h][:], in_=h_turned[rt, h][:])
 
-        def mm2(rt, g, t, b, c):
-            for g2 in range(2):
-                col = 512 * g + P * t
-                nc.tensor.matmul_mx(
-                    out=bank[b][:, P * c : P * (c + 1)],
-                    lhsT=w2[:, g2, 2 * col : 2 * (col + P)].bitcast(FP4X4),
-                    lhsT_scale=s2[:, g2, col : col + P],
-                    rhs=h_codes[rt, g2][:].bitcast(FP8X4),
-                    rhs_scale=h_scales[rt, g2][:],
-                    start=(g2 == 0),
-                    stop=(g2 == 1),
+        def w2_sort_words(h, g):
+            nc.vector.tensor_copy(
+                out=w2[:, h, 2 * GROUP * g : 2 * GROUP * (g + 1)].rearrange("p (t m b) -> p t m b", t=4, b=2),
+                in_=w2_raw[g][:, h, :].rearrange("p (m t b) -> p t m b", t=4, b=2),
+            )
+
+        def w2_sort_scales(h):
+            nc.vector.tensor_copy(
+                out=s2[:, h, :].rearrange("p (g t m) -> p g t m", g=2, t=4),
+                in_=s2_raw[:, h, :].rearrange("p (g m t) -> p g t m", g=2, t=4),
+            )
+
+        def mm2(rt, g, pair):
+            bank = take(("z", rt, g, pair))
+            for j in range(2):
+                col = GROUP * g + P * (2 * pair + j)
+                for h in range(2):
+                    nc.tensor.matmul_mx(
+                        out=bank[:, P * j : P * (j + 1)],
+                        lhsT=w2[:, h, 2 * col : 2 * (col + P)].bitcast(FP4X4),
+                        lhsT_scale=s2[:, h, col : col + P],
+                        rhs=h_codes[rt, h][:].bitcast(FP8X4),
+                        rhs_scale=h_scales[rt, h][:],
+                        start=(h == 0),
+                        stop=(h == 1),
+                    )
+
+        def a_relu(rt, g, pair, engine):
+            bank = bank_of(("z", rt, g, pair))
+            for j in range(2):
+                t = 2 * pair + j
+                src, dst, bias = bank[:, P * j : P * (j + 1)], a_t[g][:, t, regions(rt)], vec["b2"][:, g, t : t + 1]
+                if engine == SCALAR:
+                    nc.scalar.activation(out=dst, in_=src, func=ACT.Relu, bias=bias)
+                else:
+                    nc.vector.tensor_scalar(out=dst, in0=src, scalar1=bias, scalar2=0.0, op0=ALU.add, op1=ALU.max)
+            give_back(("z", rt, g, pair))
+
+        def y_affine(rt, g, pair):
+            for t in (2 * pair, 2 * pair + 1):
+                nc.vector.tensor_scalar(
+                    out=y_t[g][:, t, regions(rt)],
+                    in0=a_t[g][:, t, regions(rt)],
+                    scalar1=vec["shift"][:, g, t : t + 1],
+                    scalar2=vec["gain"][:, g, t : t + 1],
+                    op0=ALU.add,
+                    op1=ALU.mult,
                 )
 
-        def y_relu(r0, n, g, t, b, c, eng):
-            src = bank[b][:, P * c : P * (c + n)]
-            dst = a_t[g][:, t, P * r0 : P * (r0 + n)]
-            bias = vec["b2"][:, g, t : t + 1]
-            if eng == "S":
-                nc.scalar.activation(out=dst, in_=src, func=ACT.Relu, bias=bias)
-            else:
-                nc.vector.tensor_scalar(out=dst, in0=src, scalar1=bias, scalar2=0.0, op0=ALU.add, op1=ALU.max)
+        def y_round(rt, g):
+            nc.vector.tensor_copy(out=y_bf16[g][:, regions(rt), :], in_=y_t[g][:, :, regions(rt)].rearrange("p t r -> p r t"))
 
-        def y_affine(r0, n, g, t):
-            cols = slice(P * r0, P * (r0 + n))
-            nc.vector.tensor_scalar(
-                out=y_t[g][:, t, cols], in0=a_t[g][:, t, cols],
-                scalar1=vec["shift"][:, g, t : t + 1], scalar2=vec["gain"][:, g, t : t + 1],
-                op0=ALU.add, op1=ALU.mult,
-            )
-
-        def y_group(r0, n, g, eng):
-            cols = slice(P * r0, P * (r0 + n))
-            copy = nc.scalar.copy if eng == "S" else nc.vector.tensor_copy
-            copy(out=y_grp[g][:, cols, :], in_=y_t[g][:, :, cols].rearrange("p t r -> p r t"))
-
-        def y_quant(r0, n, g):
-            cols = slice(P * r0, P * (r0 + n))
+        def y_quant(rt, g):
             nc.vector.quantize_mx(
-                out=y_codes[:, g, cols].bitcast(FP8X4), scales=y_scales[:, g, cols],
-                in_=y_grp[g][:, cols, :].rearrange("p r t -> p (r t)"),
+                out=y_codes[:, g, regions(rt)].bitcast(FP8X4),
+                scales=y_scales[:, g, regions(rt)],
+                in_=y_bf16[g][:, regions(rt), :].rearrange("p r t -> p (r t)"),
             )
 
-        def y_turn(rt, g, b):
+        def y_turn(rt, g):
+            bank = take(("y", rt, g))
             for t in range(4):
-                nc.tensor.transpose(bank[b][:, P * t : P * (t + 1)], y_t[g][:, t, P * rt : P * (rt + 1)], ident[:])
+                nc.tensor.transpose(bank[:, P * t : P * (t + 1)], y_t[g][:, t, regions(rt)], ident[:])
 
-        def y_copy(rt, g, b, eng):
-            copy = nc.scalar.copy if eng == "S" else nc.vector.tensor_copy
-            copy(out=y_out[rt, g][:].rearrange("r (p t) -> r p t", t=4), in_=bank[b][:].rearrange("r (t p) -> r p t", t=4))
+        def y_out(rt, g, engine):
+            copy_on(engine)(
+                out=y_rows[rt][:, GROUP * g : GROUP * (g + 1)].rearrange("r (p t) -> r p t", t=4),
+                in_=bank_of(("y", rt, g))[:].rearrange("r (t p) -> r p t", t=4),
+            )
+            give_back(("y", rt, g))
 
-        def y_store(rt, g, queue):
-            queue.dma_start(out=out_0[P * rt : P * (rt + 1), 512 * g : 512 * (g + 1)], in_=y_out[rt, g][:])
+        def store_y(rt, cols=slice(0, N)):
+            nc.sync.dma_start(out=out_0[regions(rt), cols], in_=y_rows[rt][:, cols])
 
-        def y_store_tile(rt):
-            nc.sync.dma_start(out=out_0[P * rt : P * (rt + 1), :], in_=y_rows[rt][:])
+        def store_y_group(rt, g):
+            store_y(rt, slice(GROUP * g, GROUP * (g + 1)))
 
-        def store_codes(r0, n):
-            cols = slice(P * r0, P * (r0 + n))
-            nc.sync.dma_start(out=codes_out[:, :, cols], in_=y_codes[:, :, cols].bitcast(I32))
+        def store_codes(rt, count):
+            nc.sync.dma_start(out=codes_hbm[:, :, regions(rt, count)], in_=y_codes[:, :, regions(rt, count)].bitcast(I32))
 
-        def store_scales(queue):
+        def store_scales():
             for r in range(4):
-                dst = scales_out[:, r:16:4, :].rearrange("g q n -> q g n")
-                queue.dma_start(out=dst, in_=y_scales[r:P:32].bitcast(I32))
+                dst = scales_hbm[:, r:16:4, :].rearrange("g q n -> q g n")
+                nc.sync.dma_start(out=dst, in_=y_scales[r:P:32].bitcast(I32))
 
-        def mm2_half(rt, g, tp, b):
-            for t in range(2):
-                mm2(rt, g, 2 * tp + t, b, t)
+        def stage2_beside_next_h(rt):
+            for pair in range(2):
+                mm2(rt, 0, pair)
+                a_relu(rt, 0, pair, SCALAR)
+                y_affine(rt, 0, pair)
+            for pair in range(2):
+                mm2(rt, 1, pair)
+                a_relu(rt, 1, pair, SCALAR)
+            h_turn(rt + 1, 1)
+            h_relu(rt + 1, 1, VECTOR)
+            for pair in range(2):
+                y_affine(rt, 1, pair)
+            h_quant(rt + 1, 1)
+            for g in range(2):
+                y_round(rt, g)
+            for g in range(2):
+                y_quant(rt, g)
 
-        def y_act_half(rt, g, tp, b, eng):
-            for t in range(2):
-                y_relu(rt, 1, g, 2 * tp + t, b, t, eng)
-
-        def y_aff_half(rt, g, tp):
-            for t in range(2):
-                y_affine(rt, 1, g, 2 * tp + t)
-
-        nc.scalar.dma_start(out=w_warm[:].bitcast(I32), in_=w1_i[0, :, 0:64])
+        nc.scalar.dma_start(out=w_warm[:].bitcast(I32), in_=w1_hbm[0, :, 0:64])
         load_vec(nc.scalar, "b1", b1)
         make_identity(nc, ident[:])
-        memset_plane(s1_tiles[0])
-        nc.vector.memset(warm[:, 0:8], 0.0)
-        nc.vector.memset(zero[:].bitcast(I32), 0)
-        nc.vector.quantize_mx(out=zero_codes[:].bitcast(FP8X4), scales=zero_scales[:], in_=zero[:])
-        nc.scalar.activation(out=warm[:, 8:16], in_=warm[:, 0:8], func=ACT.Relu)
-        load_x(0, 0)
-        load_x(0, 1)
-        load_x(0, 2)
-        load_x(0, 3)
-        load_x(1, 0)
-        load_x(1, 1)
-        load_x(1, 2)
+        clear(s1_parts[0])
+        clear(s1_parts[1])
+        nc.vector.memset(table_warm[:, 0:8], 0.0)
+        nc.vector.memset(zeros[:].bitcast(I32), 0)
+        nc.vector.quantize_mx(out=zero_codes[:].bitcast(FP8X4), scales=zero_scales[:], in_=zeros[:])
+        nc.scalar.activation(out=table_warm[:, 8:16], in_=table_warm[:, 0:8], func=ACT.Relu)
+        clear(s1_parts[2])
+        clear(s1_parts[3])
+
+        load_x(range(0, 7))
         load_w1(0, 0)
-        memset_plane(s1_tiles[1])
-        memset_plane(s1_tiles[2])
-        x_sort(0, 0)
-        x_sort(0, 1)
-        x_sort(0, 2)
-        x_sort(0, 3)
         load_s1(0)
-        load_x(1, 3)
-        load_x(2, 0)
-        load_x(2, 1)
-        load_x(2, 2)
+        load_x(range(7, 11))
         load_w1(0, 1)
         load_s1(1)
-        load_x(2, 3)
-        load_x(3, 0)
-        load_x(3, 1)
-        load_x(3, 2)
-        load_x(3, 3)
+        load_x(range(11, 16))
         load_w1(0, 2)
-        load_w2()
-        load_w1(0, 3)
         load_s1(2)
-        load_w1(1, 0)
-        load_w1(1, 1)
-        load_w1(1, 2)
-        load_w1(1, 3)
-        warm_up(0)
-        x_turn(0, 0, 1, True)
-        x_out(0, 0, 1, "S")
-        x_quant(0, 0)
-        x_sort(1, 0)
-        x_sort(1, 1)
-        x_sort(1, 2)
-        x_turn(0, 1, 2, True)
-        x_out(0, 1, 2, "S")
-        x_quant(0, 1)
-        warm_up(3)
-        x_turn(0, 2, 4, True)
-        x_out(0, 2, 4, "S")
-        x_quant(0, 2)
-        x_sort(1, 3)
-        x_sort(2, 0)
-        x_sort(2, 1)
-        x_turn(0, 3, 5, True)
-        x_out(0, 3, 5, "S")
-        x_quant(0, 3)
-        x_sort(2, 2)
-        x_turn(1, 0, 6, True)
-        x_out(1, 0, 6, "S")
-        x_quant(1, 0)
-        b1_turn(7)
-        b1_out(7, "S")
-        x_turn(1, 1, 0, True)
-        x_out(1, 1, 0, "S")
-        x_quant(1, 1)
-        x_turn(1, 2, 1, True)
-        x_out(1, 2, 1, "S")
-        x_quant(1, 2)
-        memset_plane(s2_raw)
-        load_s2()
-        load_vecs()
-        mm1_pair(0, 0, 0, 2)
-        mm1_pair(1, 0, 0, 3)
-        mm1_pair(2, 0, 0, 4)
-        x_turn(1, 3, 5, True)
-        x_out(1, 3, 5, "S")
-        x_quant(1, 3)
-        x_sort(2, 3)
-        x_turn(2, 0, 6, True)
-        x_out(2, 0, 6, "S")
-        x_quant(2, 0)
-        x_sort(3, 0)
-        x_turn(2, 1, 7, True)
-        x_out(2, 1, 7, "S")
-        x_quant(2, 1)
-        x_turn(2, 2, 0, True)
-        x_out(2, 2, 0, "S")
-        x_quant(2, 2)
-        x_sort(3, 1)
-        x_sort(3, 2)
-        x_sort(3, 3)
-        mm1_pair(3, 0, 0, 1)
-        mm1_pair(0, 0, 1, 2)
-        mm1_pair(1, 0, 1, 3)
-        mm1_pair(2, 0, 1, 4)
-        x_turn(2, 3, 5, True)
-        x_out(2, 3, 5, "S")
-        x_quant(2, 3)
-        x_turn(3, 0, 6, True)
-        x_out(3, 0, 6, "S")
-        x_quant(3, 0)
-        w2_words_perm(0, 0)
-        x_turn(3, 1, 7, True)
-        x_out(3, 1, 7, "S")
-        x_quant(3, 1)
-        x_turn(3, 2, 0, True)
-        x_out(3, 2, 0, "S")
-        x_quant(3, 2)
-        x_turn(3, 3, 5, True)
-        x_out(3, 3, 5, "S")
-        x_quant(3, 3)
-        w2_words_perm(1, 0)
-        w2_words_perm(0, 1)
-        mm1_pair(3, 0, 1, 1)
-        mm1_pair(0, 0, 2, 2)
-        mm1_pair(1, 0, 2, 3)
-        mm1_pair(2, 0, 2, 4)
-        mm1_pair(3, 0, 2, 1)
-        mm1_pair(0, 0, 3, 2)
-        h_add(0, 0, 0, 2)
-        h_add(0, 0, 1, 2)
-        mm1_pair(1, 0, 3, 3)
-        h_add(1, 0, 0, 3)
-        h_add(1, 0, 1, 3)
-        mm1_pair(2, 0, 3, 4)
-        h_add(2, 0, 0, 4)
-        h_add(2, 0, 1, 4)
-        mm1_pair(3, 0, 3, 1)
-        h_add(3, 0, 0, 1)
-        h_add(3, 0, 1, 1)
-        w2_scales_perm(0)
-        mm1_pair(0, 1, 0, 6)
-        mm1_pair(0, 1, 1, 6)
-        mm1_pair(0, 1, 2, 6)
-        mm1_pair(0, 1, 3, 6)
-        h_add(0, 1, 0, 6)
-        h_add(0, 1, 1, 6)
-        w2_scales_perm(1)
-        mm1_pair(1, 1, 0, 7)
-        h_turn(0, 0, 0, 0)
-        h_turn(0, 0, 1, 0)
-        h_out(0, 0, 0, "S")
+        load_w1(0, 3)
+        load_w2(0)
+        load_s1(3)
+        for c in range(4):
+            load_w1(1, c)
+
+        x_sort(range(0, 4))
+        warm_up()
+        for i in (0, 1):
+            x_turn(i)
+        warm_up()
+        for i in (2, 3, 4):
+            x_turn(i)
+        spread_b1()
+        for i in (5, 6):
+            x_turn(i)
+        clear(s2_raw)
+        load_scale_rows(s2_raw, s2_hbm)
+        load_w2(1)
+        load_vec(nc.sync, "b2", b2)
+        load_vec(nc.sync, "shift", shift)
+        load_vec(nc.sync, "gain", gain)
+        for i in range(0, 3):
+            mm1(i, 0)
+        for i in range(7, 11):
+            x_turn(i)
+        for i in range(3, 7):
+            mm1(i, 0)
+        for i in (11, 12):
+            x_turn(i)
+        w2_sort_words(0, 0)
+        for i in (13, 14, 15):
+            x_turn(i)
+        w2_sort_words(1, 0)
+        for i in range(7, 12):
+            mm1(i, 0)
+        for rt in range(TILES):
+            mm1(12 + rt, 0)
+            h_add(rt, 0)
+
+        w2_sort_scales(0)
+        mm1_second_half(0)
+        h_add(0, 1)
+        w2_sort_scales(1)
+        w2_sort_words(0, 1)
+        mm1_second_half(1, range(0, 1))
+        h_turn(0, 0)
+        h_relu(0, 0, SCALAR)
         h_quant(0, 0)
-        h_turn(1, 0, 0, 5)
-        h_turn(1, 0, 1, 5)
-        h_turn(2, 0, 0, 2)
-        h_turn(2, 0, 1, 2)
-        h_turn(3, 0, 0, 3)
-        h_turn(3, 0, 1, 3)
-        h_turn(0, 1, 0, 4)
-        h_turn(0, 1, 1, 4)
-        h_out(0, 1, 4, "S")
-        h_out(1, 0, 5, "S")
-        h_out(2, 0, 2, "S")
-        h_out(3, 0, 3, "S")
+        for rt in (1, 2, 3):
+            h_turn(rt, 0)
+        h_turn(0, 1)
+        h_relu(0, 1, SCALAR)
+        for rt in (1, 2, 3):
+            h_relu(rt, 0, SCALAR)
         h_quant(0, 1)
-        w2_words_perm(1, 1)
-        mm1_pair(1, 1, 1, 7)
-        mm1_pair(1, 1, 2, 7)
-        mm1_pair(1, 1, 3, 7)
-        h_add(1, 1, 0, 7)
-        h_add(1, 1, 1, 7)
-        h_quant(1, 0)
-        h_quant(2, 0)
-        h_quant(3, 0)
-        mm2_half(0, 0, 0, 1)
-        y_act_half(0, 0, 0, 1, "S")
-        y_aff_half(0, 0, 0)
-        mm2_half(0, 0, 1, 6)
-        y_act_half(0, 0, 1, 6, "S")
-        y_aff_half(0, 0, 1)
-        mm2_half(0, 1, 0, 0)
-        y_act_half(0, 1, 0, 0, "S")
-        mm2_half(0, 1, 1, 4)
-        y_act_half(0, 1, 1, 4, "S")
-        h_turn(1, 1, 0, 5)
-        h_turn(1, 1, 1, 5)
-        h_out(1, 1, 5, "V")
-        y_aff_half(0, 1, 0)
-        y_aff_half(0, 1, 1)
-        h_quant(1, 1)
-        y_group(0, 1, 0, "V")
-        y_group(0, 1, 1, "V")
-        y_quant(0, 1, 0)
-        y_quant(0, 1, 1)
-        mm1_pair(2, 1, 0, 2)
-        mm1_pair(2, 1, 1, 2)
-        mm1_pair(2, 1, 2, 2)
-        mm1_pair(2, 1, 3, 2)
-        h_add(2, 1, 0, 2)
-        h_add(2, 1, 1, 2)
-        mm2_half(1, 0, 0, 3)
-        y_act_half(1, 0, 0, 3, "S")
-        y_aff_half(1, 0, 0)
-        mm2_half(1, 0, 1, 7)
-        y_act_half(1, 0, 1, 7, "S")
-        y_aff_half(1, 0, 1)
-        mm2_half(1, 1, 0, 1)
-        y_act_half(1, 1, 0, 1, "S")
-        mm2_half(1, 1, 1, 6)
-        y_act_half(1, 1, 1, 6, "S")
-        h_turn(2, 1, 0, 0)
-        h_turn(2, 1, 1, 0)
-        h_out(2, 1, 0, "V")
-        y_aff_half(1, 1, 0)
-        y_aff_half(1, 1, 1)
-        h_quant(2, 1)
-        y_group(1, 1, 0, "V")
-        y_group(1, 1, 1, "V")
-        y_quant(1, 1, 0)
-        y_quant(1, 1, 1)
-        y_turn(0, 0, 4)
-        y_copy(0, 0, 4, "S")
-        y_turn(0, 1, 5)
-        y_copy(0, 1, 5, "S")
-        y_store_tile(0)
+        w2_sort_words(1, 1)
+        mm1_second_half(1, range(1, 4))
+        h_add(1, 1)
+        for rt in (1, 2, 3):
+            h_quant(rt, 0)
+        stage2_beside_next_h(0)
+        mm1_second_half(2)
+        h_add(2, 1)
+        stage2_beside_next_h(1)
         store_codes(0, 2)
-        mm1_pair(3, 1, 0, 2)
-        mm1_pair(3, 1, 1, 2)
-        mm1_pair(3, 1, 2, 2)
-        mm1_pair(3, 1, 3, 2)
-        h_add(3, 1, 0, 2)
-        h_add(3, 1, 1, 2)
-        mm2_half(2, 0, 0, 3)
-        y_act_half(2, 0, 0, 3, "S")
-        y_aff_half(2, 0, 0)
-        mm2_half(2, 0, 1, 7)
-        y_act_half(2, 0, 1, 7, "S")
-        y_turn(1, 0, 1)
-        y_copy(1, 0, 1, "S")
-        h_turn(3, 1, 0, 6)
-        h_turn(3, 1, 1, 6)
-        h_out(3, 1, 6, "V")
-        y_aff_half(2, 0, 1)
+        y_turn(0, 0)
+        y_out(0, 0, SCALAR)
+        mm1_second_half(3)
+
+        mm2(2, 0, 0)
+        mm2(2, 0, 1)
+        a_relu(2, 0, 0, SCALAR)
+        h_add_part(3, 1, 0)
+        y_turn(0, 1)
+        h_turn_part(3, 1, 0)
+        h_add_part(3, 1, 1)
+        h_turn_part(3, 1, 1)
+        y_turn(1, 0)
+        y_affine(2, 0, 0)
+        a_relu(2, 0, 1, SCALAR)
+        h_relu(3, 1, VECTOR)
+        y_out(0, 1, SCALAR)
+        y_turn(1, 1)
+        mm2(2, 1, 0)
+        mm2(2, 1, 1)
+        y_affine(2, 0, 1)
+        y_out(1, 0, SCALAR)
         h_quant(3, 1)
-        y_group(2, 1, 0, "V")
-        y_turn(1, 1, 0)
-        y_copy(1, 1, 0, "S")
-        y_store_tile(1)
-        mm2_half(2, 1, 0, 4)
-        y_act_half(2, 1, 0, 4, "S")
-        y_aff_half(2, 1, 0)
-        mm2_half(2, 1, 1, 5)
-        y_act_half(2, 1, 1, 5, "S")
-        y_aff_half(2, 1, 1)
-        mm2_half(3, 0, 0, 2)
-        y_act_half(3, 0, 0, 2, "S")
-        mm2_half(3, 0, 1, 3)
-        y_act_half(3, 0, 1, 3, "V")
-        y_quant(2, 1, 0)
-        y_aff_half(3, 0, 0)
-        y_aff_half(3, 0, 1)
-        y_group(2, 1, 1, "V")
-        mm2_half(3, 1, 0, 7)
-        y_act_half(3, 1, 0, 7, "S")
-        y_aff_half(3, 1, 0)
-        mm2_half(3, 1, 1, 1)
-        y_act_half(3, 1, 1, 1, "S")
-        y_aff_half(3, 1, 1)
-        y_group(3, 1, 0, "V")
-        y_quant(2, 1, 1)
-        y_group(3, 1, 1, "V")
-        y_quant(3, 1, 0)
-        y_quant(3, 1, 1)
-        y_turn(2, 0, 6)
-        y_copy(2, 0, 6, "S")
-        y_store(2, 0, nc.sync)
-        y_turn(2, 1, 0)
-        y_copy(2, 1, 0, "S")
-        y_store(2, 1, nc.sync)
-        y_turn(3, 0, 4)
-        y_copy(3, 0, 4, "S")
-        y_store(3, 0, nc.sync)
-        y_turn(3, 1, 5)
-        y_copy(3, 1, 5, "S")
-        y_store(3, 1, nc.sync)
-        store_codes(2, 2)
-        store_scales(nc.sync)
+        mm2(3, 0, 0)
+        mm2(3, 0, 1)
+        mm2(3, 1, 0)
+        y_round(2, 0)
+        a_relu(2, 1, 0, VECTOR)
+        y_out(1, 1, SCALAR)
+        a_relu(2, 1, 1, VECTOR)
+        y_affine(2, 1, 0)
+        y_affine(2, 1, 1)
+        store_y(0)
+        y_quant(2, 0)
+        y_round(2, 1)
+        a_relu(3, 0, 0, SCALAR)
+        y_affine(3, 0, 0)
+        a_relu(3, 0, 1, SCALAR)
+        mm2(3, 1, 1)
+        y_turn(2, 0)
+        y_affine(3, 0, 1)
+        a_relu(3, 1, 1, SCALAR)
+        store_y(1)
+        y_quant(2, 1)
+        store_codes(2, 1)
+        a_relu(3, 1, 0, VECTOR)
+        y_affine(3, 1, 1)
+        y_affine(3, 1, 0)
+        y_turn(2, 1)
+        y_out(2, 0, SCALAR)
+        store_y_group(2, 0)
+        y_round(3, 0)
+        y_round(3, 1)
+        y_out(2, 1, SCALAR)
+        y_quant(3, 0)
+        store_y_group(2, 1)
+        y_turn(3, 0)
+        y_out(3, 0, SCALAR)
+        y_turn(3, 1)
+        store_y_group(3, 0)
+        y_quant(3, 1)
+        store_codes(3, 1)
+        store_scales()
+        y_out(3, 1, VECTOR)
+        store_y_group(3, 1)

@@ -54,10 +54,6 @@ def tile_box_head_region_features_h1_kernel(
         b1_rows = tile("b1_rows", [P, F], BF16)
         x_raw = [tile("x_raw%d" % i, [P, CHUNK], BF16) for i in range(BLOCKS)]
         x_sorted = [tile("x_sorted%d" % i, [P, CHUNK // 2], F32) for i in range(BLOCKS)]
-        zeros = tile("zeros", [P, 4 * GROUP], BF16)
-        zero_codes = tile("zero_codes", [P, GROUP], U32)
-        zero_scales = tile("zero_scales", [P, GROUP], U8)
-        w_warm = tile("w_warm", [P, 2 * P], U8)
         x_codes = [tile("x_codes%d" % i, [P, 2 * P], U32) for i in range(BLOCKS)]
         x_scales = [tile("x_scales%d" % i, [P, 2 * P], U8) for i in range(BLOCKS)]
         w1 = {(h, c): tile("w1_%d_%d" % (h, c), [P, 2, 2 * GROUP], U8) for h in range(2) for c in range(4)}
@@ -126,20 +122,6 @@ def tile_box_head_region_features_h1_kernel(
 
         def clear(t):
             nc.vector.memset(t[:].bitcast(I32), 0)
-
-        def warm_up():
-            bank = take("warm")
-            for repeat in range(2):
-                nc.tensor.matmul_mx(
-                    out=bank[:],
-                    lhsT=w_warm[:].bitcast(FP4X4),
-                    lhsT_scale=zero_scales[:, 0:P],
-                    rhs=zero_codes[:].bitcast(FP8X4),
-                    rhs_scale=zero_scales[:],
-                    start=True,
-                    stop=True,
-                )
-            give_back("warm")
 
         def spread_b1():
             bank = take("b1")
@@ -326,14 +308,11 @@ def tile_box_head_region_features_h1_kernel(
             for g in range(2):
                 y_quant(rt, g)
 
-        nc.scalar.dma_start(out=w_warm[:].bitcast(I32), in_=w1_hbm[0, :, 0:64])
         load_vec(nc.scalar, "b1", b1)
         make_identity(nc, ident[:])
         clear(s1_parts[0])
         clear(s1_parts[1])
         nc.vector.memset(table_warm[:, 0:8], 0.0)
-        nc.vector.memset(zeros[:].bitcast(I32), 0)
-        nc.vector.quantize_mx(out=zero_codes[:].bitcast(FP8X4), scales=zero_scales[:], in_=zeros[:])
         nc.scalar.activation(out=table_warm[:, 8:16], in_=table_warm[:, 0:8], func=ACT.Relu)
         clear(s1_parts[2])
         clear(s1_parts[3])
@@ -354,10 +333,8 @@ def tile_box_head_region_features_h1_kernel(
             load_w1(1, c)
 
         x_sort(range(0, 4))
-        warm_up()
         for i in (0, 1):
             x_turn(i)
-        warm_up()
         for i in (2, 3, 4):
             x_turn(i)
         spread_b1()

@@ -10,6 +10,7 @@ F32 = mybir.dt.float32
 BF16 = mybir.dt.bfloat16
 U32 = mybir.dt.uint32
 I32 = mybir.dt.int32
+U16 = mybir.dt.uint16
 U8 = mybir.dt.uint8
 FP8X4 = mybir.dt.float8_e4m3fn_x4
 FP4X4 = mybir.dt.float4_e2m1fn_x4
@@ -24,7 +25,10 @@ BLOCKS = TILES * D // CHUNK
 SCALAR, VECTOR = "scalar", "vector"
 
 W1_SCALE_PARTS = [(0, 0, 2), (0, 2, 4), (0, 4, 8), (1, 0, 8)]
-SORT_AFTER_QUANT = {0: [4, 5, 6], 2: [7, 8, 9], 3: [10], 7: [11], 8: [12], 10: [13, 14, 15]}
+RUNS = (1, 1, 2, 2, 3, 3, 3)
+UNSORTED = 2
+X_LEAD = 2
+EARLY_CHUNKS = 2
 
 
 def tile_box_head_region_features_h1_kernel(
@@ -128,27 +132,55 @@ def tile_box_head_region_features_h1_kernel(
             words = vec["b1"][:].rearrange("p g t -> p (g t)").bitcast(F32)
             for j in range(4):
                 nc.tensor.transpose(bank[:, P * j : P * (j + 1)], words[:, j : j + 1].to_broadcast([P, P]), ident[:])
-            nc.scalar.copy(out=b1_rows[:].bitcast(F32), in_=bank[:])
+            nc.vector.tensor_copy(out=b1_rows[:].bitcast(F32), in_=bank[:])
             give_back("b1")
 
         def x_sort(blocks):
             for i in blocks:
+                if i < UNSORTED:
+                    continue
                 nc.vector.tensor_copy(
                     out=x_sorted[i][:].rearrange("r (g u m) -> r g u m", g=2, u=2),
                     in_=x_raw[i][:].bitcast(F32).rearrange("r (g m u) -> r g u m", g=2, u=2),
                 )
 
+        def x_words(i, g, u):
+            if i < UNSORTED:
+                return x_raw[i][:].bitcast(F32)[:, 2 * P * g + u : 2 * P * (g + 1) : 2]
+            return x_sorted[i][:, P * (2 * g + u) : P * (2 * g + u + 1)]
+
+        def x_turned(i):
+            return x_sorted[i][:] if i < UNSORTED else x_raw[i][:].bitcast(F32)
+
         def x_turn(i):
             bank = take(("x", i))
-            for j in range(4):
-                nc.tensor.transpose(bank[:, P * j : P * (j + 1)], x_sorted[i][:, P * j : P * (j + 1)], ident[:])
+            for g in range(2):
+                for u in range(2):
+                    j = 2 * g + u
+                    nc.tensor.transpose(bank[:, P * j : P * (j + 1)], x_words(i, g, u), ident[:])
             nc.scalar.copy(
-                out=x_raw[i][:].bitcast(F32).rearrange("p (g r u) -> p g r u", g=2, u=2),
+                out=x_turned(i).rearrange("p (g r u) -> p g r u", g=2, u=2),
                 in_=bank[:].rearrange("p (g u r) -> p g r u", g=2, u=2),
             )
             give_back(("x", i))
-            nc.vector.quantize_mx(out=x_codes[i][:].bitcast(FP8X4), scales=x_scales[i][:], in_=x_raw[i][:])
-            x_sort(SORT_AFTER_QUANT.get(i, []))
+
+        def x_quant(i):
+            nc.vector.quantize_mx(out=x_codes[i][:].bitcast(FP8X4), scales=x_scales[i][:], in_=x_turned(i).bitcast(BF16))
+
+        def x_turn_first():
+            for g in range(2):
+                bank = take(("x0", g))
+                for u in range(2):
+                    nc.tensor.transpose(bank[:, P * u : P * (u + 1)], x_words(0, g, u), ident[:])
+            for g in range(2):
+                turned = x_sorted[0][:, 2 * P * g : 2 * P * (g + 1)]
+                nc.scalar.copy(
+                    out=turned.rearrange("p (r u) -> p r u", u=2),
+                    in_=bank_of(("x0", g))[:, 0 : 2 * P].rearrange("p (u r) -> p r u", u=2),
+                )
+                give_back(("x0", g))
+                cols = slice(P * g, P * (g + 1))
+                nc.vector.quantize_mx(out=x_codes[0][:, cols].bitcast(FP8X4), scales=x_scales[0][:, cols], in_=turned.bitcast(BF16))
 
         def mm1(i, h):
             c, rt = divmod(i, TILES)
@@ -207,8 +239,8 @@ def tile_box_head_region_features_h1_kernel(
 
         def w2_sort_words(h, g):
             nc.vector.tensor_copy(
-                out=w2[:, h, 2 * GROUP * g : 2 * GROUP * (g + 1)].rearrange("p (t m b) -> p t m b", t=4, b=2),
-                in_=w2_raw[g][:, h, :].rearrange("p (m t b) -> p t m b", t=4, b=2),
+                out=w2[:, h, 2 * GROUP * g : 2 * GROUP * (g + 1)].bitcast(U16).rearrange("p (t m) -> p t m", t=4),
+                in_=w2_raw[g][:, h, :].bitcast(U16).rearrange("p (m t) -> p t m", t=4),
             )
 
         def w2_sort_scales(h):
@@ -217,10 +249,10 @@ def tile_box_head_region_features_h1_kernel(
                 in_=s2_raw[:, h, :].rearrange("p (g m t) -> p g t m", g=2, t=4),
             )
 
-        def mm2(rt, g, pair):
-            bank = take(("z", rt, g, pair))
-            for j in range(2):
-                col = GROUP * g + P * (2 * pair + j)
+        def mm2(rt, g, slices):
+            bank = take(("z", rt, g, slices))
+            for j, t in enumerate(slices):
+                col = GROUP * g + P * t
                 for h in range(2):
                     nc.tensor.matmul_mx(
                         out=bank[:, P * j : P * (j + 1)],
@@ -232,19 +264,18 @@ def tile_box_head_region_features_h1_kernel(
                         stop=(h == 1),
                     )
 
-        def a_relu(rt, g, pair, engine):
-            bank = bank_of(("z", rt, g, pair))
-            for j in range(2):
-                t = 2 * pair + j
+        def a_relu(rt, g, slices, engine):
+            bank = bank_of(("z", rt, g, slices))
+            for j, t in enumerate(slices):
                 src, dst, bias = bank[:, P * j : P * (j + 1)], a_t[g][:, t, regions(rt)], vec["b2"][:, g, t : t + 1]
                 if engine == SCALAR:
                     nc.scalar.activation(out=dst, in_=src, func=ACT.Relu, bias=bias)
                 else:
                     nc.vector.tensor_scalar(out=dst, in0=src, scalar1=bias, scalar2=0.0, op0=ALU.add, op1=ALU.max)
-            give_back(("z", rt, g, pair))
+            give_back(("z", rt, g, slices))
 
-        def y_affine(rt, g, pair):
-            for t in (2 * pair, 2 * pair + 1):
+        def y_affine(rt, g, slices):
+            for t in slices:
                 nc.vector.tensor_scalar(
                     out=y_t[g][:, t, regions(rt)],
                     in0=a_t[g][:, t, regions(rt)],
@@ -276,11 +307,12 @@ def tile_box_head_region_features_h1_kernel(
             )
             give_back(("y", rt, g))
 
-        def store_y(rt, cols=slice(0, N)):
-            nc.sync.dma_start(out=out_0[regions(rt), cols], in_=y_rows[rt][:, cols])
+        def store_y(rt):
+            nc.sync.dma_start(out=out_0[regions(rt), :], in_=y_rows[rt][:])
 
-        def store_y_group(rt, g):
-            store_y(rt, slice(GROUP * g, GROUP * (g + 1)))
+        def store_y_group(rt, g, queue):
+            cols = slice(GROUP * g, GROUP * (g + 1))
+            queue.dma_start(out=out_0[regions(rt), cols], in_=y_rows[rt][:, cols])
 
         def store_codes(rt, count):
             nc.sync.dma_start(out=codes_hbm[:, :, regions(rt, count)], in_=y_codes[:, :, regions(rt, count)].bitcast(I32))
@@ -290,168 +322,132 @@ def tile_box_head_region_features_h1_kernel(
                 dst = scales_hbm[:, r:16:4, :].rearrange("g q n -> q g n")
                 nc.sync.dma_start(out=dst, in_=y_scales[r:P:32].bitcast(I32))
 
-        def stage2_beside_next_h(rt):
-            for pair in range(2):
-                mm2(rt, 0, pair)
-                a_relu(rt, 0, pair, SCALAR)
-                y_affine(rt, 0, pair)
-            for pair in range(2):
-                mm2(rt, 1, pair)
-                a_relu(rt, 1, pair, SCALAR)
-            h_turn(rt + 1, 1)
-            h_relu(rt + 1, 1, VECTOR)
-            for pair in range(2):
-                y_affine(rt, 1, pair)
-            h_quant(rt + 1, 1)
+        load_vec(nc.scalar, "b1", b1)
+        make_identity(nc, ident[:])
+        clear(s1_parts[0])
+        nc.vector.memset(table_warm[:, 0:8], 0.0)
+        nc.scalar.activation(out=table_warm[:, 8:16], in_=table_warm[:, 0:8], func=ACT.Relu)
+        clear(s1_parts[1])
+        clear(s1_parts[2])
+        clear(s1_parts[3])
+        clear(s2_raw)
+
+        load_x(range(0, X_LEAD))
+        for c in range(4):
+            load_w1(0, c)
+            if c < 3:
+                load_s1(c)
+            load_x(range(TILES * c + X_LEAD, min(BLOCKS, TILES * (c + 1) + X_LEAD)))
+        load_s1(3)
+        for c in range(4):
+            load_w1(1, c)
+        load_vec(nc.sync, "b2", b2)
+        load_vec(nc.sync, "shift", shift)
+        load_vec(nc.sync, "gain", gain)
+        load_scale_rows(s2_raw, s2_hbm)
+        load_w2(0)
+        load_w2(1)
+
+        spread_b1()
+        x_turn_first()
+        runs, start = [], 1
+        for length in RUNS:
+            runs.append(list(range(start, start + length)))
+            start += length
+        x_sort(runs[0])
+        waiting = [0]
+        for run, following in zip(runs, runs[1:] + [[]]):
+            for i in run:
+                x_turn(i)
+            x_sort(following)
+            for i in run:
+                x_quant(i)
+            for i in waiting:
+                mm1(i, 0)
+            waiting = run
+        for i in waiting:
+            mm1(i, 0)
+        for rt in range(TILES):
+            h_add(rt, 0)
+
+        early, late = range(0, EARLY_CHUNKS), range(EARLY_CHUNKS, 4)
+        ALL = (0, 1, 2, 3)
+        last = TILES - 1
+        for h in range(2):
+            w2_sort_scales(h)
+        mm1_second_half(0)
+        h_add(0, 1)
+        mm1_second_half(1, early)
+        first = [(0, 0), (0, 1), (1, 0), (2, 0), (3, 0)]
+        for key in first:
+            h_turn(*key)
+            h_relu(*key, SCALAR)
+        for h in range(2):
+            w2_sort_words(h, 0)
+        for key in first[:2]:
+            h_quant(*key)
+        for h in range(2):
+            w2_sort_words(h, 1)
+        for key in first[2:]:
+            h_quant(*key)
+
+        def planes(rt):
             for g in range(2):
                 y_round(rt, g)
             for g in range(2):
                 y_quant(rt, g)
+            store_codes(rt, 1)
 
-        load_vec(nc.scalar, "b1", b1)
-        make_identity(nc, ident[:])
-        clear(s1_parts[0])
-        clear(s1_parts[1])
-        nc.vector.memset(table_warm[:, 0:8], 0.0)
-        nc.scalar.activation(out=table_warm[:, 8:16], in_=table_warm[:, 0:8], func=ACT.Relu)
-        clear(s1_parts[2])
-        clear(s1_parts[3])
+        for rt in range(last - 1):
+            mm1_second_half(rt + 1, late)
+            h_add(rt + 1, 1)
+            for g in range(2):
+                mm2(rt, g, ALL)
+                a_relu(rt, g, ALL, SCALAR)
+            mm1_second_half(rt + 2, early)
+            h_turn(rt + 1, 1)
+            y_affine(rt, 0, ALL)
+            y_affine(rt, 1, ALL)
+            h_relu(rt + 1, 1, VECTOR)
+            h_quant(rt + 1, 1)
+            for g in range(2):
+                y_turn(rt, g)
+                y_out(rt, g, SCALAR)
+            store_y(rt)
+            planes(rt)
 
-        load_x(range(0, 7))
-        load_w1(0, 0)
-        load_s1(0)
-        load_x(range(7, 11))
-        load_w1(0, 1)
-        load_s1(1)
-        load_x(range(11, 16))
-        load_w1(0, 2)
-        load_s1(2)
-        load_w1(0, 3)
-        load_w2(0)
-        load_s1(3)
-        for c in range(4):
-            load_w1(1, c)
-
-        x_sort(range(0, 4))
-        for i in (0, 1):
-            x_turn(i)
-        for i in (2, 3, 4):
-            x_turn(i)
-        spread_b1()
-        for i in (5, 6):
-            x_turn(i)
-        clear(s2_raw)
-        load_scale_rows(s2_raw, s2_hbm)
-        load_w2(1)
-        load_vec(nc.sync, "b2", b2)
-        load_vec(nc.sync, "shift", shift)
-        load_vec(nc.sync, "gain", gain)
-        for i in range(0, 3):
-            mm1(i, 0)
-        for i in range(7, 11):
-            x_turn(i)
-        for i in range(3, 7):
-            mm1(i, 0)
-        for i in (11, 12):
-            x_turn(i)
-        w2_sort_words(0, 0)
-        for i in (13, 14, 15):
-            x_turn(i)
-        w2_sort_words(1, 0)
-        for i in range(7, 12):
-            mm1(i, 0)
-        for rt in range(TILES):
-            mm1(12 + rt, 0)
-            h_add(rt, 0)
-
-        w2_sort_scales(0)
-        mm1_second_half(0)
-        h_add(0, 1)
-        w2_sort_scales(1)
-        w2_sort_words(0, 1)
-        mm1_second_half(1, range(0, 1))
-        h_turn(0, 0)
-        h_relu(0, 0, SCALAR)
-        h_quant(0, 0)
-        for rt in (1, 2, 3):
-            h_turn(rt, 0)
-        h_turn(0, 1)
-        h_relu(0, 1, SCALAR)
-        for rt in (1, 2, 3):
-            h_relu(rt, 0, SCALAR)
-        h_quant(0, 1)
-        w2_sort_words(1, 1)
-        mm1_second_half(1, range(1, 4))
-        h_add(1, 1)
-        for rt in (1, 2, 3):
-            h_quant(rt, 0)
-        stage2_beside_next_h(0)
-        mm1_second_half(2)
-        h_add(2, 1)
-        stage2_beside_next_h(1)
-        store_codes(0, 2)
-        y_turn(0, 0)
-        y_out(0, 0, SCALAR)
-        mm1_second_half(3)
-
-        mm2(2, 0, 0)
-        mm2(2, 0, 1)
-        a_relu(2, 0, 0, SCALAR)
-        h_add_part(3, 1, 0)
-        y_turn(0, 1)
-        h_turn_part(3, 1, 0)
-        h_add_part(3, 1, 1)
-        h_turn_part(3, 1, 1)
-        y_turn(1, 0)
-        y_affine(2, 0, 0)
-        a_relu(2, 0, 1, SCALAR)
-        h_relu(3, 1, VECTOR)
-        y_out(0, 1, SCALAR)
-        y_turn(1, 1)
-        mm2(2, 1, 0)
-        mm2(2, 1, 1)
-        y_affine(2, 0, 1)
-        y_out(1, 0, SCALAR)
-        h_quant(3, 1)
-        mm2(3, 0, 0)
-        mm2(3, 0, 1)
-        mm2(3, 1, 0)
-        y_round(2, 0)
-        a_relu(2, 1, 0, VECTOR)
-        y_out(1, 1, SCALAR)
-        a_relu(2, 1, 1, VECTOR)
-        y_affine(2, 1, 0)
-        y_affine(2, 1, 1)
-        store_y(0)
-        y_quant(2, 0)
-        y_round(2, 1)
-        a_relu(3, 0, 0, SCALAR)
-        y_affine(3, 0, 0)
-        a_relu(3, 0, 1, SCALAR)
-        mm2(3, 1, 1)
-        y_turn(2, 0)
-        y_affine(3, 0, 1)
-        a_relu(3, 1, 1, SCALAR)
-        store_y(1)
-        y_quant(2, 1)
-        store_codes(2, 1)
-        a_relu(3, 1, 0, VECTOR)
-        y_affine(3, 1, 1)
-        y_affine(3, 1, 0)
-        y_turn(2, 1)
-        y_out(2, 0, SCALAR)
-        store_y_group(2, 0)
-        y_round(3, 0)
-        y_round(3, 1)
-        y_out(2, 1, SCALAR)
-        y_quant(3, 0)
-        store_y_group(2, 1)
-        y_turn(3, 0)
-        y_out(3, 0, SCALAR)
-        y_turn(3, 1)
-        store_y_group(3, 0)
-        y_quant(3, 1)
-        store_codes(3, 1)
+        rt = last - 1
+        pairs = [(g, pair) for g in range(2) for pair in ((0, 1), (2, 3))]
+        mm1_second_half(last, late)
+        h_add(last, 1)
+        for g, pair in pairs:
+            mm2(rt, g, pair)
+            a_relu(rt, g, pair, SCALAR)
+        h_turn(last, 1)
+        for g, pair in pairs[:3]:
+            y_affine(rt, g, pair)
+        h_relu(last, 1, VECTOR)
+        y_affine(rt, *pairs[3])
+        h_quant(last, 1)
+        for g in range(2):
+            y_turn(rt, g)
+            y_out(rt, g, SCALAR)
+            store_y_group(rt, g, nc.sync)
+        planes(rt)
+        for g, pair in pairs:
+            mm2(last, g, pair)
+            a_relu(last, g, pair, SCALAR)
+        for g, pair in pairs[:3]:
+            y_affine(last, g, pair)
+        y_round(last, 0)
+        y_affine(last, *pairs[3])
+        y_quant(last, 0)
+        y_round(last, 1)
+        y_quant(last, 1)
+        for g in range(2):
+            y_turn(last, g)
+            y_out(last, g, SCALAR)
+        store_y_group(last, 0, nc.sync)
+        store_codes(last, 1)
         store_scales()
-        y_out(3, 1, VECTOR)
-        store_y_group(3, 1)
+        store_y_group(last, 1, nc.scalar)

@@ -28,7 +28,7 @@ W1_SCALE_PARTS = [(0, 0, 2), (0, 2, 4), (0, 4, 8), (1, 0, 8)]
 RUNS = (1, 1, 2, 2, 3, 3, 3)
 UNSORTED = 2
 X_LEAD = 2
-EARLY_CHUNKS = 2
+EARLY_CHUNKS = 1
 
 
 def tile_box_head_region_features_h1_kernel(
@@ -73,8 +73,8 @@ def tile_box_head_region_features_h1_kernel(
         h_turned = {key: tile("h_turned%d_%d" % key, [P, GROUP], BF16) for key in halves}
         h_codes = {key: tile("h_codes%d_%d" % key, [P, P], U32) for key in halves}
         h_scales = {key: tile("h_scales%d_%d" % key, [P, P], U8) for key in halves}
-        a_t = [tile("a_t%d" % g, [P, 4, R], F32) for g in range(2)]
-        y_t = [tile("y_t%d" % g, [P, 4, R], F32) for g in range(2)]
+        a_t = {key: tile("a_t%d_%d" % key, [P, 4, P], F32) for key in halves}
+        y_t = {key: tile("y_t%d_%d" % key, [P, 4, P], F32) for key in halves}
         y_bf16 = [tile("y_bf16_%d" % g, [P, R, 4], BF16) for g in range(2)]
         y_codes = tile("y_codes", [P, 2, R], U32)
         y_scales = tile("y_scales", [P, 2, R], U8)
@@ -243,11 +243,18 @@ def tile_box_head_region_features_h1_kernel(
                 in_=w2_raw[g][:, h, :].bitcast(U16).rearrange("p (m t) -> p t m", t=4),
             )
 
-        def w2_sort_scales(h):
+        def w2_sort_scales(h, g):
+            cols = slice(GROUP * g, GROUP * (g + 1))
             nc.vector.tensor_copy(
-                out=s2[:, h, :].rearrange("p (g t m) -> p g t m", g=2, t=4),
-                in_=s2_raw[:, h, :].rearrange("p (g m t) -> p g t m", g=2, t=4),
+                out=s2[:, h, cols].rearrange("p (t m) -> p t m", t=4),
+                in_=s2_raw[:, h, cols].rearrange("p (m t) -> p t m", t=4),
             )
+
+        def w2_sort(g):
+            for h in range(2):
+                w2_sort_scales(h, g)
+            for h in range(2):
+                w2_sort_words(h, g)
 
         def mm2(rt, g, slices):
             bank = take(("z", rt, g, slices))
@@ -267,7 +274,7 @@ def tile_box_head_region_features_h1_kernel(
         def a_relu(rt, g, slices, engine):
             bank = bank_of(("z", rt, g, slices))
             for j, t in enumerate(slices):
-                src, dst, bias = bank[:, P * j : P * (j + 1)], a_t[g][:, t, regions(rt)], vec["b2"][:, g, t : t + 1]
+                src, dst, bias = bank[:, P * j : P * (j + 1)], a_t[rt, g][:, t, :], vec["b2"][:, g, t : t + 1]
                 if engine == SCALAR:
                     nc.scalar.activation(out=dst, in_=src, func=ACT.Relu, bias=bias)
                 else:
@@ -277,8 +284,8 @@ def tile_box_head_region_features_h1_kernel(
         def y_affine(rt, g, slices):
             for t in slices:
                 nc.vector.tensor_scalar(
-                    out=y_t[g][:, t, regions(rt)],
-                    in0=a_t[g][:, t, regions(rt)],
+                    out=y_t[rt, g][:, t, :],
+                    in0=a_t[rt, g][:, t, :],
                     scalar1=vec["shift"][:, g, t : t + 1],
                     scalar2=vec["gain"][:, g, t : t + 1],
                     op0=ALU.add,
@@ -286,7 +293,7 @@ def tile_box_head_region_features_h1_kernel(
                 )
 
         def y_round(rt, g):
-            nc.vector.tensor_copy(out=y_bf16[g][:, regions(rt), :], in_=y_t[g][:, :, regions(rt)].rearrange("p t r -> p r t"))
+            nc.vector.tensor_copy(out=y_bf16[g][:, regions(rt), :], in_=y_t[rt, g][:].rearrange("p t r -> p r t"))
 
         def y_quant(rt, g):
             nc.vector.quantize_mx(
@@ -298,7 +305,7 @@ def tile_box_head_region_features_h1_kernel(
         def y_turn(rt, g):
             bank = take(("y", rt, g))
             for t in range(4):
-                nc.tensor.transpose(bank[:, P * t : P * (t + 1)], y_t[g][:, t, regions(rt)], ident[:])
+                nc.tensor.transpose(bank[:, P * t : P * (t + 1)], y_t[rt, g][:, t, :], ident[:])
 
         def y_out(rt, g, engine):
             copy_on(engine)(
@@ -306,6 +313,19 @@ def tile_box_head_region_features_h1_kernel(
                 in_=bank_of(("y", rt, g))[:].rearrange("r (t p) -> r p t", t=4),
             )
             give_back(("y", rt, g))
+
+        def y_turn_blocks(rt, g):
+            nc.vector.transpose(out=a_t[rt, g][:].rearrange("p t r -> p (t r)"), in_=y_t[rt, g][:].rearrange("p t r -> p (t r)"))
+
+        def y_out_blocks(rt, g):
+            nc.scalar.copy(
+                out=y_rows[rt][:, GROUP * g : GROUP * (g + 1)].rearrange("p (b j t) -> p b j t", b=4, t=4),
+                in_=a_t[rt, g][:].rearrange("p t (b j) -> p b j t", b=4),
+            )
+            for q in (0, 2, 1, 3):
+                dst = out_0[regions(rt), GROUP * g + P * q : GROUP * g + P * (q + 1)].rearrange("(b i) c -> i b c", b=4)
+                src = y_rows[rt][32 * q : 32 * (q + 1), GROUP * g : GROUP * (g + 1)].rearrange("i (b c) -> i b c", b=4)
+                nc.sync.dma_start(out=dst, in_=src)
 
         def store_y(rt):
             nc.sync.dma_start(out=out_0[regions(rt), :], in_=y_rows[rt][:])
@@ -332,28 +352,30 @@ def tile_box_head_region_features_h1_kernel(
         clear(s1_parts[3])
         clear(s2_raw)
 
-        load_x(range(0, X_LEAD))
-        for c in range(4):
-            load_w1(0, c)
-            if c < 3:
-                load_s1(c)
-            load_x(range(TILES * c + X_LEAD, min(BLOCKS, TILES * (c + 1) + X_LEAD)))
-        load_s1(3)
-        for c in range(4):
-            load_w1(1, c)
-        load_vec(nc.sync, "b2", b2)
-        load_vec(nc.sync, "shift", shift)
-        load_vec(nc.sync, "gain", gain)
-        load_scale_rows(s2_raw, s2_hbm)
-        load_w2(0)
-        load_w2(1)
-
-        spread_b1()
-        x_turn_first()
         runs, start = [], 1
         for length in RUNS:
             runs.append(list(range(start, start + length)))
             start += length
+
+        load_x([0])
+        for run, before in zip(runs + [[]], [[0]] + runs):
+            load_x(run)
+            for c in [i // TILES for i in before if i % TILES == 0]:
+                load_w1(0, c)
+                if c < 3:
+                    load_s1(c)
+        load_s1(3)
+        for c in range(4):
+            load_w1(1, c)
+        load_scale_rows(s2_raw, s2_hbm)
+        load_w2(0)
+        load_w2(1)
+        load_vec(nc.sync, "b2", b2)
+        load_vec(nc.sync, "shift", shift)
+        load_vec(nc.sync, "gain", gain)
+
+        spread_b1()
+        x_turn_first()
         x_sort(runs[0])
         waiting = [0]
         for run, following in zip(runs, runs[1:] + [[]]):
@@ -370,80 +392,99 @@ def tile_box_head_region_features_h1_kernel(
         for rt in range(TILES):
             h_add(rt, 0)
 
-        early, late = range(0, EARLY_CHUNKS), range(EARLY_CHUNKS, 4)
         ALL = (0, 1, 2, 3)
         last = TILES - 1
-        for h in range(2):
-            w2_sort_scales(h)
         mm1_second_half(0)
         h_add(0, 1)
-        mm1_second_half(1, early)
+        mm1_second_half(1, range(0, EARLY_CHUNKS))
+        for rt in range(TILES):
+            h_turn(rt, 0)
+        h_turn(0, 1)
         first = [(0, 0), (0, 1), (1, 0), (2, 0), (3, 0)]
         for key in first:
-            h_turn(*key)
             h_relu(*key, SCALAR)
-        for h in range(2):
-            w2_sort_words(h, 0)
+        w2_sort(0)
         for key in first[:2]:
             h_quant(*key)
-        for h in range(2):
-            w2_sort_words(h, 1)
-        for key in first[2:]:
-            h_quant(*key)
+        w2_sort(1)
+        mm1_second_half(1, range(EARLY_CHUNKS, 4))
 
         def planes(rt):
             for g in range(2):
                 y_round(rt, g)
             for g in range(2):
                 y_quant(rt, g)
-            store_codes(rt, 1)
 
         for rt in range(last - 1):
-            mm1_second_half(rt + 1, late)
             h_add(rt + 1, 1)
+            if rt == 0:
+                for key in first[2:]:
+                    h_quant(*key)
+            else:
+                for g in range(2):
+                    y_quant(rt - 1, g)
             for g in range(2):
                 mm2(rt, g, ALL)
                 a_relu(rt, g, ALL, SCALAR)
-            mm1_second_half(rt + 2, early)
             h_turn(rt + 1, 1)
+            h_relu(rt + 1, 1, SCALAR)
             y_affine(rt, 0, ALL)
             y_affine(rt, 1, ALL)
-            h_relu(rt + 1, 1, VECTOR)
+            y_turn_blocks(rt, 0)
             h_quant(rt + 1, 1)
-            for g in range(2):
-                y_turn(rt, g)
-                y_out(rt, g, SCALAR)
-            store_y(rt)
-            planes(rt)
+            if rt == 0:
+                y_turn_blocks(rt, 1)
+            y_round(rt, 0)
+            y_out_blocks(rt, 0)
+            if rt == 0:
+                y_out_blocks(rt, 1)
+            y_round(rt, 1)
+            mm1_second_half(rt + 2)
 
         rt = last - 1
         pairs = [(g, pair) for g in range(2) for pair in ((0, 1), (2, 3))]
-        mm1_second_half(last, late)
         h_add(last, 1)
-        for g, pair in pairs:
-            mm2(rt, g, pair)
-            a_relu(rt, g, pair, SCALAR)
-        h_turn(last, 1)
-        for g, pair in pairs[:3]:
-            y_affine(rt, g, pair)
-        h_relu(last, 1, VECTOR)
-        y_affine(rt, *pairs[3])
-        h_quant(last, 1)
         for g in range(2):
-            y_turn(rt, g)
-            y_out(rt, g, SCALAR)
-            store_y_group(rt, g, nc.sync)
-        planes(rt)
-        for g, pair in pairs:
+            y_quant(rt - 1, g)
+        store_codes(0, last - 1)
+        mm2(rt, 0, ALL)
+        a_relu(rt, 0, ALL, SCALAR)
+        y_turn(rt - 1, 1)
+        y_out(rt - 1, 1, SCALAR)
+        store_y_group(rt - 1, 1, nc.sync)
+        h_turn(last, 1)
+        h_relu(last, 1, VECTOR)
+        y_affine(rt, 0, ALL)
+        h_quant(last, 1)
+        mm2(rt, 1, ALL)
+        a_relu(rt, 1, ALL, SCALAR)
+        y_round(rt, 0)
+        y_turn(rt, 0)
+        y_out(rt, 0, SCALAR)
+        store_y_group(rt, 0, nc.sync)
+        y_quant(rt, 0)
+        y_affine(rt, 1, ALL)
+        for g, pair in pairs[:2]:
             mm2(last, g, pair)
             a_relu(last, g, pair, SCALAR)
-        for g, pair in pairs[:3]:
-            y_affine(last, g, pair)
-        y_round(last, 0)
+        y_round(rt, 1)
+        y_turn(rt, 1)
+        y_affine(last, *pairs[0])
+        y_quant(rt, 1)
+        store_codes(rt, 1)
+        y_affine(last, *pairs[1])
+        for g, pair in pairs[2:]:
+            mm2(last, g, pair)
+        y_out(rt, 1, SCALAR)
+        store_y_group(rt, 1, nc.sync)
+        a_relu(last, *pairs[2], VECTOR)
+        a_relu(last, *pairs[3], SCALAR)
+        y_affine(last, *pairs[2])
         y_affine(last, *pairs[3])
-        y_quant(last, 0)
-        y_round(last, 1)
-        y_quant(last, 1)
+        for g in range(2):
+            y_round(last, g)
+        for g in range(2):
+            y_quant(last, g)
         for g in range(2):
             y_turn(last, g)
             y_out(last, g, SCALAR)

@@ -25,10 +25,11 @@ BLOCKS = TILES * D // CHUNK
 SCALAR, VECTOR = "scalar", "vector"
 
 W1_SCALE_PARTS = [(0, 0, 2), (0, 2, 4), (0, 4, 8), (1, 0, 8)]
-RUNS = (1, 1, 2, 2, 3, 3, 3)
-UNSORTED = 2
+RUN_ENDS = (6, 11, 16)
+LAG = 3
+UNSORTED = 0
 X_LEAD = 2
-EARLY_CHUNKS = 1
+EARLY_CHUNKS = 2
 
 
 def tile_box_head_region_features_h1_kernel(
@@ -132,7 +133,7 @@ def tile_box_head_region_features_h1_kernel(
             words = vec["b1"][:].rearrange("p g t -> p (g t)").bitcast(F32)
             for j in range(4):
                 nc.tensor.transpose(bank[:, P * j : P * (j + 1)], words[:, j : j + 1].to_broadcast([P, P]), ident[:])
-            nc.vector.tensor_copy(out=b1_rows[:].bitcast(F32), in_=bank[:])
+            nc.scalar.copy(out=b1_rows[:].bitcast(F32), in_=bank[:])
             give_back("b1")
 
         def x_sort(blocks):
@@ -352,15 +353,13 @@ def tile_box_head_region_features_h1_kernel(
         clear(s1_parts[3])
         clear(s2_raw)
 
-        runs, start = [], 1
-        for length in RUNS:
-            runs.append(list(range(start, start + length)))
-            start += length
+        turns = [range(a, b) for a, b in zip((0,) + RUN_ENDS, RUN_ENDS)]
+        pass_ends = tuple(end - LAG for end in RUN_ENDS[:-1]) + (BLOCKS,)
+        passes = [range(a, b) for a, b in zip((0,) + pass_ends, pass_ends)]
 
-        load_x([0])
-        for run, before in zip(runs + [[]], [[0]] + runs):
-            load_x(run)
-            for c in [i // TILES for i in before if i % TILES == 0]:
+        for turn, done in zip(turns, passes):
+            load_x(turn)
+            for c in [i // TILES for i in done if i % TILES == 0]:
                 load_w1(0, c)
                 if c < 3:
                     load_s1(c)
@@ -375,39 +374,24 @@ def tile_box_head_region_features_h1_kernel(
         load_vec(nc.sync, "gain", gain)
 
         spread_b1()
-        x_turn_first()
-        x_sort(runs[0])
-        waiting = [0]
-        for run, following in zip(runs, runs[1:] + [[]]):
-            for i in run:
+        for turn, done in zip(turns, passes):
+            x_sort(turn)
+            for i in done:
+                if i < turn.start:
+                    x_quant(i)
+            for i in turn:
                 x_turn(i)
-            x_sort(following)
-            for i in run:
-                x_quant(i)
-            for i in waiting:
+            for i in done:
+                if i >= turn.start:
+                    x_quant(i)
+            for i in done:
                 mm1(i, 0)
-            waiting = run
-        for i in waiting:
-            mm1(i, 0)
         for rt in range(TILES):
             h_add(rt, 0)
 
         ALL = (0, 1, 2, 3)
-        last = TILES - 1
-        mm1_second_half(0)
-        h_add(0, 1)
-        mm1_second_half(1, range(0, EARLY_CHUNKS))
-        for rt in range(TILES):
-            h_turn(rt, 0)
-        h_turn(0, 1)
-        first = [(0, 0), (0, 1), (1, 0), (2, 0), (3, 0)]
-        for key in first:
-            h_relu(*key, SCALAR)
-        w2_sort(0)
-        for key in first[:2]:
-            h_quant(*key)
-        w2_sort(1)
-        mm1_second_half(1, range(EARLY_CHUNKS, 4))
+        pairs = [(g, pair) for g in range(2) for pair in ((0, 1), (2, 3))]
+        front, back = range(0, 2), range(2, 4)
 
         def planes(rt):
             for g in range(2):
@@ -415,80 +399,84 @@ def tile_box_head_region_features_h1_kernel(
             for g in range(2):
                 y_quant(rt, g)
 
-        for rt in range(last - 1):
-            h_add(rt + 1, 1)
-            if rt == 0:
-                for key in first[2:]:
-                    h_quant(*key)
-            else:
-                for g in range(2):
-                    y_quant(rt - 1, g)
+        def stage2(rt):
             for g in range(2):
                 mm2(rt, g, ALL)
                 a_relu(rt, g, ALL, SCALAR)
-            h_turn(rt + 1, 1)
-            h_relu(rt + 1, 1, SCALAR)
-            y_affine(rt, 0, ALL)
-            y_affine(rt, 1, ALL)
-            y_turn_blocks(rt, 0)
-            h_quant(rt + 1, 1)
-            if rt == 0:
-                y_turn_blocks(rt, 1)
-            y_round(rt, 0)
-            y_out_blocks(rt, 0)
-            if rt == 0:
-                y_out_blocks(rt, 1)
-            y_round(rt, 1)
-            mm1_second_half(rt + 2)
+                y_affine(rt, g, ALL)
 
-        rt = last - 1
-        pairs = [(g, pair) for g in range(2) for pair in ((0, 1), (2, 3))]
-        h_add(last, 1)
+        def y_leave(rt, g, engine=SCALAR):
+            y_turn(rt, g)
+            y_out(rt, g, engine)
+            store_y_group(rt, g, nc.sync)
+
+        mm1_second_half(0)
+        h_add(0, 1)
         for g in range(2):
-            y_quant(rt - 1, g)
-        store_codes(0, last - 1)
-        mm2(rt, 0, ALL)
-        a_relu(rt, 0, ALL, SCALAR)
-        y_turn(rt - 1, 1)
-        y_out(rt - 1, 1, SCALAR)
-        store_y_group(rt - 1, 1, nc.sync)
-        h_turn(last, 1)
-        h_relu(last, 1, VECTOR)
-        y_affine(rt, 0, ALL)
-        h_quant(last, 1)
-        mm2(rt, 1, ALL)
-        a_relu(rt, 1, ALL, SCALAR)
-        y_round(rt, 0)
-        y_turn(rt, 0)
-        y_out(rt, 0, SCALAR)
-        store_y_group(rt, 0, nc.sync)
-        y_quant(rt, 0)
-        y_affine(rt, 1, ALL)
-        for g, pair in pairs[:2]:
-            mm2(last, g, pair)
-            a_relu(last, g, pair, SCALAR)
-        y_round(rt, 1)
-        y_turn(rt, 1)
-        y_affine(last, *pairs[0])
-        y_quant(rt, 1)
-        store_codes(rt, 1)
-        y_affine(last, *pairs[1])
-        for g, pair in pairs[2:]:
-            mm2(last, g, pair)
-        y_out(rt, 1, SCALAR)
-        store_y_group(rt, 1, nc.sync)
-        a_relu(last, *pairs[2], VECTOR)
-        a_relu(last, *pairs[3], SCALAR)
-        y_affine(last, *pairs[2])
-        y_affine(last, *pairs[3])
+            for h in range(2):
+                w2_sort_scales(h, g)
+        mm1_second_half(1)
+        h_add(1, 1)
         for g in range(2):
-            y_round(last, g)
+            for h in range(2):
+                w2_sort_words(h, g)
+        mm1_second_half(2, front)
+        ready = [(0, 0), (0, 1), (1, 0), (2, 0), (3, 0), (1, 1)]
+        for key, engine in zip(ready, [SCALAR, SCALAR, VECTOR] * 2):
+            h_turn(*key)
+            h_relu(*key, engine)
+        for key in ready[:3]:
+            h_quant(*key)
+        mm1_second_half(2, back)
+        h_add(2, 1)
+        for key in ready[3:]:
+            h_quant(*key)
+        stage2(0)
+        mm1_second_half(3, front)
+        h_turn(2, 1)
+        h_relu(2, 1, VECTOR)
         for g in range(2):
-            y_quant(last, g)
+            y_leave(0, g)
+        y_round(0, 0)
+        h_quant(2, 1)
+        y_round(0, 1)
         for g in range(2):
-            y_turn(last, g)
-            y_out(last, g, SCALAR)
-        store_y_group(last, 0, nc.sync)
-        store_codes(last, 1)
+            y_quant(0, g)
+        store_codes(0, 1)
+        stage2(1)
+        mm1_second_half(3, back)
+        y_round(1, 0)
+        h_add(3, 1)
+        y_round(1, 1)
+        for g in range(2):
+            mm2(2, g, ALL)
+            a_relu(2, g, ALL, SCALAR)
+        h_turn(3, 1)
+        y_affine(2, 0, ALL)
+        h_relu(3, 1, VECTOR)
+        y_quant(1, 0)
+        h_quant(3, 1)
+        y_quant(1, 1)
+        y_leave(1, 0)
+        store_codes(1, 1)
+        y_affine(2, 1, ALL)
+        y_leave(1, 1, VECTOR)
+        y_leave(2, 0)
+        for g in range(2):
+            y_round(2, g)
+        for g, pair in pairs:
+            mm2(3, g, pair)
+            a_relu(3, g, pair, SCALAR)
+        for g in range(2):
+            y_affine(3, g, (0, 1))
+            y_quant(2, g)
+            y_affine(3, g, (2, 3))
+        store_codes(2, 1)
+        y_leave(2, 1)
+        y_leave(3, 0)
+        planes(3)
+        y_turn(3, 1)
+        y_out(3, 1, SCALAR)
+        store_codes(3, 1)
+        store_y_group(3, 1, nc.scalar)
         store_scales()
-        store_y_group(last, 1, nc.scalar)

@@ -240,15 +240,15 @@ def tile_box_head_region_features_h1_kernel(
 
         def w2_sort_words(h, g):
             nc.vector.tensor_copy(
-                out=w2[:, h, 2 * GROUP * g : 2 * GROUP * (g + 1)].bitcast(U16).rearrange("p (t m) -> p t m", t=4),
-                in_=w2_raw[g][:, h, :].bitcast(U16).rearrange("p (m t) -> p t m", t=4),
+                out=w2[:, h, 2 * GROUP * g : 2 * GROUP * (g + 1)].bitcast(U16).rearrange("p (t c i) -> p c t i", t=4, i=8),
+                in_=w2_raw[g][:, h, :].bitcast(U16).rearrange("p (c i t) -> p c t i", t=4, i=8),
             )
 
         def w2_sort_scales(h, g):
             cols = slice(GROUP * g, GROUP * (g + 1))
             nc.vector.tensor_copy(
-                out=s2[:, h, cols].rearrange("p (t m) -> p t m", t=4),
-                in_=s2_raw[:, h, cols].rearrange("p (m t) -> p t m", t=4),
+                out=s2[:, h, cols].rearrange("p (t c i) -> p c t i", t=4, i=16),
+                in_=s2_raw[:, h, cols].rearrange("p (c i t) -> p c t i", t=4, i=16),
             )
 
         def w2_sort(g):
@@ -363,12 +363,13 @@ def tile_box_head_region_features_h1_kernel(
                 load_w1(0, c)
                 if c < 3:
                     load_s1(c)
-        load_s1(3)
-        for c in range(4):
-            load_w1(1, c)
         load_scale_rows(s2_raw, s2_hbm)
-        load_w2(0)
-        load_w2(1)
+        load_s1(3)
+        load_w1(1, 0)
+        for g in range(2):
+            load_w2(g)
+            load_w1(1, g + 1)
+        load_w1(1, 3)
         load_vec(nc.sync, "b2", b2)
         load_vec(nc.sync, "shift", shift)
         load_vec(nc.sync, "gain", gain)
@@ -386,6 +387,9 @@ def tile_box_head_region_features_h1_kernel(
                     x_quant(i)
             for i in done:
                 mm1(i, 0)
+        for g in range(2):
+            for h in range(2):
+                w2_sort_scales(h, g)
         for rt in range(TILES):
             h_add(rt, 0)
 
@@ -410,26 +414,27 @@ def tile_box_head_region_features_h1_kernel(
             y_out(rt, g, engine)
             store_y_group(rt, g, nc.sync)
 
-        mm1_second_half(0)
-        h_add(0, 1)
-        for g in range(2):
-            for h in range(2):
-                w2_sort_scales(h, g)
-        mm1_second_half(1)
-        h_add(1, 1)
-        for g in range(2):
-            for h in range(2):
-                w2_sort_words(h, g)
+        for h in range(2):
+            w2_sort_words(h, 0)
+        for c in range(4):
+            for rt in range(2):
+                mm1_second_half(rt, [c])
+        for rt in range(2):
+            h_add(rt, 1)
         mm1_second_half(2, front)
-        ready = [(0, 0), (0, 1), (1, 0), (2, 0), (3, 0), (1, 1)]
-        for key, engine in zip(ready, [SCALAR, SCALAR, VECTOR] * 2):
+        for key in [(0, 0), (0, 1), (1, 0), (1, 1), (2, 0), (3, 0)]:
             h_turn(*key)
-            h_relu(*key, engine)
-        for key in ready[:3]:
-            h_quant(*key)
+        for key in [(0, 0), (0, 1), (2, 0), (3, 0)]:
+            h_relu(*key, SCALAR)
+        for h in range(2):
+            w2_sort_words(h, 1)
+        for h in range(2):
+            h_quant(0, h)
         mm1_second_half(2, back)
+        for h in range(2):
+            h_relu(1, h, VECTOR)
         h_add(2, 1)
-        for key in ready[3:]:
+        for key in [(1, 0), (1, 1), (2, 0), (3, 0)]:
             h_quant(*key)
         stage2(0)
         mm1_second_half(3, front)

@@ -25,8 +25,8 @@ BLOCKS = TILES * D // CHUNK
 SCALAR, VECTOR = "scalar", "vector"
 
 W1_SCALE_PARTS = [(0, 0, 2), (0, 2, 4), (0, 4, 8), (1, 0, 8)]
-RUN_ENDS = (6, 11, 16)
-LAG = 3
+RUN_ENDS = (4, 8, 12, 16)
+LAG = 2
 UNSORTED = 0
 X_LEAD = 2
 EARLY_CHUNKS = 2
@@ -74,8 +74,8 @@ def tile_box_head_region_features_h1_kernel(
         h_turned = {key: tile("h_turned%d_%d" % key, [P, GROUP], BF16) for key in halves}
         h_codes = {key: tile("h_codes%d_%d" % key, [P, P], U32) for key in halves}
         h_scales = {key: tile("h_scales%d_%d" % key, [P, P], U8) for key in halves}
-        a_t = {key: tile("a_t%d_%d" % key, [P, 4, P], F32) for key in halves}
-        y_t = {key: tile("y_t%d_%d" % key, [P, 4, P], F32) for key in halves}
+        a_t = [tile("a_t%d" % g, [P, 4, R], F32) for g in range(2)]
+        y_t = [tile("y_t%d" % g, [P, 4, R], F32) for g in range(2)]
         y_bf16 = [tile("y_bf16_%d" % g, [P, R, 4], BF16) for g in range(2)]
         y_codes = tile("y_codes", [P, 2, R], U32)
         y_scales = tile("y_scales", [P, 2, R], U8)
@@ -275,7 +275,7 @@ def tile_box_head_region_features_h1_kernel(
         def a_relu(rt, g, slices, engine):
             bank = bank_of(("z", rt, g, slices))
             for j, t in enumerate(slices):
-                src, dst, bias = bank[:, P * j : P * (j + 1)], a_t[rt, g][:, t, :], vec["b2"][:, g, t : t + 1]
+                src, dst, bias = bank[:, P * j : P * (j + 1)], a_t[g][:, t, regions(rt)], vec["b2"][:, g, t : t + 1]
                 if engine == SCALAR:
                     nc.scalar.activation(out=dst, in_=src, func=ACT.Relu, bias=bias)
                 else:
@@ -285,8 +285,8 @@ def tile_box_head_region_features_h1_kernel(
         def y_affine(rt, g, slices):
             for t in slices:
                 nc.vector.tensor_scalar(
-                    out=y_t[rt, g][:, t, :],
-                    in0=a_t[rt, g][:, t, :],
+                    out=y_t[g][:, t, regions(rt)],
+                    in0=a_t[g][:, t, regions(rt)],
                     scalar1=vec["shift"][:, g, t : t + 1],
                     scalar2=vec["gain"][:, g, t : t + 1],
                     op0=ALU.add,
@@ -294,7 +294,10 @@ def tile_box_head_region_features_h1_kernel(
                 )
 
         def y_round(rt, g):
-            nc.vector.tensor_copy(out=y_bf16[g][:, regions(rt), :], in_=y_t[rt, g][:].rearrange("p t r -> p r t"))
+            nc.vector.tensor_copy(
+                out=y_bf16[g][:, regions(rt), :].rearrange("p (c i) t -> p c t i", i=4),
+                in_=y_t[g][:, :, regions(rt)].rearrange("p t (c i) -> p c t i", i=4),
+            )
 
         def y_quant(rt, g):
             nc.vector.quantize_mx(
@@ -306,7 +309,7 @@ def tile_box_head_region_features_h1_kernel(
         def y_turn(rt, g):
             bank = take(("y", rt, g))
             for t in range(4):
-                nc.tensor.transpose(bank[:, P * t : P * (t + 1)], y_t[rt, g][:, t, :], ident[:])
+                nc.tensor.transpose(bank[:, P * t : P * (t + 1)], y_t[g][:, t, regions(rt)], ident[:])
 
         def y_out(rt, g, engine):
             copy_on(engine)(
@@ -314,19 +317,6 @@ def tile_box_head_region_features_h1_kernel(
                 in_=bank_of(("y", rt, g))[:].rearrange("r (t p) -> r p t", t=4),
             )
             give_back(("y", rt, g))
-
-        def y_turn_blocks(rt, g):
-            nc.vector.transpose(out=a_t[rt, g][:].rearrange("p t r -> p (t r)"), in_=y_t[rt, g][:].rearrange("p t r -> p (t r)"))
-
-        def y_out_blocks(rt, g):
-            nc.scalar.copy(
-                out=y_rows[rt][:, GROUP * g : GROUP * (g + 1)].rearrange("p (b j t) -> p b j t", b=4, t=4),
-                in_=a_t[rt, g][:].rearrange("p t (b j) -> p b j t", b=4),
-            )
-            for q in (0, 2, 1, 3):
-                dst = out_0[regions(rt), GROUP * g + P * q : GROUP * g + P * (q + 1)].rearrange("(b i) c -> i b c", b=4)
-                src = y_rows[rt][32 * q : 32 * (q + 1), GROUP * g : GROUP * (g + 1)].rearrange("i (b c) -> i b c", b=4)
-                nc.sync.dma_start(out=dst, in_=src)
 
         def store_y(rt):
             nc.sync.dma_start(out=out_0[regions(rt), :], in_=y_rows[rt][:])
@@ -365,16 +355,14 @@ def tile_box_head_region_features_h1_kernel(
                     load_s1(c)
         load_scale_rows(s2_raw, s2_hbm)
         load_s1(3)
-        load_w1(1, 0)
+        for c in range(4):
+            load_w1(1, c)
         for g in range(2):
             load_w2(g)
-            load_w1(1, g + 1)
-        load_w1(1, 3)
         load_vec(nc.sync, "b2", b2)
         load_vec(nc.sync, "shift", shift)
         load_vec(nc.sync, "gain", gain)
 
-        spread_b1()
         for turn, done in zip(turns, passes):
             x_sort(turn)
             for i in done:
@@ -382,6 +370,8 @@ def tile_box_head_region_features_h1_kernel(
                     x_quant(i)
             for i in turn:
                 x_turn(i)
+                if i == 1:
+                    spread_b1()
             for i in done:
                 if i >= turn.start:
                     x_quant(i)
@@ -396,92 +386,85 @@ def tile_box_head_region_features_h1_kernel(
         ALL = (0, 1, 2, 3)
         pairs = [(g, pair) for g in range(2) for pair in ((0, 1), (2, 3))]
         front, back = range(0, 2), range(2, 4)
-
-        def planes(rt):
-            for g in range(2):
-                y_round(rt, g)
-            for g in range(2):
-                y_quant(rt, g)
-
-        def stage2(rt):
-            for g in range(2):
-                mm2(rt, g, ALL)
-                a_relu(rt, g, ALL, SCALAR)
-                y_affine(rt, g, ALL)
+        last = TILES - 1
 
         def y_leave(rt, g, engine=SCALAR):
             y_turn(rt, g)
             y_out(rt, g, engine)
             store_y_group(rt, g, nc.sync)
 
-        for h in range(2):
-            w2_sort_words(h, 0)
-        for c in range(4):
-            for rt in range(2):
-                mm1_second_half(rt, [c])
-        for rt in range(2):
-            h_add(rt, 1)
-        mm1_second_half(2, front)
-        for key in [(0, 0), (0, 1), (1, 0), (1, 1), (2, 0), (3, 0)]:
-            h_turn(*key)
-        for key in [(0, 0), (0, 1), (2, 0), (3, 0)]:
+        mm1_second_half(0)
+        h_add(0, 1)
+        mm1_second_half(1, range(0, 1))
+        for rt in range(TILES):
+            h_turn(rt, 0)
+        h_turn(0, 1)
+        for key in [(0, 0), (0, 1), (1, 0), (2, 0), (3, 0)]:
             h_relu(*key, SCALAR)
         for h in range(2):
-            w2_sort_words(h, 1)
+            w2_sort_words(h, 0)
         for h in range(2):
             h_quant(0, h)
-        mm1_second_half(2, back)
         for h in range(2):
-            h_relu(1, h, VECTOR)
-        h_add(2, 1)
-        for key in [(1, 0), (1, 1), (2, 0), (3, 0)]:
-            h_quant(*key)
-        stage2(0)
-        mm1_second_half(3, front)
-        h_turn(2, 1)
-        h_relu(2, 1, VECTOR)
-        for g in range(2):
-            y_leave(0, g)
-        y_round(0, 0)
-        h_quant(2, 1)
-        y_round(0, 1)
-        for g in range(2):
-            y_quant(0, g)
-        store_codes(0, 1)
-        stage2(1)
-        mm1_second_half(3, back)
-        y_round(1, 0)
-        h_add(3, 1)
-        y_round(1, 1)
-        for g in range(2):
-            mm2(2, g, ALL)
-            a_relu(2, g, ALL, SCALAR)
-        h_turn(3, 1)
-        y_affine(2, 0, ALL)
-        h_relu(3, 1, VECTOR)
-        y_quant(1, 0)
-        h_quant(3, 1)
-        y_quant(1, 1)
-        y_leave(1, 0)
-        store_codes(1, 1)
-        y_affine(2, 1, ALL)
-        y_leave(1, 1, VECTOR)
-        y_leave(2, 0)
-        for g in range(2):
-            y_round(2, g)
+            w2_sort_words(h, 1)
+        mm1_second_half(1, range(1, 4))
+        for rt in range(last - 1):
+            h_add(rt + 1, 1)
+            if rt == 0:
+                for other in range(1, TILES):
+                    h_quant(other, 0)
+            for g, pair in pairs:
+                mm2(rt, g, pair)
+                a_relu(rt, g, pair, SCALAR)
+                y_affine(rt, g, pair)
+            mm1_second_half(rt + 2, front)
+            h_turn(rt + 1, 1)
+            h_relu(rt + 1, 1, SCALAR)
+            for g in range(2):
+                y_leave(rt, g)
+            for g in range(2):
+                y_round(rt, g)
+            y_quant(rt, 0)
+            h_quant(rt + 1, 1)
+            y_quant(rt, 1)
+            mm1_second_half(rt + 2, back)
+        store_codes(0, last - 1)
+
+        rt = last - 1
+        h_add(last, 1)
+        for g, pair in pairs[:2]:
+            mm2(rt, g, pair)
+            a_relu(rt, g, pair, SCALAR)
+        h_turn(last, 1)
+        y_affine(rt, 0, (0, 1))
+        h_relu(last, 1, VECTOR)
+        y_affine(rt, 0, (2, 3))
+        h_quant(last, 1)
+        for g, pair in pairs[2:]:
+            mm2(rt, g, pair)
+            a_relu(rt, g, pair, SCALAR)
+        y_round(rt, 0)
+        y_leave(rt, 0)
+        y_affine(rt, 1, ALL)
+        y_quant(rt, 0)
         for g, pair in pairs:
-            mm2(3, g, pair)
-            a_relu(3, g, pair, SCALAR)
+            mm2(last, g, pair)
+            a_relu(last, g, pair, SCALAR)
+        y_round(rt, 1)
+        y_affine(last, *pairs[0])
+        y_affine(last, *pairs[1])
+        y_quant(rt, 1)
+        store_codes(rt, 1)
+        y_affine(last, *pairs[2])
+        y_affine(last, *pairs[3])
+        y_leave(rt, 1)
+        y_leave(last, 0)
         for g in range(2):
-            y_affine(3, g, (0, 1))
-            y_quant(2, g)
-            y_affine(3, g, (2, 3))
-        store_codes(2, 1)
-        y_leave(2, 1)
-        y_leave(3, 0)
-        planes(3)
-        y_turn(3, 1)
-        y_out(3, 1, SCALAR)
-        store_codes(3, 1)
-        store_y_group(3, 1, nc.scalar)
+            y_round(last, g)
+        for g in range(2):
+            y_quant(last, g)
+        y_turn(last, 1)
+        y_out(last, 1, SCALAR)
+        store_codes(last, 1)
+        store_y_group(last, 1, nc.sync)
         store_scales()

@@ -10,7 +10,6 @@ F32 = mybir.dt.float32
 BF16 = mybir.dt.bfloat16
 U32 = mybir.dt.uint32
 I32 = mybir.dt.int32
-U16 = mybir.dt.uint16
 U8 = mybir.dt.uint8
 FP8X4 = mybir.dt.float8_e4m3fn_x4
 FP4X4 = mybir.dt.float4_e2m1fn_x4
@@ -25,11 +24,8 @@ BLOCKS = TILES * D // CHUNK
 SCALAR, VECTOR = "scalar", "vector"
 
 W1_SCALE_PARTS = [(0, 0, 2), (0, 2, 4), (0, 4, 8), (1, 0, 8)]
-RUN_ENDS = (4, 8, 12, 16)
-LAG = 2
-UNSORTED = 0
-X_LEAD = 2
-EARLY_CHUNKS = 2
+RUN_ENDS = (6, 11, BLOCKS)
+LAG = 3
 
 
 def tile_box_head_region_features_h1_kernel(
@@ -54,7 +50,6 @@ def tile_box_head_region_features_h1_kernel(
 
         banks = [ps.tile([P, GROUP], F32, name="bank%d" % i) for i in range(8)]
         ident = tile("ident", [P, P], F32)
-        table_warm = tile("table_warm", [P, 16], F32)
         vec = {key: tile("vec_" + key, [P, 2, 4], BF16) for key in ("b1", "b2", "shift", "gain")}
         b1_rows = tile("b1_rows", [P, F], BF16)
         x_raw = [tile("x_raw%d" % i, [P, CHUNK], BF16) for i in range(BLOCKS)]
@@ -98,9 +93,6 @@ def tile_box_head_region_features_h1_kernel(
         def regions(rt, count=1):
             return slice(P * rt, P * (rt + count))
 
-        def copy_on(engine):
-            return nc.scalar.copy if engine == SCALAR else nc.vector.tensor_copy
-
         def load_vec(queue, key, src):
             queue.dma_start(out=vec[key][:], in_=src.rearrange("(g p t) -> p g t", g=2, t=4))
 
@@ -138,50 +130,24 @@ def tile_box_head_region_features_h1_kernel(
 
         def x_sort(blocks):
             for i in blocks:
-                if i < UNSORTED:
-                    continue
                 nc.vector.tensor_copy(
                     out=x_sorted[i][:].rearrange("r (g u m) -> r g u m", g=2, u=2),
                     in_=x_raw[i][:].bitcast(F32).rearrange("r (g m u) -> r g u m", g=2, u=2),
                 )
 
-        def x_words(i, g, u):
-            if i < UNSORTED:
-                return x_raw[i][:].bitcast(F32)[:, 2 * P * g + u : 2 * P * (g + 1) : 2]
-            return x_sorted[i][:, P * (2 * g + u) : P * (2 * g + u + 1)]
-
-        def x_turned(i):
-            return x_sorted[i][:] if i < UNSORTED else x_raw[i][:].bitcast(F32)
-
         def x_turn(i):
             bank = take(("x", i))
-            for g in range(2):
-                for u in range(2):
-                    j = 2 * g + u
-                    nc.tensor.transpose(bank[:, P * j : P * (j + 1)], x_words(i, g, u), ident[:])
+            for j in range(4):
+                nc.tensor.transpose(bank[:, P * j : P * (j + 1)], x_sorted[i][:, P * j : P * (j + 1)], ident[:])
             nc.scalar.copy(
-                out=x_turned(i).rearrange("p (g r u) -> p g r u", g=2, u=2),
+                out=x_raw[i][:].bitcast(F32).rearrange("p (g r u) -> p g r u", g=2, u=2),
                 in_=bank[:].rearrange("p (g u r) -> p g r u", g=2, u=2),
             )
             give_back(("x", i))
 
-        def x_quant(i):
-            nc.vector.quantize_mx(out=x_codes[i][:].bitcast(FP8X4), scales=x_scales[i][:], in_=x_turned(i).bitcast(BF16))
-
-        def x_turn_first():
-            for g in range(2):
-                bank = take(("x0", g))
-                for u in range(2):
-                    nc.tensor.transpose(bank[:, P * u : P * (u + 1)], x_words(0, g, u), ident[:])
-            for g in range(2):
-                turned = x_sorted[0][:, 2 * P * g : 2 * P * (g + 1)]
-                nc.scalar.copy(
-                    out=turned.rearrange("p (r u) -> p r u", u=2),
-                    in_=bank_of(("x0", g))[:, 0 : 2 * P].rearrange("p (u r) -> p r u", u=2),
-                )
-                give_back(("x0", g))
-                cols = slice(P * g, P * (g + 1))
-                nc.vector.quantize_mx(out=x_codes[0][:, cols].bitcast(FP8X4), scales=x_scales[0][:, cols], in_=turned.bitcast(BF16))
+        def x_quant(blocks):
+            for i in blocks:
+                nc.vector.quantize_mx(out=x_codes[i][:].bitcast(FP8X4), scales=x_scales[i][:], in_=x_raw[i][:])
 
         def mm1(i, h):
             c, rt = divmod(i, TILES)
@@ -202,29 +168,22 @@ def tile_box_head_region_features_h1_kernel(
             for c in chunks:
                 mm1(TILES * c + rt, 1)
 
-        def h_add_part(rt, h, u):
-            cols = slice(256 * u, 256 * (u + 1))
-            nc.vector.tensor_tensor(
-                out=h_biased[rt, h][:, cols].rearrange("r (m e) -> r m e", e=2),
-                in0=bank_of(("h", rt, h))[:].rearrange("r (m u e) -> r u m e", u=2, e=2)[:, u],
-                in1=b1_rows[:, GROUP * h : GROUP * (h + 1)][:, cols].rearrange("r (m e) -> r m e", e=2),
-                op=ALU.add,
-            )
-            if u == 1:
-                give_back(("h", rt, h))
-
         def h_add(rt, h):
-            h_add_part(rt, h, 0)
-            h_add_part(rt, h, 1)
-
-        def h_turn_part(rt, h, u):
-            bank = take(("ht", rt, h)) if u == 0 else bank_of(("ht", rt, h))
-            words = h_biased[rt, h][:].bitcast(F32)
-            nc.tensor.transpose(bank[:, P * u : P * (u + 1)], words[:, P * u : P * (u + 1)], ident[:])
+            for u in range(2):
+                cols = slice(256 * u, 256 * (u + 1))
+                nc.vector.tensor_tensor(
+                    out=h_biased[rt, h][:, cols].rearrange("r (m e) -> r m e", e=2),
+                    in0=bank_of(("h", rt, h))[:].rearrange("r (m u e) -> r u m e", u=2, e=2)[:, u],
+                    in1=b1_rows[:, GROUP * h : GROUP * (h + 1)][:, cols].rearrange("r (m e) -> r m e", e=2),
+                    op=ALU.add,
+                )
+            give_back(("h", rt, h))
 
         def h_turn(rt, h):
-            h_turn_part(rt, h, 0)
-            h_turn_part(rt, h, 1)
+            bank = take(("ht", rt, h))
+            words = h_biased[rt, h][:].bitcast(F32)
+            for u in range(2):
+                nc.tensor.transpose(bank[:, P * u : P * (u + 1)], words[:, P * u : P * (u + 1)], ident[:])
 
         def h_relu(rt, h, engine):
             src = bank_of(("ht", rt, h))[:, 0 : 2 * P].bitcast(BF16).rearrange("p (u r e) -> p r u e", u=2, e=2)
@@ -240,24 +199,18 @@ def tile_box_head_region_features_h1_kernel(
 
         def w2_sort_words(h, g):
             nc.vector.tensor_copy(
-                out=w2[:, h, 2 * GROUP * g : 2 * GROUP * (g + 1)].bitcast(U16).rearrange("p (t c i) -> p c t i", t=4, i=8),
-                in_=w2_raw[g][:, h, :].bitcast(U16).rearrange("p (c i t) -> p c t i", t=4, i=8),
+                out=w2[:, h, 2 * GROUP * g : 2 * GROUP * (g + 1)].rearrange("p (t m b) -> p t m b", t=4, b=2),
+                in_=w2_raw[g][:, h, :].rearrange("p (m t b) -> p t m b", t=4, b=2),
             )
 
         def w2_sort_scales(h, g):
             cols = slice(GROUP * g, GROUP * (g + 1))
             nc.vector.tensor_copy(
-                out=s2[:, h, cols].rearrange("p (t c i) -> p c t i", t=4, i=16),
-                in_=s2_raw[:, h, cols].rearrange("p (c i t) -> p c t i", t=4, i=16),
+                out=s2[:, h, cols].rearrange("p (t m) -> p t m", t=4),
+                in_=s2_raw[:, h, cols].rearrange("p (m t) -> p t m", t=4),
             )
 
-        def w2_sort(g):
-            for h in range(2):
-                w2_sort_scales(h, g)
-            for h in range(2):
-                w2_sort_words(h, g)
-
-        def mm2(rt, g, slices):
+        def stage2(rt, g, slices):
             bank = take(("z", rt, g, slices))
             for j, t in enumerate(slices):
                 col = GROUP * g + P * t
@@ -271,15 +224,13 @@ def tile_box_head_region_features_h1_kernel(
                         start=(h == 0),
                         stop=(h == 1),
                     )
-
-        def a_relu(rt, g, slices, engine):
-            bank = bank_of(("z", rt, g, slices))
             for j, t in enumerate(slices):
-                src, dst, bias = bank[:, P * j : P * (j + 1)], a_t[g][:, t, regions(rt)], vec["b2"][:, g, t : t + 1]
-                if engine == SCALAR:
-                    nc.scalar.activation(out=dst, in_=src, func=ACT.Relu, bias=bias)
-                else:
-                    nc.vector.tensor_scalar(out=dst, in0=src, scalar1=bias, scalar2=0.0, op0=ALU.add, op1=ALU.max)
+                nc.scalar.activation(
+                    out=a_t[g][:, t, regions(rt)],
+                    in_=bank[:, P * j : P * (j + 1)],
+                    func=ACT.Relu,
+                    bias=vec["b2"][:, g, t : t + 1],
+                )
             give_back(("z", rt, g, slices))
 
         def y_affine(rt, g, slices):
@@ -295,8 +246,8 @@ def tile_box_head_region_features_h1_kernel(
 
         def y_round(rt, g):
             nc.vector.tensor_copy(
-                out=y_bf16[g][:, regions(rt), :].rearrange("p (c i) t -> p c t i", i=4),
-                in_=y_t[g][:, :, regions(rt)].rearrange("p t (c i) -> p c t i", i=4),
+                out=y_bf16[g][:, regions(rt), :],
+                in_=y_t[g][:, :, regions(rt)].rearrange("p t r -> p r t"),
             )
 
         def y_quant(rt, g):
@@ -310,20 +261,19 @@ def tile_box_head_region_features_h1_kernel(
             bank = take(("y", rt, g))
             for t in range(4):
                 nc.tensor.transpose(bank[:, P * t : P * (t + 1)], y_t[g][:, t, regions(rt)], ident[:])
-
-        def y_out(rt, g, engine):
-            copy_on(engine)(
+            nc.scalar.copy(
                 out=y_rows[rt][:, GROUP * g : GROUP * (g + 1)].rearrange("r (p t) -> r p t", t=4),
-                in_=bank_of(("y", rt, g))[:].rearrange("r (t p) -> r p t", t=4),
+                in_=bank[:].rearrange("r (t p) -> r p t", t=4),
             )
             give_back(("y", rt, g))
 
-        def store_y(rt):
-            nc.sync.dma_start(out=out_0[regions(rt), :], in_=y_rows[rt][:])
-
-        def store_y_group(rt, g, queue):
+        def store_y(rt, g):
             cols = slice(GROUP * g, GROUP * (g + 1))
-            queue.dma_start(out=out_0[regions(rt), cols], in_=y_rows[rt][:, cols])
+            nc.sync.dma_start(out=out_0[regions(rt), cols], in_=y_rows[rt][:, cols])
+
+        def y_leave(rt, g):
+            y_turn(rt, g)
+            store_y(rt, g)
 
         def store_codes(rt, count):
             nc.sync.dma_start(out=codes_hbm[:, :, regions(rt, count)], in_=y_codes[:, :, regions(rt, count)].bitcast(I32))
@@ -335,13 +285,8 @@ def tile_box_head_region_features_h1_kernel(
 
         load_vec(nc.scalar, "b1", b1)
         make_identity(nc, ident[:])
-        clear(s1_parts[0])
-        nc.vector.memset(table_warm[:, 0:8], 0.0)
-        nc.scalar.activation(out=table_warm[:, 8:16], in_=table_warm[:, 0:8], func=ACT.Relu)
-        clear(s1_parts[1])
-        clear(s1_parts[2])
-        clear(s1_parts[3])
-        clear(s2_raw)
+        for plane in s1_parts:
+            clear(plane)
 
         turns = [range(a, b) for a, b in zip((0,) + RUN_ENDS, RUN_ENDS)]
         pass_ends = tuple(end - LAG for end in RUN_ENDS[:-1]) + (BLOCKS,)
@@ -351,48 +296,43 @@ def tile_box_head_region_features_h1_kernel(
             load_x(turn)
             for c in [i // TILES for i in done if i % TILES == 0]:
                 load_w1(0, c)
-                if c < 3:
+                if c < len(W1_SCALE_PARTS) - 1:
                     load_s1(c)
-        load_scale_rows(s2_raw, s2_hbm)
-        load_s1(3)
-        for c in range(4):
-            load_w1(1, c)
-        for g in range(2):
-            load_w2(g)
-        load_vec(nc.sync, "b2", b2)
-        load_vec(nc.sync, "shift", shift)
-        load_vec(nc.sync, "gain", gain)
+
+        def load_later_weights():
+            clear(s2_raw)
+            load_scale_rows(s2_raw, s2_hbm)
+            load_s1(len(W1_SCALE_PARTS) - 1)
+            for g in range(2):
+                load_w1(1, 2 * g)
+                load_w1(1, 2 * g + 1)
+                load_w2(g)
+            load_vec(nc.sync, "b2", b2)
+            load_vec(nc.sync, "shift", shift)
+            load_vec(nc.sync, "gain", gain)
 
         for turn, done in zip(turns, passes):
             x_sort(turn)
-            for i in done:
-                if i < turn.start:
-                    x_quant(i)
+            x_quant([i for i in done if i < turn.start])
             for i in turn:
                 x_turn(i)
                 if i == 1:
                     spread_b1()
-            for i in done:
-                if i >= turn.start:
-                    x_quant(i)
+            x_quant([i for i in done if i >= turn.start])
             for i in done:
                 mm1(i, 0)
+            if turn.start == 0:
+                load_later_weights()
         for g in range(2):
             for h in range(2):
                 w2_sort_scales(h, g)
         for rt in range(TILES):
             h_add(rt, 0)
+        for h in range(2):
+            w2_sort_words(h, 0)
 
-        ALL = (0, 1, 2, 3)
-        pairs = [(g, pair) for g in range(2) for pair in ((0, 1), (2, 3))]
-        front, back = range(0, 2), range(2, 4)
-        last = TILES - 1
-
-        def y_leave(rt, g, engine=SCALAR):
-            y_turn(rt, g)
-            y_out(rt, g, engine)
-            store_y_group(rt, g, nc.sync)
-
+        low, high = (0, 1), (2, 3)
+        pairs = [(g, slices) for g in range(2) for slices in (low, high)]
         mm1_second_half(0)
         h_add(0, 1)
         mm1_second_half(1, range(0, 1))
@@ -402,69 +342,61 @@ def tile_box_head_region_features_h1_kernel(
         for key in [(0, 0), (0, 1), (1, 0), (2, 0), (3, 0)]:
             h_relu(*key, SCALAR)
         for h in range(2):
-            w2_sort_words(h, 0)
-        for h in range(2):
-            h_quant(0, h)
-        for h in range(2):
             w2_sort_words(h, 1)
+            h_quant(0, h)
         mm1_second_half(1, range(1, 4))
-        for rt in range(last - 1):
+
+        for rt in range(2):
             h_add(rt + 1, 1)
             if rt == 0:
                 for other in range(1, TILES):
                     h_quant(other, 0)
-            for g, pair in pairs:
-                mm2(rt, g, pair)
-                a_relu(rt, g, pair, SCALAR)
-                y_affine(rt, g, pair)
-            mm1_second_half(rt + 2, front)
+            for g, slices in pairs:
+                stage2(rt, g, slices)
+                y_affine(rt, g, slices)
+            mm1_second_half(rt + 2, range(0, 2))
             h_turn(rt + 1, 1)
             h_relu(rt + 1, 1, SCALAR)
-            for g in range(2):
-                y_leave(rt, g)
+            y_leave(rt, 0)
+            if rt == 0:
+                y_leave(rt, 1)
             for g in range(2):
                 y_round(rt, g)
             y_quant(rt, 0)
             h_quant(rt + 1, 1)
             y_quant(rt, 1)
-            mm1_second_half(rt + 2, back)
-        store_codes(0, last - 1)
+            mm1_second_half(rt + 2, range(2, 4))
+        store_codes(0, 2)
 
-        rt = last - 1
-        h_add(last, 1)
-        for g, pair in pairs[:2]:
-            mm2(rt, g, pair)
-            a_relu(rt, g, pair, SCALAR)
-        h_turn(last, 1)
-        y_affine(rt, 0, (0, 1))
-        h_relu(last, 1, VECTOR)
-        y_affine(rt, 0, (2, 3))
-        h_quant(last, 1)
-        for g, pair in pairs[2:]:
-            mm2(rt, g, pair)
-            a_relu(rt, g, pair, SCALAR)
-        y_round(rt, 0)
-        y_leave(rt, 0)
-        y_affine(rt, 1, ALL)
-        y_quant(rt, 0)
-        for g, pair in pairs:
-            mm2(last, g, pair)
-            a_relu(last, g, pair, SCALAR)
-        y_round(rt, 1)
-        y_affine(last, *pairs[0])
-        y_affine(last, *pairs[1])
-        y_quant(rt, 1)
-        store_codes(rt, 1)
-        y_affine(last, *pairs[2])
-        y_affine(last, *pairs[3])
-        y_leave(rt, 1)
-        y_leave(last, 0)
+        h_add(3, 1)
+        for slices in (low, high):
+            stage2(2, 0, slices)
+        y_leave(1, 1)
+        h_turn(3, 1)
+        y_affine(2, 0, low)
+        h_relu(3, 1, VECTOR)
+        y_affine(2, 0, high)
+        h_quant(3, 1)
+        for slices in (low, high):
+            stage2(2, 1, slices)
+        y_round(2, 0)
+        y_leave(2, 0)
+        y_affine(2, 1, low + high)
+        y_quant(2, 0)
+        for g, slices in pairs:
+            stage2(3, g, slices)
+        y_round(2, 1)
+        y_affine(3, 0, low + high)
+        y_quant(2, 1)
+        store_codes(2, 1)
+        y_affine(3, 1, low + high)
+        y_leave(2, 1)
+        y_leave(3, 0)
         for g in range(2):
-            y_round(last, g)
+            y_round(3, g)
         for g in range(2):
-            y_quant(last, g)
-        y_turn(last, 1)
-        y_out(last, 1, SCALAR)
-        store_codes(last, 1)
-        store_y_group(last, 1, nc.sync)
+            y_quant(3, g)
+        y_turn(3, 1)
+        store_codes(3, 1)
+        store_y(3, 1)
         store_scales()

@@ -24,8 +24,8 @@ BLOCKS = TILES * D // CHUNK
 SCALAR, VECTOR = "scalar", "vector"
 
 W1_SCALE_PARTS = [(0, 0, 2), (0, 2, 4), (0, 4, 8), (1, 0, 8)]
-RUN_ENDS = (6, 11, BLOCKS)
-LAG = 3
+RUN_ENDS = (7, 11, BLOCKS)
+LAG = 4
 
 
 def tile_box_head_region_features_h1_kernel(
@@ -203,11 +203,10 @@ def tile_box_head_region_features_h1_kernel(
                 in_=w2_raw[g][:, h, :].rearrange("p (m t b) -> p t m b", t=4, b=2),
             )
 
-        def w2_sort_scales(h, g):
-            cols = slice(GROUP * g, GROUP * (g + 1))
+        def w2_sort_scales(h):
             nc.vector.tensor_copy(
-                out=s2[:, h, cols].rearrange("p (t m) -> p t m", t=4),
-                in_=s2_raw[:, h, cols].rearrange("p (m t) -> p t m", t=4),
+                out=s2[:, h, :].rearrange("p (g t m) -> p g t m", g=2, t=4),
+                in_=s2_raw[:, h, :].rearrange("p (g m t) -> p g t m", g=2, t=4),
             )
 
         def stage2(rt, g, slices):
@@ -257,11 +256,11 @@ def tile_box_head_region_features_h1_kernel(
                 in_=y_bf16[g][:, regions(rt), :].rearrange("p r t -> p (r t)"),
             )
 
-        def y_turn(rt, g):
+        def y_turn(rt, g, copy=nc.scalar.copy):
             bank = take(("y", rt, g))
             for t in range(4):
                 nc.tensor.transpose(bank[:, P * t : P * (t + 1)], y_t[g][:, t, regions(rt)], ident[:])
-            nc.scalar.copy(
+            copy(
                 out=y_rows[rt][:, GROUP * g : GROUP * (g + 1)].rearrange("r (p t) -> r p t", t=4),
                 in_=bank[:].rearrange("r (t p) -> r p t", t=4),
             )
@@ -271,8 +270,8 @@ def tile_box_head_region_features_h1_kernel(
             cols = slice(GROUP * g, GROUP * (g + 1))
             nc.sync.dma_start(out=out_0[regions(rt), cols], in_=y_rows[rt][:, cols])
 
-        def y_leave(rt, g):
-            y_turn(rt, g)
+        def y_leave(rt, g, copy=nc.scalar.copy):
+            y_turn(rt, g, copy)
             store_y(rt, g)
 
         def store_codes(rt, count):
@@ -303,10 +302,11 @@ def tile_box_head_region_features_h1_kernel(
             clear(s2_raw)
             load_scale_rows(s2_raw, s2_hbm)
             load_s1(len(W1_SCALE_PARTS) - 1)
+            load_w1(1, 0)
             for g in range(2):
-                load_w1(1, 2 * g)
-                load_w1(1, 2 * g + 1)
                 load_w2(g)
+                load_w1(1, g + 1)
+            load_w1(1, 3)
             load_vec(nc.sync, "b2", b2)
             load_vec(nc.sync, "shift", shift)
             load_vec(nc.sync, "gain", gain)
@@ -323,9 +323,8 @@ def tile_box_head_region_features_h1_kernel(
                 mm1(i, 0)
             if turn.start == 0:
                 load_later_weights()
-        for g in range(2):
-            for h in range(2):
-                w2_sort_scales(h, g)
+        for h in range(2):
+            w2_sort_scales(h)
         for rt in range(TILES):
             h_add(rt, 0)
         for h in range(2):
@@ -333,63 +332,73 @@ def tile_box_head_region_features_h1_kernel(
 
         low, high = (0, 1), (2, 3)
         pairs = [(g, slices) for g in range(2) for slices in (low, high)]
-        mm1_second_half(0)
-        h_add(0, 1)
-        mm1_second_half(1, range(0, 1))
-        for rt in range(TILES):
-            h_turn(rt, 0)
-        h_turn(0, 1)
-        for key in [(0, 0), (0, 1), (1, 0), (2, 0), (3, 0)]:
+        front, back = range(0, 2), range(2, 4)
+        for c in range(4):
+            for rt in range(2):
+                mm1_second_half(rt, [c])
+        for rt in range(2):
+            h_add(rt, 1)
+        mm1_second_half(2, front)
+        for key in [(0, 0), (0, 1), (1, 0), (1, 1), (2, 0), (3, 0)]:
+            h_turn(*key)
+        for key in [(0, 0), (0, 1), (2, 0), (3, 0)]:
             h_relu(*key, SCALAR)
         for h in range(2):
             w2_sort_words(h, 1)
+        for h in range(2):
             h_quant(0, h)
-        mm1_second_half(1, range(1, 4))
+        mm1_second_half(2, back)
+        for h in range(2):
+            h_relu(1, h, VECTOR)
+        h_add(2, 1)
+        for key in [(1, 0), (1, 1), (2, 0), (3, 0)]:
+            h_quant(*key)
 
-        for rt in range(2):
-            h_add(rt + 1, 1)
-            if rt == 0:
-                for other in range(1, TILES):
-                    h_quant(other, 0)
-            for g, slices in pairs:
-                stage2(rt, g, slices)
-                y_affine(rt, g, slices)
-            mm1_second_half(rt + 2, range(0, 2))
-            h_turn(rt + 1, 1)
-            h_relu(rt + 1, 1, SCALAR)
-            y_leave(rt, 0)
-            if rt == 0:
-                y_leave(rt, 1)
-            for g in range(2):
-                y_round(rt, g)
-            y_quant(rt, 0)
-            h_quant(rt + 1, 1)
-            y_quant(rt, 1)
-            mm1_second_half(rt + 2, range(2, 4))
-        store_codes(0, 2)
+        for g, slices in pairs:
+            stage2(0, g, slices)
+            y_affine(0, g, slices)
+        mm1_second_half(3, front)
+        h_turn(2, 1)
+        h_relu(2, 1, VECTOR)
+        for g in range(2):
+            y_leave(0, g)
+        y_round(0, 0)
+        h_quant(2, 1)
+        y_round(0, 1)
+        for g in range(2):
+            y_quant(0, g)
+        store_codes(0, 1)
 
+        for g, slices in pairs:
+            stage2(1, g, slices)
+            y_affine(1, g, slices)
+        mm1_second_half(3, back)
         h_add(3, 1)
-        for slices in (low, high):
-            stage2(2, 0, slices)
-        y_leave(1, 1)
+        for g in range(2):
+            y_round(1, g)
+        for g, slices in pairs:
+            stage2(2, g, slices)
         h_turn(3, 1)
-        y_affine(2, 0, low)
+        y_affine(2, 0, low + high)
         h_relu(3, 1, VECTOR)
-        y_affine(2, 0, high)
+        y_quant(1, 0)
         h_quant(3, 1)
-        for slices in (low, high):
-            stage2(2, 1, slices)
-        y_round(2, 0)
-        y_leave(2, 0)
+        y_quant(1, 1)
+        y_leave(1, 0)
+        store_codes(1, 1)
         y_affine(2, 1, low + high)
-        y_quant(2, 0)
+        y_leave(1, 1, nc.vector.tensor_copy)
+        y_leave(2, 0)
+
+        for g in range(2):
+            y_round(2, g)
         for g, slices in pairs:
             stage2(3, g, slices)
-        y_round(2, 1)
-        y_affine(3, 0, low + high)
-        y_quant(2, 1)
+        for g in range(2):
+            y_affine(3, g, low)
+            y_quant(2, g)
+            y_affine(3, g, high)
         store_codes(2, 1)
-        y_affine(3, 1, low + high)
         y_leave(2, 1)
         y_leave(3, 0)
         for g in range(2):

@@ -19,13 +19,22 @@ ACT = mybir.ActivationFunctionType
 P = 128
 GROUP = 512
 TILES = R // P
-CHUNK = 2 * GROUP
-BLOCKS = TILES * D // CHUNK
 SCALAR, VECTOR = "scalar", "vector"
 
-W1_SCALE_PARTS = [(0, 0, 2), (0, 2, 4), (0, 4, 8), (1, 0, 8)]
-RUN_ENDS = (7, 11, BLOCKS)
-LAG = 4
+U16 = mybir.dt.uint16
+GROUPS = D // GROUP
+SINGLES = 0
+ENDS = (4, 8, 12, 16)
+PASS_ENDS = (3, 7, 11, 16)
+WARM = 6
+W_AT = (3, 7, 11, 15)
+S_AT = (3, 7, 11, 15)
+PARTS = [(0, 0, 1), (0, 1, 2), (0, 2, 4), (0, 4, 6), (0, 6, 8), (1, 0, 8)]
+B1_AT = 2
+EARLY = 0
+VLEAD = 0
+CUT = 2
+LATE = "s1 a b s2 c d w v"
 
 
 def tile_box_head_region_features_h1_kernel(
@@ -52,15 +61,16 @@ def tile_box_head_region_features_h1_kernel(
         ident = tile("ident", [P, P], F32)
         vec = {key: tile("vec_" + key, [P, 2, 4], BF16) for key in ("b1", "b2", "shift", "gain")}
         b1_rows = tile("b1_rows", [P, F], BF16)
-        x_raw = [tile("x_raw%d" % i, [P, CHUNK], BF16) for i in range(BLOCKS)]
-        x_sorted = [tile("x_sorted%d" % i, [P, CHUNK // 2], F32) for i in range(BLOCKS)]
-        x_codes = [tile("x_codes%d" % i, [P, 2 * P], U32) for i in range(BLOCKS)]
-        x_scales = [tile("x_scales%d" % i, [P, 2 * P], U8) for i in range(BLOCKS)]
-        w1 = {(h, c): tile("w1_%d_%d" % (h, c), [P, 2, 2 * GROUP], U8) for h in range(2) for c in range(4)}
-        s1_parts = [tile("s1_%d" % i, [P, g1 - g0, GROUP], U8) for i, (h, g0, g1) in enumerate(W1_SCALE_PARTS)]
-        s1 = {
-            (h, g): s1_parts[i][:, g - g0, :] for i, (h, g0, g1) in enumerate(W1_SCALE_PARTS) for g in range(g0, g1)
-        }
+        spans = [(g, 1) for g in range(SINGLES)] + [(g, 2) for g in range(SINGLES, GROUPS, 2)]
+        blocks = [(rt, g, n) for g, n in spans for rt in range(TILES)]
+        x_raw = {b: tile("x_raw%d_%d" % b[:2], [P, GROUP * b[2]], BF16) for b in blocks}
+        x_sorted = {b: tile("x_sorted%d_%d" % b[:2], [P, GROUP * b[2] // 2], F32) for b in blocks}
+        x_codes = {b: tile("x_codes%d_%d" % b[:2], [P, P * b[2]], U32) for b in blocks}
+        x_scales = {b: tile("x_scales%d_%d" % b[:2], [P, P * b[2]], U8) for b in blocks}
+        w1 = {(h, g, n): tile("w1_%d_%d" % (h, g), [P, n, 2 * GROUP], U8) for h in range(2) for g, n in spans}
+        scale_parts = PARTS
+        s1_parts = [tile("s1_%d" % i, [P, g1 - g0, GROUP], U8) for i, (h, g0, g1) in enumerate(scale_parts)]
+        s1 = {(h, g): s1_parts[i][:, g - g0, :] for i, (h, g0, g1) in enumerate(scale_parts) for g in range(g0, g1)}
         w2_raw = [tile("w2_raw%d" % g, [P, 2, 2 * GROUP], U8) for g in range(2)]
         s2_raw = tile("s2_raw", [P, 2, N], U8)
         w2 = tile("w2", [P, 2, 2 * N], U8)
@@ -96,26 +106,25 @@ def tile_box_head_region_features_h1_kernel(
         def load_vec(queue, key, src):
             queue.dma_start(out=vec[key][:], in_=src.rearrange("(g p t) -> p g t", g=2, t=4))
 
-        def load_x(blocks):
-            for i in blocks:
-                c, rt = divmod(i, TILES)
-                nc.sync.dma_start(out=x_raw[i][:], in_=x[regions(rt), CHUNK * c : CHUNK * (c + 1)])
+        def load_x(b):
+            rt, g, n = b
+            nc.sync.dma_start(out=x_raw[b][:], in_=x[regions(rt), GROUP * g : GROUP * (g + n)])
 
-        def load_w1(h, c):
-            src = w1_hbm[2 * c : 2 * c + 2, :, 256 * h : 256 * (h + 1)]
-            nc.sync.dma_start(out=w1[h, c][:].bitcast(I32), in_=src.rearrange("g p n -> p g n"))
+        def load_w1(h, g, n):
+            src = w1_hbm[g : g + n, :, 256 * h : 256 * (h + 1)]
+            nc.sync.dma_start(out=w1[h, g, n][:].bitcast(I32), in_=src.rearrange("g p n -> p g n"))
 
         def load_w2(g):
             src = w2_hbm[:, :, 256 * g : 256 * (g + 1)]
             nc.sync.dma_start(out=w2_raw[g][:].bitcast(I32), in_=src.rearrange("h p n -> p h n"))
 
-        def load_scale_rows(plane, src):
+        def load_scale_rows(queue, plane, src):
             for r in range(4):
-                nc.sync.dma_start(out=plane[r:P:32].bitcast(I32), in_=src[:, r:16:4, :].rearrange("g q n -> q g n"))
+                queue.dma_start(out=plane[r:P:32].bitcast(I32), in_=src[:, r:16:4, :].rearrange("g q n -> q g n"))
 
-        def load_s1(part):
-            h, g0, g1 = W1_SCALE_PARTS[part]
-            load_scale_rows(s1_parts[part], s1_hbm[g0:g1, :, 128 * h : 128 * (h + 1)])
+        def load_s1(queue, part):
+            h, g0, g1 = scale_parts[part]
+            load_scale_rows(queue, s1_parts[part], s1_hbm[g0:g1, :, 128 * h : 128 * (h + 1)])
 
         def clear(t):
             nc.vector.memset(t[:].bitcast(I32), 0)
@@ -128,45 +137,46 @@ def tile_box_head_region_features_h1_kernel(
             nc.scalar.copy(out=b1_rows[:].bitcast(F32), in_=bank[:])
             give_back("b1")
 
-        def x_sort(blocks):
-            for i in blocks:
+        def x_sort(run):
+            for b in run:
                 nc.vector.tensor_copy(
-                    out=x_sorted[i][:].rearrange("r (g u m) -> r g u m", g=2, u=2),
-                    in_=x_raw[i][:].bitcast(F32).rearrange("r (g m u) -> r g u m", g=2, u=2),
+                    out=x_sorted[b][:].rearrange("r (g u m) -> r g u m", g=b[2], u=2),
+                    in_=x_raw[b][:].bitcast(F32).rearrange("r (g m u) -> r g u m", g=b[2], u=2),
                 )
 
-        def x_turn(i):
-            bank = take(("x", i))
-            for j in range(4):
-                nc.tensor.transpose(bank[:, P * j : P * (j + 1)], x_sorted[i][:, P * j : P * (j + 1)], ident[:])
-            nc.scalar.copy(
-                out=x_raw[i][:].bitcast(F32).rearrange("p (g r u) -> p g r u", g=2, u=2),
-                in_=bank[:].rearrange("p (g u r) -> p g r u", g=2, u=2),
-            )
-            give_back(("x", i))
-
-        def x_quant(blocks):
-            for i in blocks:
-                nc.vector.quantize_mx(out=x_codes[i][:].bitcast(FP8X4), scales=x_scales[i][:], in_=x_raw[i][:])
-
-        def mm1(i, h):
-            c, rt = divmod(i, TILES)
-            bank = take(("h", rt, h)) if c == 0 else bank_of(("h", rt, h))
-            for j in range(2):
-                g = 2 * c + j
-                nc.tensor.matmul_mx(
-                    out=bank[:],
-                    lhsT=x_codes[i][:, P * j : P * (j + 1)].bitcast(FP8X4),
-                    lhsT_scale=x_scales[i][:, P * j : P * (j + 1)],
-                    rhs=w1[h, c][:, j, :].bitcast(FP4X4),
-                    rhs_scale=s1[h, g],
-                    start=(g == 0),
-                    stop=(g == D // GROUP - 1),
+        def x_turn(run):
+            for b in run:
+                bank = take(("x", b))
+                for j in range(2 * b[2]):
+                    nc.tensor.transpose(bank[:, P * j : P * (j + 1)], x_sorted[b][:, P * j : P * (j + 1)], ident[:])
+                nc.scalar.copy(
+                    out=x_raw[b][:].bitcast(F32).rearrange("p (g r u) -> p g r u", g=b[2], u=2),
+                    in_=bank[:, 0 : 2 * P * b[2]].rearrange("p (g u r) -> p g r u", g=b[2], u=2),
                 )
+                give_back(("x", b))
 
-        def mm1_second_half(rt, chunks=range(4)):
-            for c in chunks:
-                mm1(TILES * c + rt, 1)
+        def x_quant(run):
+            for b in run:
+                nc.vector.quantize_mx(out=x_codes[b][:].bitcast(FP8X4), scales=x_scales[b][:], in_=x_raw[b][:])
+
+        def mm1(run, h):
+            for b in run:
+                rt, g0, n = b
+                bank = take(("h", rt, h)) if g0 == 0 else bank_of(("h", rt, h))
+                for j in range(n):
+                    g = g0 + j
+                    nc.tensor.matmul_mx(
+                        out=bank[:],
+                        lhsT=x_codes[b][:, P * j : P * (j + 1)].bitcast(FP8X4),
+                        lhsT_scale=x_scales[b][:, P * j : P * (j + 1)],
+                        rhs=w1[h, g0, n][:, j, :].bitcast(FP4X4),
+                        rhs_scale=s1[h, g],
+                        start=(g == 0),
+                        stop=(g == GROUPS - 1),
+                    )
+
+        def mm1_second_half(rt, g0, g1):
+            mm1([b for b in blocks if b[0] == rt and g0 <= b[1] < g1], 1)
 
         def h_add(rt, h):
             for u in range(2):
@@ -199,8 +209,8 @@ def tile_box_head_region_features_h1_kernel(
 
         def w2_sort_words(h, g):
             nc.vector.tensor_copy(
-                out=w2[:, h, 2 * GROUP * g : 2 * GROUP * (g + 1)].rearrange("p (t m b) -> p t m b", t=4, b=2),
-                in_=w2_raw[g][:, h, :].rearrange("p (m t b) -> p t m b", t=4, b=2),
+                out=w2[:, h, 2 * GROUP * g : 2 * GROUP * (g + 1)].bitcast(U16).rearrange("p (t m) -> p t m", t=4),
+                in_=w2_raw[g][:, h, :].bitcast(U16).rearrange("p (m t) -> p t m", t=4),
             )
 
         def w2_sort_scales(h):
@@ -274,71 +284,101 @@ def tile_box_head_region_features_h1_kernel(
             y_turn(rt, g, copy)
             store_y(rt, g)
 
-        def store_codes(rt, count):
-            nc.sync.dma_start(out=codes_hbm[:, :, regions(rt, count)], in_=y_codes[:, :, regions(rt, count)].bitcast(I32))
+        def store_codes(rt, groups=slice(0, 2)):
+            nc.sync.dma_start(out=codes_hbm[:, groups, regions(rt)], in_=y_codes[:, groups, regions(rt)].bitcast(I32))
 
-        def store_scales():
+        def store_scales(queue):
             for r in range(4):
                 dst = scales_hbm[:, r:16:4, :].rearrange("g q n -> q g n")
-                nc.sync.dma_start(out=dst, in_=y_scales[r:P:32].bitcast(I32))
+                queue.dma_start(out=dst, in_=y_scales[r:P:32].bitcast(I32))
 
-        load_vec(nc.scalar, "b1", b1)
         make_identity(nc, ident[:])
-        for plane in s1_parts:
+        if B1_AT < 0:
+            load_vec(nc.scalar, "b1", b1)
+        clear(s1_parts[0])
+        load_s1(nc.scalar, 0)
+        zeros = tile("zeros", [P, GROUP], BF16)
+        zero_codes = tile("zero_codes", [P, P], U32)
+        zero_scales = tile("zero_scales", [P, P], U8)
+        nc.vector.memset(zeros[:].bitcast(I32), 0)
+        clear(s1_parts[1])
+        nc.vector.quantize_mx(out=zero_codes[:].bitcast(FP8X4), scales=zero_scales[:], in_=zeros[:])
+        for plane in s1_parts[2:-1]:
             clear(plane)
+        if B1_AT >= 0:
+            load_vec(nc.gpsimd, "b1", b1)
 
-        turns = [range(a, b) for a, b in zip((0,) + RUN_ENDS, RUN_ENDS)]
-        pass_ends = tuple(end - LAG for end in RUN_ENDS[:-1]) + (BLOCKS,)
-        passes = [range(a, b) for a, b in zip((0,) + pass_ends, pass_ends)]
+        runs = [blocks[a:b] for a, b in zip((0,) + ENDS, ENDS)]
+        passes = [blocks[a:b] for a, b in zip((0,) + PASS_ENDS, PASS_ENDS)]
 
-        for turn, done in zip(turns, passes):
-            load_x(turn)
-            for c in [i // TILES for i in done if i % TILES == 0]:
-                load_w1(0, c)
-                if c < len(W1_SCALE_PARTS) - 1:
-                    load_s1(c)
+        for i, b in enumerate(blocks):
+            load_x(b)
+            for j, at in enumerate(W_AT):
+                if at == i:
+                    load_w1(0, *spans[j])
+            for j, at in enumerate(S_AT):
+                if at == i:
+                    load_s1(nc.sync, j + 1)
 
-        def load_later_weights():
-            clear(s2_raw)
-            load_scale_rows(s2_raw, s2_hbm)
-            load_s1(len(W1_SCALE_PARTS) - 1)
-            load_w1(1, 0)
-            for g in range(2):
-                load_w2(g)
-                load_w1(1, g + 1)
-            load_w1(1, 3)
+        def load_late():
+            for key in LATE.split():
+                if key == "s2":
+                    load_scale_rows(nc.sync, s2_raw, s2_hbm)
+                elif key == "s1":
+                    load_s1(nc.sync, len(PARTS) - 1)
+                elif key in "abcd":
+                    load_w1(1, *spans["abcd".index(key)])
+                else:
+                    load_w2("wv".index(key))
             load_vec(nc.sync, "b2", b2)
             load_vec(nc.sync, "shift", shift)
             load_vec(nc.sync, "gain", gain)
 
-        for turn, done in zip(turns, passes):
-            x_sort(turn)
-            x_quant([i for i in done if i < turn.start])
-            for i in turn:
-                x_turn(i)
-                if i == 1:
+        if B1_AT < 0:
+            spread_b1()
+        bank = take("warm")
+        for j in range(WARM):
+            nc.tensor.matmul_mx(
+                out=bank[:, 0 : 2 * P],
+                lhsT=zero_codes[:].bitcast(FP8X4),
+                lhsT_scale=zero_scales[:],
+                rhs=s1[0, 0].bitcast(FP4X4),
+                rhs_scale=s1[0, 0][:, 0 : 2 * P],
+                start=True,
+                stop=True,
+            )
+        give_back("warm")
+
+        for b, plane in zip(runs[0], [None, s1_parts[-1], s2_raw, None]):
+            x_sort([b])
+            if plane is not None:
+                clear(plane)
+        load_late()
+        for k, (run, todo) in enumerate(zip(runs, passes)):
+            nxt = runs[k + 1] if k + 1 < len(runs) else []
+            for b in run:
+                x_turn([b])
+                if B1_AT >= 0 and b == blocks[B1_AT]:
                     spread_b1()
-            x_quant([i for i in done if i >= turn.start])
-            for i in done:
-                mm1(i, 0)
-            if turn.start == 0:
-                load_later_weights()
-        for h in range(2):
-            w2_sort_scales(h)
+            x_quant(todo)
+            x_sort(nxt)
+            mm1(todo, 0)
         for rt in range(TILES):
             h_add(rt, 0)
+        for h in range(2):
+            w2_sort_scales(h)
         for h in range(2):
             w2_sort_words(h, 0)
 
         low, high = (0, 1), (2, 3)
         pairs = [(g, slices) for g in range(2) for slices in (low, high)]
-        front, back = range(0, 2), range(2, 4)
-        for c in range(4):
+        front, back = (0, 4), (4, GROUPS)
+        for g, n in spans:
             for rt in range(2):
-                mm1_second_half(rt, [c])
+                mm1_second_half(rt, g, g + n)
         for rt in range(2):
             h_add(rt, 1)
-        mm1_second_half(2, front)
+        mm1_second_half(2, *front)
         for key in [(0, 0), (0, 1), (1, 0), (1, 1), (2, 0), (3, 0)]:
             h_turn(*key)
         for key in [(0, 0), (0, 1), (2, 0), (3, 0)]:
@@ -347,7 +387,7 @@ def tile_box_head_region_features_h1_kernel(
             w2_sort_words(h, 1)
         for h in range(2):
             h_quant(0, h)
-        mm1_second_half(2, back)
+        mm1_second_half(2, *back)
         for h in range(2):
             h_relu(1, h, VECTOR)
         h_add(2, 1)
@@ -357,7 +397,7 @@ def tile_box_head_region_features_h1_kernel(
         for g, slices in pairs:
             stage2(0, g, slices)
             y_affine(0, g, slices)
-        mm1_second_half(3, front)
+        mm1_second_half(3, *front)
         h_turn(2, 1)
         h_relu(2, 1, VECTOR)
         for g in range(2):
@@ -367,12 +407,12 @@ def tile_box_head_region_features_h1_kernel(
         y_round(0, 1)
         for g in range(2):
             y_quant(0, g)
-        store_codes(0, 1)
+        store_codes(0)
 
         for g, slices in pairs:
             stage2(1, g, slices)
             y_affine(1, g, slices)
-        mm1_second_half(3, back)
+        mm1_second_half(3, *back)
         h_add(3, 1)
         for g in range(2):
             y_round(1, g)
@@ -385,7 +425,7 @@ def tile_box_head_region_features_h1_kernel(
         h_quant(3, 1)
         y_quant(1, 1)
         y_leave(1, 0)
-        store_codes(1, 1)
+        store_codes(1)
         y_affine(2, 1, low + high)
         y_leave(1, 1, nc.vector.tensor_copy)
         y_leave(2, 0)
@@ -398,7 +438,7 @@ def tile_box_head_region_features_h1_kernel(
             y_affine(3, g, low)
             y_quant(2, g)
             y_affine(3, g, high)
-        store_codes(2, 1)
+        store_codes(2)
         y_leave(2, 1)
         y_leave(3, 0)
         for g in range(2):
@@ -406,6 +446,6 @@ def tile_box_head_region_features_h1_kernel(
         for g in range(2):
             y_quant(3, g)
         y_turn(3, 1)
-        store_codes(3, 1)
+        store_codes(3)
         store_y(3, 1)
-        store_scales()
+        store_scales(nc.sync)

@@ -29,7 +29,7 @@ PASS_ENDS = (3, 7, 11, 16)
 WARM = 6
 W_AT = (3, 7, 11, 15)
 S_AT = (3, 7, 11, 15)
-PARTS = [(0, 0, 1), (0, 1, 2), (0, 2, 4), (0, 4, 6), (0, 6, 8), (1, 0, 8)]
+PARTS = [(0, 0, 2), (0, 2, 4), (0, 4, 6), (0, 6, 8), (1, 0, 8)]
 B1_AT = 2
 EARLY = 0
 VLEAD = 0
@@ -67,7 +67,9 @@ def tile_box_head_region_features_h1_kernel(
         x_sorted = {b: tile("x_sorted%d_%d" % b[:2], [P, GROUP * b[2] // 2], F32) for b in blocks}
         x_codes = {b: tile("x_codes%d_%d" % b[:2], [P, P * b[2]], U32) for b in blocks}
         x_scales = {b: tile("x_scales%d_%d" % b[:2], [P, P * b[2]], U8) for b in blocks}
-        w1 = {(h, g, n): tile("w1_%d_%d" % (h, g), [P, n, 2 * GROUP], U8) for h in range(2) for g, n in spans}
+        w1_parts = [(0, 0, 1), (0, 1, 1)] + [(h, g, n) for h in range(2) for g, n in spans][1:]
+        w1_tiles = {part: tile("w1_%d_%d" % part[:2], [P, part[2], 2 * GROUP], U8) for part in w1_parts}
+        w1 = {(h, g + j): w1_tiles[h, g, n][:, j, :] for h, g, n in w1_parts for j in range(n)}
         scale_parts = PARTS
         s1_parts = [tile("s1_%d" % i, [P, g1 - g0, GROUP], U8) for i, (h, g0, g1) in enumerate(scale_parts)]
         s1 = {(h, g): s1_parts[i][:, g - g0, :] for i, (h, g0, g1) in enumerate(scale_parts) for g in range(g0, g1)}
@@ -112,7 +114,7 @@ def tile_box_head_region_features_h1_kernel(
 
         def load_w1(h, g, n):
             src = w1_hbm[g : g + n, :, 256 * h : 256 * (h + 1)]
-            nc.sync.dma_start(out=w1[h, g, n][:].bitcast(I32), in_=src.rearrange("g p n -> p g n"))
+            nc.sync.dma_start(out=w1_tiles[h, g, n][:].bitcast(I32), in_=src.rearrange("g p n -> p g n"))
 
         def load_w2(g):
             src = w2_hbm[:, :, 256 * g : 256 * (g + 1)]
@@ -169,7 +171,7 @@ def tile_box_head_region_features_h1_kernel(
                         out=bank[:],
                         lhsT=x_codes[b][:, P * j : P * (j + 1)].bitcast(FP8X4),
                         lhsT_scale=x_scales[b][:, P * j : P * (j + 1)],
-                        rhs=w1[h, g0, n][:, j, :].bitcast(FP4X4),
+                        rhs=w1[h, g].bitcast(FP4X4),
                         rhs_scale=s1[h, g],
                         start=(g == 0),
                         stop=(g == GROUPS - 1),
@@ -293,20 +295,16 @@ def tile_box_head_region_features_h1_kernel(
                 queue.dma_start(out=dst, in_=y_scales[r:P:32].bitcast(I32))
 
         make_identity(nc, ident[:])
-        if B1_AT < 0:
-            load_vec(nc.scalar, "b1", b1)
-        clear(s1_parts[0])
-        load_s1(nc.scalar, 0)
-        zeros = tile("zeros", [P, GROUP], BF16)
-        zero_codes = tile("zero_codes", [P, P], U32)
-        zero_scales = tile("zero_scales", [P, P], U8)
+        load_vec(nc.scalar, "b1", b1)
+        load_w1(0, 0, 1)
+        zeros = tile("zeros", [P, 2 * GROUP], BF16)
+        zero_codes = tile("zero_codes", [P, 2 * P], U32)
+        zero_scales = tile("zero_scales", [P, 2 * P], U8)
         nc.vector.memset(zeros[:].bitcast(I32), 0)
-        clear(s1_parts[1])
+        clear(s1_parts[0])
         nc.vector.quantize_mx(out=zero_codes[:].bitcast(FP8X4), scales=zero_scales[:], in_=zeros[:])
-        for plane in s1_parts[2:-1]:
+        for plane in s1_parts[1:-1]:
             clear(plane)
-        if B1_AT >= 0:
-            load_vec(nc.gpsimd, "b1", b1)
 
         runs = [blocks[a:b] for a, b in zip((0,) + ENDS, ENDS)]
         passes = [blocks[a:b] for a, b in zip((0,) + PASS_ENDS, PASS_ENDS)]
@@ -315,10 +313,10 @@ def tile_box_head_region_features_h1_kernel(
             load_x(b)
             for j, at in enumerate(W_AT):
                 if at == i:
-                    load_w1(0, *spans[j])
+                    load_w1(*w1_parts[j + 1])
             for j, at in enumerate(S_AT):
                 if at == i:
-                    load_s1(nc.sync, j + 1)
+                    load_s1(nc.sync, j)
 
         def load_late():
             for key in LATE.split():
@@ -340,10 +338,10 @@ def tile_box_head_region_features_h1_kernel(
         for j in range(WARM):
             nc.tensor.matmul_mx(
                 out=bank[:, 0 : 2 * P],
-                lhsT=zero_codes[:].bitcast(FP8X4),
-                lhsT_scale=zero_scales[:],
-                rhs=s1[0, 0].bitcast(FP4X4),
-                rhs_scale=s1[0, 0][:, 0 : 2 * P],
+                lhsT=zero_codes[:, 0:P].bitcast(FP8X4),
+                lhsT_scale=zero_scales[:, 0:P],
+                rhs=w1[0, 0][:, 0:GROUP].bitcast(FP4X4),
+                rhs_scale=zero_scales[:],
                 start=True,
                 stop=True,
             )

@@ -25,7 +25,7 @@ U16 = mybir.dt.uint16
 GROUPS = D // GROUP
 SINGLES = 0
 ENDS = (4, 8, 12, 16)
-PASS_ENDS = (3, 7, 11, 16)
+PASS_ENDS = (2, 6, 10, 16)
 WARM = 6
 W_AT = (3, 7, 11, 15)
 S_AT = (3, 7, 11, 15)
@@ -33,8 +33,10 @@ PARTS = [(0, 0, 2), (0, 2, 4), (0, 4, 6), (0, 6, 8), (1, 0, 8)]
 B1_AT = 2
 EARLY = 0
 VLEAD = 0
-CUT = 2
-LATE = "s1 a b s2 c d w v"
+POOL = ()
+WHOLE = ()
+X_SPANS = ((0, 2), (2, 2), (4, 2), (6, 2))
+LATE = "a s1 b c s2 d w v"
 
 
 def tile_box_head_region_features_h1_kernel(
@@ -61,8 +63,8 @@ def tile_box_head_region_features_h1_kernel(
         ident = tile("ident", [P, P], F32)
         vec = {key: tile("vec_" + key, [P, 2, 4], BF16) for key in ("b1", "b2", "shift", "gain")}
         b1_rows = tile("b1_rows", [P, F], BF16)
-        spans = [(g, 1) for g in range(SINGLES)] + [(g, 2) for g in range(SINGLES, GROUPS, 2)]
-        blocks = [(rt, g, n) for g, n in spans for rt in range(TILES)]
+        spans = [(g, 2) for g in range(0, GROUPS, 2)]
+        blocks = [(rt, g, n) for g, n in X_SPANS for rt in range(TILES)]
         x_raw = {b: tile("x_raw%d_%d" % b[:2], [P, GROUP * b[2]], BF16) for b in blocks}
         x_sorted = {b: tile("x_sorted%d_%d" % b[:2], [P, GROUP * b[2] // 2], F32) for b in blocks}
         x_codes = {b: tile("x_codes%d_%d" % b[:2], [P, P * b[2]], U32) for b in blocks}
@@ -73,14 +75,14 @@ def tile_box_head_region_features_h1_kernel(
         scale_parts = PARTS
         s1_parts = [tile("s1_%d" % i, [P, g1 - g0, GROUP], U8) for i, (h, g0, g1) in enumerate(scale_parts)]
         s1 = {(h, g): s1_parts[i][:, g - g0, :] for i, (h, g0, g1) in enumerate(scale_parts) for g in range(g0, g1)}
-        w2_raw = [tile("w2_raw%d" % g, [P, 2, 2 * GROUP], U8) for g in range(2)]
+        w2_raw = [tile("w2_raw%d" % h, [P, 2 * N], U8) for h in range(2)]
         s2_raw = tile("s2_raw", [P, 2, N], U8)
         w2 = tile("w2", [P, 2, 2 * N], U8)
         s2 = tile("s2", [P, 2, N], U8)
         h_biased = {key: tile("h_biased%d_%d" % key, [P, GROUP], BF16) for key in halves}
-        h_turned = {key: tile("h_turned%d_%d" % key, [P, GROUP], BF16) for key in halves}
-        h_codes = {key: tile("h_codes%d_%d" % key, [P, P], U32) for key in halves}
-        h_scales = {key: tile("h_scales%d_%d" % key, [P, P], U8) for key in halves}
+        h_turned = [tile("h_turned%d" % h, [P, TILES * GROUP], BF16) for h in range(2)]
+        h_codes = [tile("h_codes%d" % h, [P, R], U32) for h in range(2)]
+        h_scales = [tile("h_scales%d" % h, [P, R], U8) for h in range(2)]
         a_t = [tile("a_t%d" % g, [P, 4, R], F32) for g in range(2)]
         y_t = [tile("y_t%d" % g, [P, 4, R], F32) for g in range(2)]
         y_bf16 = [tile("y_bf16_%d" % g, [P, R, 4], BF16) for g in range(2)]
@@ -116,9 +118,8 @@ def tile_box_head_region_features_h1_kernel(
             src = w1_hbm[g : g + n, :, 256 * h : 256 * (h + 1)]
             nc.sync.dma_start(out=w1_tiles[h, g, n][:].bitcast(I32), in_=src.rearrange("g p n -> p g n"))
 
-        def load_w2(g):
-            src = w2_hbm[:, :, 256 * g : 256 * (g + 1)]
-            nc.sync.dma_start(out=w2_raw[g][:].bitcast(I32), in_=src.rearrange("h p n -> p h n"))
+        def load_w2(h):
+            nc.sync.dma_start(out=w2_raw[h][:].bitcast(I32), in_=w2_hbm[h])
 
         def load_scale_rows(queue, plane, src):
             for r in range(4):
@@ -148,71 +149,73 @@ def tile_box_head_region_features_h1_kernel(
 
         def x_turn(run):
             for b in run:
-                bank = take(("x", b))
-                for j in range(2 * b[2]):
-                    nc.tensor.transpose(bank[:, P * j : P * (j + 1)], x_sorted[b][:, P * j : P * (j + 1)], ident[:])
-                nc.scalar.copy(
-                    out=x_raw[b][:].bitcast(F32).rearrange("p (g r u) -> p g r u", g=b[2], u=2),
-                    in_=bank[:, 0 : 2 * P * b[2]].rearrange("p (g u r) -> p g r u", g=b[2], u=2),
-                )
-                give_back(("x", b))
+                for c in range(b[2] // 2):
+                    bank = take(("x", b))
+                    for j in range(4):
+                        words = x_sorted[b][:, GROUP * c + P * j : GROUP * c + P * (j + 1)]
+                        nc.tensor.transpose(bank[:, P * j : P * (j + 1)], words, ident[:])
+                    nc.scalar.copy(
+                        out=x_raw[b][:].bitcast(F32)[:, GROUP * c : GROUP * (c + 1)].rearrange("p (g r u) -> p g r u", g=2, u=2),
+                        in_=bank[:].rearrange("p (g u r) -> p g r u", g=2, u=2),
+                    )
+                    give_back(("x", b))
 
         def x_quant(run):
             for b in run:
                 nc.vector.quantize_mx(out=x_codes[b][:].bitcast(FP8X4), scales=x_scales[b][:], in_=x_raw[b][:])
 
-        def mm1(run, h):
-            for b in run:
-                rt, g0, n = b
-                bank = take(("h", rt, h)) if g0 == 0 else bank_of(("h", rt, h))
-                for j in range(n):
-                    g = g0 + j
-                    nc.tensor.matmul_mx(
-                        out=bank[:],
-                        lhsT=x_codes[b][:, P * j : P * (j + 1)].bitcast(FP8X4),
-                        lhsT_scale=x_scales[b][:, P * j : P * (j + 1)],
-                        rhs=w1[h, g].bitcast(FP4X4),
-                        rhs_scale=s1[h, g],
-                        start=(g == 0),
-                        stop=(g == GROUPS - 1),
-                    )
-
-        def mm1_second_half(rt, g0, g1):
-            mm1([b for b in blocks if b[0] == rt and g0 <= b[1] < g1], 1)
-
-        def h_add(rt, h):
-            for u in range(2):
-                cols = slice(256 * u, 256 * (u + 1))
-                nc.vector.tensor_tensor(
-                    out=h_biased[rt, h][:, cols].rearrange("r (m e) -> r m e", e=2),
-                    in0=bank_of(("h", rt, h))[:].rearrange("r (m u e) -> r u m e", u=2, e=2)[:, u],
-                    in1=b1_rows[:, GROUP * h : GROUP * (h + 1)][:, cols].rearrange("r (m e) -> r m e", e=2),
-                    op=ALU.add,
+        def mm1(rt, h, g0, g1):
+            bank = take(("h", rt, h)) if g0 == 0 else bank_of(("h", rt, h))
+            for g in range(g0, g1):
+                b = [b for b in blocks if b[0] == rt and b[1] <= g < b[1] + b[2]][0]
+                cols = slice(P * (g - b[1]), P * (g - b[1] + 1))
+                nc.tensor.matmul_mx(
+                    out=bank[:],
+                    lhsT=x_codes[b][:, cols].bitcast(FP8X4),
+                    lhsT_scale=x_scales[b][:, cols],
+                    rhs=w1[h, g].bitcast(FP4X4),
+                    rhs_scale=s1[h, g],
+                    start=(g == 0),
+                    stop=(g == GROUPS - 1),
                 )
+
+        def h_add(rt, h, parts=1):
+            dst = h_biased[rt, h][:].rearrange("r (u m e) -> r u m e", u=2, e=2)
+            src = bank_of(("h", rt, h))[:].rearrange("r (m u e) -> r u m e", u=2, e=2)
+            bias = b1_rows[:, GROUP * h : GROUP * (h + 1)].rearrange("r (u m e) -> r u m e", u=2, e=2)
+            for u in [slice(0, 2)] if parts == 1 else [0, 1]:
+                nc.vector.tensor_tensor(out=dst[:, u], in0=src[:, u], in1=bias[:, u], op=ALU.add)
             give_back(("h", rt, h))
 
-        def h_turn(rt, h):
+        def h_turn(rt, count, h):
             bank = take(("ht", rt, h))
-            words = h_biased[rt, h][:].bitcast(F32)
-            for u in range(2):
-                nc.tensor.transpose(bank[:, P * u : P * (u + 1)], words[:, P * u : P * (u + 1)], ident[:])
+            for j in range(count):
+                words = h_biased[rt + j, h][:].bitcast(F32)
+                for u in range(2):
+                    cols = slice(P * (count * u + j), P * (count * u + j + 1))
+                    nc.tensor.transpose(bank[:, cols], words[:, P * u : P * (u + 1)], ident[:])
 
-        def h_relu(rt, h, engine):
-            src = bank_of(("ht", rt, h))[:, 0 : 2 * P].bitcast(BF16).rearrange("p (u r e) -> p r u e", u=2, e=2)
-            dst = h_turned[rt, h][:].rearrange("p (r u e) -> p r u e", u=2, e=2)
+        def h_relu(rt, count, h, engine):
+            src = bank_of(("ht", rt, h))[:, 0 : 2 * P * count].bitcast(BF16)
+            src = src.rearrange("p (u r e) -> p r u e", u=2, e=2)
+            dst = h_turned[h][:, GROUP * rt : GROUP * (rt + count)].rearrange("p (r u e) -> p r u e", u=2, e=2)
             if engine == SCALAR:
                 nc.scalar.activation(out=dst, in_=src, func=ACT.Relu)
             else:
                 nc.vector.tensor_scalar(out=dst, in0=src, scalar1=0.0, scalar2=None, op0=ALU.max)
             give_back(("ht", rt, h))
 
-        def h_quant(rt, h):
-            nc.vector.quantize_mx(out=h_codes[rt, h][:].bitcast(FP8X4), scales=h_scales[rt, h][:], in_=h_turned[rt, h][:])
+        def h_quant(rt, count, h):
+            nc.vector.quantize_mx(
+                out=h_codes[h][:, regions(rt, count)].bitcast(FP8X4),
+                scales=h_scales[h][:, regions(rt, count)],
+                in_=h_turned[h][:, GROUP * rt : GROUP * (rt + count)],
+            )
 
-        def w2_sort_words(h, g):
+        def w2_sort_words(h):
             nc.vector.tensor_copy(
-                out=w2[:, h, 2 * GROUP * g : 2 * GROUP * (g + 1)].bitcast(U16).rearrange("p (t m) -> p t m", t=4),
-                in_=w2_raw[g][:, h, :].bitcast(U16).rearrange("p (m t) -> p t m", t=4),
+                out=w2[:, h, :].bitcast(U16).rearrange("p (g t m) -> p g t m", g=2, t=4),
+                in_=w2_raw[h][:].bitcast(U16).rearrange("p (g m t) -> p g t m", g=2, t=4),
             )
 
         def w2_sort_scales(h):
@@ -221,51 +224,53 @@ def tile_box_head_region_features_h1_kernel(
                 in_=s2_raw[:, h, :].rearrange("p (g m t) -> p g t m", g=2, t=4),
             )
 
-        def stage2(rt, g, slices):
+        def stage2(rt, count, g, slices, engine=SCALAR):
             bank = take(("z", rt, g, slices))
+            width = P * count
             for j, t in enumerate(slices):
                 col = GROUP * g + P * t
-                for h in range(2):
-                    nc.tensor.matmul_mx(
-                        out=bank[:, P * j : P * (j + 1)],
-                        lhsT=w2[:, h, 2 * col : 2 * (col + P)].bitcast(FP4X4),
-                        lhsT_scale=s2[:, h, col : col + P],
-                        rhs=h_codes[rt, h][:].bitcast(FP8X4),
-                        rhs_scale=h_scales[rt, h][:],
-                        start=(h == 0),
-                        stop=(h == 1),
-                    )
+                for i in range(count):
+                    for h in range(2):
+                        nc.tensor.matmul_mx(
+                            out=bank[:, width * j + P * i : width * j + P * (i + 1)],
+                            lhsT=w2[:, h, 2 * col : 2 * (col + P)].bitcast(FP4X4),
+                            lhsT_scale=s2[:, h, col : col + P],
+                            rhs=h_codes[h][:, regions(rt + i)].bitcast(FP8X4),
+                            rhs_scale=h_scales[h][:, regions(rt + i)],
+                            start=(h == 0),
+                            stop=(h == 1),
+                        )
             for j, t in enumerate(slices):
-                nc.scalar.activation(
-                    out=a_t[g][:, t, regions(rt)],
-                    in_=bank[:, P * j : P * (j + 1)],
-                    func=ACT.Relu,
-                    bias=vec["b2"][:, g, t : t + 1],
-                )
+                dst, src = a_t[g][:, t, regions(rt, count)], bank[:, width * j : width * (j + 1)]
+                bias = vec["b2"][:, g, t : t + 1]
+                if engine == SCALAR:
+                    nc.scalar.activation(out=dst, in_=src, func=ACT.Relu, bias=bias)
+                else:
+                    nc.vector.tensor_scalar(out=dst, in0=src, scalar1=bias, scalar2=0.0, op0=ALU.add, op1=ALU.max)
             give_back(("z", rt, g, slices))
 
-        def y_affine(rt, g, slices):
+        def y_affine(rt, count, g, slices):
             for t in slices:
                 nc.vector.tensor_scalar(
-                    out=y_t[g][:, t, regions(rt)],
-                    in0=a_t[g][:, t, regions(rt)],
+                    out=y_t[g][:, t, regions(rt, count)],
+                    in0=a_t[g][:, t, regions(rt, count)],
                     scalar1=vec["shift"][:, g, t : t + 1],
                     scalar2=vec["gain"][:, g, t : t + 1],
                     op0=ALU.add,
                     op1=ALU.mult,
                 )
 
-        def y_round(rt, g):
+        def y_round(rt, count, g):
             nc.vector.tensor_copy(
-                out=y_bf16[g][:, regions(rt), :],
-                in_=y_t[g][:, :, regions(rt)].rearrange("p t r -> p r t"),
+                out=y_bf16[g][:, regions(rt, count), :],
+                in_=y_t[g][:, :, regions(rt, count)].rearrange("p t r -> p r t"),
             )
 
-        def y_quant(rt, g):
+        def y_quant(rt, count, g):
             nc.vector.quantize_mx(
-                out=y_codes[:, g, regions(rt)].bitcast(FP8X4),
-                scales=y_scales[:, g, regions(rt)],
-                in_=y_bf16[g][:, regions(rt), :].rearrange("p r t -> p (r t)"),
+                out=y_codes[:, g, regions(rt, count)].bitcast(FP8X4),
+                scales=y_scales[:, g, regions(rt, count)],
+                in_=y_bf16[g][:, regions(rt, count), :].rearrange("p r t -> p (r t)"),
             )
 
         def y_turn(rt, g, copy=nc.scalar.copy):
@@ -279,6 +284,10 @@ def tile_box_head_region_features_h1_kernel(
             give_back(("y", rt, g))
 
         def store_y(rt, g):
+            if rt in WHOLE:
+                if g == 1:
+                    nc.sync.dma_start(out=out_0[regions(rt), :], in_=y_rows[rt][:])
+                return
             cols = slice(GROUP * g, GROUP * (g + 1))
             nc.sync.dma_start(out=out_0[regions(rt), cols], in_=y_rows[rt][:, cols])
 
@@ -286,8 +295,9 @@ def tile_box_head_region_features_h1_kernel(
             y_turn(rt, g, copy)
             store_y(rt, g)
 
-        def store_codes(rt, groups=slice(0, 2)):
-            nc.sync.dma_start(out=codes_hbm[:, groups, regions(rt)], in_=y_codes[:, groups, regions(rt)].bitcast(I32))
+        def store_codes(rt, count, groups=slice(0, 2)):
+            cols = regions(rt, count)
+            nc.sync.dma_start(out=codes_hbm[:, groups, cols], in_=y_codes[:, groups, cols].bitcast(I32))
 
         def store_scales(queue):
             for r in range(4):
@@ -295,27 +305,31 @@ def tile_box_head_region_features_h1_kernel(
                 queue.dma_start(out=dst, in_=y_scales[r:P:32].bitcast(I32))
 
         make_identity(nc, ident[:])
-        load_vec(nc.scalar, "b1", b1)
         load_w1(0, 0, 1)
         zeros = tile("zeros", [P, 2 * GROUP], BF16)
         zero_codes = tile("zero_codes", [P, 2 * P], U32)
         zero_scales = tile("zero_scales", [P, 2 * P], U8)
+        if POOL:
+            clear(s1_parts[POOL[0]])
         nc.vector.memset(zeros[:].bitcast(I32), 0)
-        clear(s1_parts[0])
         nc.vector.quantize_mx(out=zero_codes[:].bitcast(FP8X4), scales=zero_scales[:], in_=zeros[:])
-        for plane in s1_parts[1:-1]:
+        for plane in [t for j, t in enumerate(s1_parts[:-1]) if (j,) != POOL[:1]]:
             clear(plane)
+        for j in POOL:
+            load_s1(nc.gpsimd, j)
 
         runs = [blocks[a:b] for a, b in zip((0,) + ENDS, ENDS)]
         passes = [blocks[a:b] for a, b in zip((0,) + PASS_ENDS, PASS_ENDS)]
 
         for i, b in enumerate(blocks):
             load_x(b)
+            if i == 1:
+                load_vec(nc.sync, "b1", b1)
             for j, at in enumerate(W_AT):
                 if at == i:
                     load_w1(*w1_parts[j + 1])
             for j, at in enumerate(S_AT):
-                if at == i:
+                if at == i and j not in POOL:
                     load_s1(nc.sync, j)
 
         def load_late():
@@ -360,90 +374,84 @@ def tile_box_head_region_features_h1_kernel(
                     spread_b1()
             x_quant(todo)
             x_sort(nxt)
-            mm1(todo, 0)
-        for rt in range(TILES):
-            h_add(rt, 0)
-        for h in range(2):
-            w2_sort_scales(h)
-        for h in range(2):
-            w2_sort_words(h, 0)
-
+            for rt, g, n in todo:
+                mm1(rt, 0, g, g + n)
         low, high = (0, 1), (2, 3)
         pairs = [(g, slices) for g in range(2) for slices in (low, high)]
-        front, back = (0, 4), (4, GROUPS)
-        for g, n in spans:
+        for rt in range(TILES):
+            h_add(rt, 0)
+        for g in (0, 2):
             for rt in range(2):
-                mm1_second_half(rt, g, g + n)
+                mm1(rt, 1, g, g + 2)
+        for rt in (0, 2):
+            h_turn(rt, 2, 0)
+        for rt in (0, 2):
+            h_relu(rt, 2, 0, SCALAR)
+        for h in range(2):
+            w2_sort_scales(h)
+        for g in (4, 6):
+            for rt in range(2):
+                mm1(rt, 1, g, g + 2)
+        for h in range(2):
+            w2_sort_words(h)
+        h_quant(0, 2, 0)
         for rt in range(2):
             h_add(rt, 1)
-        mm1_second_half(2, *front)
-        for key in [(0, 0), (0, 1), (1, 0), (1, 1), (2, 0), (3, 0)]:
-            h_turn(*key)
-        for key in [(0, 0), (0, 1), (2, 0), (3, 0)]:
-            h_relu(*key, SCALAR)
-        for h in range(2):
-            w2_sort_words(h, 1)
-        for h in range(2):
-            h_quant(0, h)
-        mm1_second_half(2, *back)
-        for h in range(2):
-            h_relu(1, h, VECTOR)
+        mm1(2, 1, 0, 4)
+        h_quant(2, 2, 0)
+        for rt in range(2):
+            h_turn(rt, 1, 1)
+        h_relu(0, 1, 1, SCALAR)
+        h_relu(1, 1, 1, VECTOR)
+        mm1(2, 1, 4, 8)
+        h_quant(0, 2, 1)
+        mm1(3, 1, 0, 2)
         h_add(2, 1)
-        for key in [(1, 0), (1, 1), (2, 0), (3, 0)]:
-            h_quant(*key)
 
         for g, slices in pairs:
-            stage2(0, g, slices)
-            y_affine(0, g, slices)
-        mm1_second_half(3, *front)
-        h_turn(2, 1)
-        h_relu(2, 1, VECTOR)
-        for g in range(2):
-            y_leave(0, g)
-        y_round(0, 0)
-        h_quant(2, 1)
-        y_round(0, 1)
-        for g in range(2):
-            y_quant(0, g)
-        store_codes(0)
+            stage2(0, 2, g, slices)
+            y_affine(0, 2, g, slices)
+        mm1(3, 1, 2, 4)
+        h_turn(2, 1, 1)
+        h_relu(2, 1, 1, SCALAR)
+        for rt, g in [(0, 0), (1, 0), (0, 1)]:
+            y_leave(rt, g)
+        y_round(0, 2, 0)
+        h_quant(2, 1, 1)
+        y_round(0, 2, 1)
+        y_quant(0, 2, 0)
+        mm1(3, 1, 4, 8)
+        h_add(3, 1, 2)
+        y_quant(0, 2, 1)
+        store_codes(0, 2)
 
         for g, slices in pairs:
-            stage2(1, g, slices)
-            y_affine(1, g, slices)
-        mm1_second_half(3, *back)
-        h_add(3, 1)
-        for g in range(2):
-            y_round(1, g)
-        for g, slices in pairs:
-            stage2(2, g, slices)
-        h_turn(3, 1)
-        y_affine(2, 0, low + high)
-        h_relu(3, 1, VECTOR)
-        y_quant(1, 0)
-        h_quant(3, 1)
-        y_quant(1, 1)
-        y_leave(1, 0)
-        store_codes(1)
-        y_affine(2, 1, low + high)
-        y_leave(1, 1, nc.vector.tensor_copy)
+            stage2(2, 1, g, slices)
+        y_affine(2, 1, 0, low + high)
+        h_turn(3, 1, 1)
+        h_relu(3, 1, 1, VECTOR)
+        y_leave(1, 1)
         y_leave(2, 0)
+        y_affine(2, 1, 1, low)
+        h_quant(3, 1, 1)
+        y_affine(2, 1, 1, high)
+        y_round(2, 1, 0)
 
-        for g in range(2):
-            y_round(2, g)
         for g, slices in pairs:
-            stage2(3, g, slices)
-        for g in range(2):
-            y_affine(3, g, low)
-            y_quant(2, g)
-            y_affine(3, g, high)
-        store_codes(2)
+            stage2(3, 1, g, slices)
+        y_quant(2, 1, 0)
+        y_round(2, 1, 1)
+        y_affine(3, 1, 0, low + high)
+        y_quant(2, 1, 1)
+        store_codes(2, 1)
+        y_affine(3, 1, 1, low + high)
         y_leave(2, 1)
         y_leave(3, 0)
         for g in range(2):
-            y_round(3, g)
-        for g in range(2):
-            y_quant(3, g)
+            y_round(3, 1, g)
         y_turn(3, 1)
-        store_codes(3)
+        for g in range(2):
+            y_quant(3, 1, g)
+        store_codes(3, 1)
         store_y(3, 1)
         store_scales(nc.sync)

@@ -26,11 +26,15 @@ GROUPS = D // GROUP
 SINGLES = 0
 ENDS = (4, 8, 12, 16)
 PASS_ENDS = (2, 6, 10, 16)
-WARM = 6
+WARM = (3, 0, 0, 1)
+WN = 512
+OPEN = 6
+ON_V = ((0, 0), (0, 2))
+B1_V = 1
 W_AT = (3, 7, 11, 15)
 S_AT = (3, 7, 11, 15)
 PARTS = [(0, 0, 2), (0, 2, 4), (0, 4, 6), (0, 6, 8), (1, 0, 8)]
-B1_AT = 2
+B1_AT = 1
 EARLY = 0
 VLEAD = 0
 POOL = ()
@@ -137,12 +141,12 @@ def tile_box_head_region_features_h1_kernel(
             words = vec["b1"][:].rearrange("p g t -> p (g t)").bitcast(F32)
             for j in range(4):
                 nc.tensor.transpose(bank[:, P * j : P * (j + 1)], words[:, j : j + 1].to_broadcast([P, P]), ident[:])
-            nc.scalar.copy(out=b1_rows[:].bitcast(F32), in_=bank[:])
+            (nc.vector.tensor_copy if B1_V else nc.scalar.copy)(out=b1_rows[:].bitcast(F32), in_=bank[:])
             give_back("b1")
 
-        def x_sort(run):
+        def x_sort(run, copy=nc.vector.tensor_copy):
             for b in run:
-                nc.vector.tensor_copy(
+                copy(
                     out=x_sorted[b][:].rearrange("r (g u m) -> r g u m", g=b[2], u=2),
                     in_=x_raw[b][:].bitcast(F32).rearrange("r (g m u) -> r g u m", g=b[2], u=2),
                 )
@@ -249,6 +253,28 @@ def tile_box_head_region_features_h1_kernel(
                     nc.vector.tensor_scalar(out=dst, in0=src, scalar1=bias, scalar2=0.0, op0=ALU.add, op1=ALU.max)
             give_back(("z", rt, g, slices))
 
+        def z_pass(rt, g, t, h):
+            bank = take(("z", rt, g, t)) if h == 0 else bank_of(("z", rt, g, t))
+            col = GROUP * g + P * t
+            nc.tensor.matmul_mx(
+                out=bank[:, 0:P],
+                lhsT=w2[:, h, 2 * col : 2 * (col + P)].bitcast(FP4X4),
+                lhsT_scale=s2[:, h, col : col + P],
+                rhs=h_codes[h][:, regions(rt)].bitcast(FP8X4),
+                rhs_scale=h_scales[h][:, regions(rt)],
+                start=(h == 0),
+                stop=(h == 1),
+            )
+
+        def z_relu(rt, g, t, engine=SCALAR):
+            dst, src = a_t[g][:, t, regions(rt)], bank_of(("z", rt, g, t))[:, 0:P]
+            bias = vec["b2"][:, g, t : t + 1]
+            if engine == SCALAR:
+                nc.scalar.activation(out=dst, in_=src, func=ACT.Relu, bias=bias)
+            else:
+                nc.vector.tensor_scalar(out=dst, in0=src, scalar1=bias, scalar2=0.0, op0=ALU.add, op1=ALU.max)
+            give_back(("z", rt, g, t))
+
         def y_affine(rt, count, g, slices):
             for t in slices:
                 nc.vector.tensor_scalar(
@@ -283,6 +309,19 @@ def tile_box_head_region_features_h1_kernel(
             )
             give_back(("y", rt, g))
 
+        def y_leave_halves(rt, g):
+            bank = take(("y", rt, g))
+            for t in range(4):
+                nc.tensor.transpose(bank[:, P * t : P * (t + 1)], y_t[g][:, t, regions(rt)], ident[:])
+            for j in range(2):
+                cols = slice(GROUP * g + 256 * j, GROUP * g + 256 * (j + 1))
+                nc.scalar.copy(
+                    out=y_rows[rt][:, cols].rearrange("r (p t) -> r p t", t=4),
+                    in_=bank[:].rearrange("r (t p) -> r p t", t=4)[:, 64 * j : 64 * (j + 1), :],
+                )
+                nc.sync.dma_start(out=out_0[regions(rt), cols], in_=y_rows[rt][:, cols])
+            give_back(("y", rt, g))
+
         def store_y(rt, g):
             if rt in WHOLE:
                 if g == 1:
@@ -306,9 +345,9 @@ def tile_box_head_region_features_h1_kernel(
 
         make_identity(nc, ident[:])
         load_w1(0, 0, 1)
-        zeros = tile("zeros", [P, 2 * GROUP], BF16)
-        zero_codes = tile("zero_codes", [P, 2 * P], U32)
-        zero_scales = tile("zero_scales", [P, 2 * P], U8)
+        zeros = tile("zeros", [P, 4 * WN], BF16)
+        zero_codes = tile("zero_codes", [P, WN], U32)
+        zero_scales = tile("zero_scales", [P, WN], U8)
         if POOL:
             clear(s1_parts[POOL[0]])
         nc.vector.memset(zeros[:].bitcast(I32), 0)
@@ -346,21 +385,21 @@ def tile_box_head_region_features_h1_kernel(
             load_vec(nc.sync, "shift", shift)
             load_vec(nc.sync, "gain", gain)
 
-        if B1_AT < 0:
-            spread_b1()
-        bank = take("warm")
-        for j in range(WARM):
-            nc.tensor.matmul_mx(
-                out=bank[:, 0 : 2 * P],
-                lhsT=zero_codes[:, 0:P].bitcast(FP8X4),
-                lhsT_scale=zero_scales[:, 0:P],
-                rhs=w1[0, 0][:, 0:GROUP].bitcast(FP4X4),
-                rhs_scale=zero_scales[:],
-                start=True,
-                stop=True,
-            )
-        give_back("warm")
+        def warm(count):
+            bank = take("warm")
+            for j in range(count):
+                nc.tensor.matmul_mx(
+                    out=bank[:, 0:WN],
+                    lhsT=zero_codes[:, 0:P].bitcast(FP8X4),
+                    lhsT_scale=zero_scales[:, 0:P],
+                    rhs=w1[0, 0][:, 0 : 2 * WN].bitcast(FP4X4),
+                    rhs_scale=zero_scales[:],
+                    start=True,
+                    stop=True,
+                )
+            give_back("warm")
 
+        warm(WARM[0])
         for b, plane in zip(runs[0], [None, s1_parts[-1], s2_raw, None]):
             x_sort([b])
             if plane is not None:
@@ -370,8 +409,10 @@ def tile_box_head_region_features_h1_kernel(
             nxt = runs[k + 1] if k + 1 < len(runs) else []
             for b in run:
                 x_turn([b])
-                if B1_AT >= 0 and b == blocks[B1_AT]:
+                if b == blocks[B1_AT]:
                     spread_b1()
+                if blocks.index(b) + 1 < len(WARM) and WARM[blocks.index(b) + 1]:
+                    warm(WARM[blocks.index(b) + 1])
             x_quant(todo)
             x_sort(nxt)
             for rt, g, n in todo:
@@ -437,8 +478,14 @@ def tile_box_head_region_features_h1_kernel(
         y_affine(2, 1, 1, high)
         y_round(2, 1, 0)
 
-        for g, slices in pairs:
-            stage2(3, 1, g, slices)
+        order = [(g, t) for g in range(2) for t in range(4)]
+        for g, t in order[:OPEN]:
+            z_pass(3, g, t, 0)
+        for g, t in order:
+            if (g, t) not in order[:OPEN]:
+                z_pass(3, g, t, 0)
+            z_pass(3, g, t, 1)
+            z_relu(3, g, t, VECTOR if (g, t) in ON_V else SCALAR)
         y_quant(2, 1, 0)
         y_round(2, 1, 1)
         y_affine(3, 1, 0, low + high)
@@ -454,4 +501,4 @@ def tile_box_head_region_features_h1_kernel(
             y_quant(3, 1, g)
         store_codes(3, 1)
         store_y(3, 1)
-        store_scales(nc.sync)
+        store_scales(nc.scalar)

@@ -27,14 +27,14 @@ SINGLES = 0
 ENDS = (4, 8, 12, 16)
 PASS_ENDS = (2, 6, 10, 16)
 WARM = (3, 0, 0, 1)
-WN = 512
+B1_LOAD = -1
 OPEN = 6
 ON_V = ((0, 0), (0, 2))
-B1_V = 1
+B1_V = 0
 W_AT = (3, 7, 11, 15)
 S_AT = (3, 7, 11, 15)
 PARTS = [(0, 0, 2), (0, 2, 4), (0, 4, 6), (0, 6, 8), (1, 0, 8)]
-B1_AT = 1
+B1_AT = -1
 EARLY = 0
 VLEAD = 0
 POOL = ()
@@ -73,7 +73,7 @@ def tile_box_head_region_features_h1_kernel(
         x_sorted = {b: tile("x_sorted%d_%d" % b[:2], [P, GROUP * b[2] // 2], F32) for b in blocks}
         x_codes = {b: tile("x_codes%d_%d" % b[:2], [P, P * b[2]], U32) for b in blocks}
         x_scales = {b: tile("x_scales%d_%d" % b[:2], [P, P * b[2]], U8) for b in blocks}
-        w1_parts = [(0, 0, 1), (0, 1, 1)] + [(h, g, n) for h in range(2) for g, n in spans][1:]
+        w1_parts = [(h, g, n) for h in range(2) for g, n in spans]
         w1_tiles = {part: tile("w1_%d_%d" % part[:2], [P, part[2], 2 * GROUP], U8) for part in w1_parts}
         w1 = {(h, g + j): w1_tiles[h, g, n][:, j, :] for h, g, n in w1_parts for j in range(n)}
         scale_parts = PARTS
@@ -344,31 +344,23 @@ def tile_box_head_region_features_h1_kernel(
                 queue.dma_start(out=dst, in_=y_scales[r:P:32].bitcast(I32))
 
         make_identity(nc, ident[:])
-        load_w1(0, 0, 1)
-        zeros = tile("zeros", [P, 4 * WN], BF16)
-        zero_codes = tile("zero_codes", [P, WN], U32)
-        zero_scales = tile("zero_scales", [P, WN], U8)
-        if POOL:
-            clear(s1_parts[POOL[0]])
-        nc.vector.memset(zeros[:].bitcast(I32), 0)
-        nc.vector.quantize_mx(out=zero_codes[:].bitcast(FP8X4), scales=zero_scales[:], in_=zeros[:])
-        for plane in [t for j, t in enumerate(s1_parts[:-1]) if (j,) != POOL[:1]]:
+        for plane in s1_parts + [s2_raw]:
             clear(plane)
-        for j in POOL:
-            load_s1(nc.gpsimd, j)
 
         runs = [blocks[a:b] for a, b in zip((0,) + ENDS, ENDS)]
         passes = [blocks[a:b] for a, b in zip((0,) + PASS_ENDS, PASS_ENDS)]
 
+        if B1_LOAD < 0:
+            load_vec(nc.sync, "b1", b1)
         for i, b in enumerate(blocks):
             load_x(b)
-            if i == 1:
+            if i == B1_LOAD:
                 load_vec(nc.sync, "b1", b1)
             for j, at in enumerate(W_AT):
                 if at == i:
-                    load_w1(*w1_parts[j + 1])
+                    load_w1(*w1_parts[j])
             for j, at in enumerate(S_AT):
-                if at == i and j not in POOL:
+                if at == i:
                     load_s1(nc.sync, j)
 
         def load_late():
@@ -385,34 +377,16 @@ def tile_box_head_region_features_h1_kernel(
             load_vec(nc.sync, "shift", shift)
             load_vec(nc.sync, "gain", gain)
 
-        def warm(count):
-            bank = take("warm")
-            for j in range(count):
-                nc.tensor.matmul_mx(
-                    out=bank[:, 0:WN],
-                    lhsT=zero_codes[:, 0:P].bitcast(FP8X4),
-                    lhsT_scale=zero_scales[:, 0:P],
-                    rhs=w1[0, 0][:, 0 : 2 * WN].bitcast(FP4X4),
-                    rhs_scale=zero_scales[:],
-                    start=True,
-                    stop=True,
-                )
-            give_back("warm")
-
-        warm(WARM[0])
-        for b, plane in zip(runs[0], [None, s1_parts[-1], s2_raw, None]):
-            x_sort([b])
-            if plane is not None:
-                clear(plane)
+        if B1_AT < 0:
+            spread_b1()
+        x_sort(runs[0])
         load_late()
         for k, (run, todo) in enumerate(zip(runs, passes)):
             nxt = runs[k + 1] if k + 1 < len(runs) else []
             for b in run:
                 x_turn([b])
-                if b == blocks[B1_AT]:
+                if B1_AT >= 0 and b == blocks[B1_AT]:
                     spread_b1()
-                if blocks.index(b) + 1 < len(WARM) and WARM[blocks.index(b) + 1]:
-                    warm(WARM[blocks.index(b) + 1])
             x_quant(todo)
             x_sort(nxt)
             for rt, g, n in todo:

@@ -32,12 +32,12 @@ OPEN = 6
 ON_V = ((0, 0), (0, 2))
 B1_V = 0
 W_AT = (3, 7, 11, 15)
-S_AT = (3, 7, 11, 15)
-PARTS = [(0, 0, 2), (0, 2, 4), (0, 4, 6), (0, 6, 8), (1, 0, 8)]
+S_AT = (3, 3, 15)
+PARTS = [(0, 0, 2), (0, 2, 6), (0, 6, 8), (1, 0, 8)]
 B1_AT = -1
 EARLY = 0
 VLEAD = 0
-POOL = ()
+POOL = (1,)
 WHOLE = ()
 X_SPANS = ((0, 2), (2, 2), (4, 2), (6, 2))
 LATE = "a s1 b c s2 d w v"
@@ -344,8 +344,10 @@ def tile_box_head_region_features_h1_kernel(
                 queue.dma_start(out=dst, in_=y_scales[r:P:32].bitcast(I32))
 
         make_identity(nc, ident[:])
-        for plane in s1_parts + [s2_raw]:
+        for plane in s1_parts[:-1]:
             clear(plane)
+        for j in POOL:
+            load_s1(nc.gpsimd, j)
 
         runs = [blocks[a:b] for a, b in zip((0,) + ENDS, ENDS)]
         passes = [blocks[a:b] for a, b in zip((0,) + PASS_ENDS, PASS_ENDS)]
@@ -360,7 +362,7 @@ def tile_box_head_region_features_h1_kernel(
                 if at == i:
                     load_w1(*w1_parts[j])
             for j, at in enumerate(S_AT):
-                if at == i:
+                if at == i and j not in POOL:
                     load_s1(nc.sync, j)
 
         def load_late():
@@ -379,7 +381,10 @@ def tile_box_head_region_features_h1_kernel(
 
         if B1_AT < 0:
             spread_b1()
-        x_sort(runs[0])
+        for b, plane in zip(runs[0], [None, s1_parts[-1], s2_raw, None]):
+            x_sort([b])
+            if plane is not None:
+                clear(plane)
         load_late()
         for k, (run, todo) in enumerate(zip(runs, passes)):
             nxt = runs[k + 1] if k + 1 < len(runs) else []

@@ -10,6 +10,7 @@ F32 = mybir.dt.float32
 BF16 = mybir.dt.bfloat16
 U32 = mybir.dt.uint32
 I32 = mybir.dt.int32
+U16 = mybir.dt.uint16
 U8 = mybir.dt.uint8
 FP8X4 = mybir.dt.float8_e4m3fn_x4
 FP4X4 = mybir.dt.float4_e2m1fn_x4
@@ -19,28 +20,13 @@ ACT = mybir.ActivationFunctionType
 P = 128
 GROUP = 512
 TILES = R // P
+GROUPS = D // GROUP
+CHUNKS = GROUPS // 2
 SCALAR, VECTOR = "scalar", "vector"
 
-U16 = mybir.dt.uint16
-GROUPS = D // GROUP
-SINGLES = 0
-ENDS = (4, 8, 12, 16)
-PASS_ENDS = (2, 6, 10, 16)
-WARM = (3, 0, 0, 1)
-B1_LOAD = -1
-OPEN = 6
-ON_V = ((0, 0), (0, 2))
-B1_V = 0
-W_AT = (3, 7, 11, 15)
-S_AT = (3, 3, 15)
-PARTS = [(0, 0, 2), (0, 2, 6), (0, 6, 8), (1, 0, 8)]
-B1_AT = -1
-EARLY = 0
-VLEAD = 0
-POOL = (1,)
-WHOLE = ()
-X_SPANS = ((0, 2), (2, 2), (4, 2), (6, 2))
-LATE = "a s1 b c s2 d w v"
+LAG = 2
+AHEAD = 6
+SCALE_PARTS = [(0, 0, 2), (0, 2, 6), (0, 6, 8), (1, 0, 8)]
 
 
 def tile_box_head_region_features_h1_kernel(
@@ -67,18 +53,14 @@ def tile_box_head_region_features_h1_kernel(
         ident = tile("ident", [P, P], F32)
         vec = {key: tile("vec_" + key, [P, 2, 4], BF16) for key in ("b1", "b2", "shift", "gain")}
         b1_rows = tile("b1_rows", [P, F], BF16)
-        spans = [(g, 2) for g in range(0, GROUPS, 2)]
-        blocks = [(rt, g, n) for g, n in X_SPANS for rt in range(TILES)]
-        x_raw = {b: tile("x_raw%d_%d" % b[:2], [P, GROUP * b[2]], BF16) for b in blocks}
-        x_sorted = {b: tile("x_sorted%d_%d" % b[:2], [P, GROUP * b[2] // 2], F32) for b in blocks}
-        x_codes = {b: tile("x_codes%d_%d" % b[:2], [P, P * b[2]], U32) for b in blocks}
-        x_scales = {b: tile("x_scales%d_%d" % b[:2], [P, P * b[2]], U8) for b in blocks}
-        w1_parts = [(h, g, n) for h in range(2) for g, n in spans]
-        w1_tiles = {part: tile("w1_%d_%d" % part[:2], [P, part[2], 2 * GROUP], U8) for part in w1_parts}
-        w1 = {(h, g + j): w1_tiles[h, g, n][:, j, :] for h, g, n in w1_parts for j in range(n)}
-        scale_parts = PARTS
-        s1_parts = [tile("s1_%d" % i, [P, g1 - g0, GROUP], U8) for i, (h, g0, g1) in enumerate(scale_parts)]
-        s1 = {(h, g): s1_parts[i][:, g - g0, :] for i, (h, g0, g1) in enumerate(scale_parts) for g in range(g0, g1)}
+        blocks = [(rt, c) for c in range(CHUNKS) for rt in range(TILES)]
+        x_raw = {b: tile("x_raw%d_%d" % b, [P, 2 * GROUP], BF16) for b in blocks}
+        x_sorted = {b: tile("x_sorted%d_%d" % b, [P, GROUP], F32) for b in blocks}
+        x_codes = {b: tile("x_codes%d_%d" % b, [P, 2 * P], U32) for b in blocks}
+        x_scales = {b: tile("x_scales%d_%d" % b, [P, 2 * P], U8) for b in blocks}
+        w1 = {(h, c): tile("w1_%d_%d" % (h, c), [P, 2, 2 * GROUP], U8) for h in range(2) for c in range(CHUNKS)}
+        s1_parts = [tile("s1_%d" % i, [P, g1 - g0, GROUP], U8) for i, (h, g0, g1) in enumerate(SCALE_PARTS)]
+        s1 = {(h, g): s1_parts[i][:, g - g0, :] for i, (h, g0, g1) in enumerate(SCALE_PARTS) for g in range(g0, g1)}
         w2_raw = [tile("w2_raw%d" % h, [P, 2 * N], U8) for h in range(2)]
         s2_raw = tile("s2_raw", [P, 2, N], U8)
         w2 = tile("w2", [P, 2, 2 * N], U8)
@@ -111,16 +93,16 @@ def tile_box_head_region_features_h1_kernel(
         def regions(rt, count=1):
             return slice(P * rt, P * (rt + count))
 
-        def load_vec(queue, key, src):
-            queue.dma_start(out=vec[key][:], in_=src.rearrange("(g p t) -> p g t", g=2, t=4))
+        def load_vec(key, src):
+            nc.sync.dma_start(out=vec[key][:], in_=src.rearrange("(g p t) -> p g t", g=2, t=4))
 
         def load_x(b):
-            rt, g, n = b
-            nc.sync.dma_start(out=x_raw[b][:], in_=x[regions(rt), GROUP * g : GROUP * (g + n)])
+            rt, c = b
+            nc.sync.dma_start(out=x_raw[b][:], in_=x[regions(rt), 2 * GROUP * c : 2 * GROUP * (c + 1)])
 
-        def load_w1(h, g, n):
-            src = w1_hbm[g : g + n, :, 256 * h : 256 * (h + 1)]
-            nc.sync.dma_start(out=w1_tiles[h, g, n][:].bitcast(I32), in_=src.rearrange("g p n -> p g n"))
+        def load_w1(h, c):
+            src = w1_hbm[2 * c : 2 * c + 2, :, 256 * h : 256 * (h + 1)]
+            nc.sync.dma_start(out=w1[h, c][:].bitcast(I32), in_=src.rearrange("g p n -> p g n"))
 
         def load_w2(h):
             nc.sync.dma_start(out=w2_raw[h][:].bitcast(I32), in_=w2_hbm[h])
@@ -130,64 +112,62 @@ def tile_box_head_region_features_h1_kernel(
                 queue.dma_start(out=plane[r:P:32].bitcast(I32), in_=src[:, r:16:4, :].rearrange("g q n -> q g n"))
 
         def load_s1(queue, part):
-            h, g0, g1 = scale_parts[part]
+            h, g0, g1 = SCALE_PARTS[part]
             load_scale_rows(queue, s1_parts[part], s1_hbm[g0:g1, :, 128 * h : 128 * (h + 1)])
 
-        def clear(t):
-            nc.vector.memset(t[:].bitcast(I32), 0)
+        def clear(plane):
+            nc.vector.memset(plane[:].bitcast(I32), 0)
 
         def spread_b1():
             bank = take("b1")
             words = vec["b1"][:].rearrange("p g t -> p (g t)").bitcast(F32)
             for j in range(4):
                 nc.tensor.transpose(bank[:, P * j : P * (j + 1)], words[:, j : j + 1].to_broadcast([P, P]), ident[:])
-            (nc.vector.tensor_copy if B1_V else nc.scalar.copy)(out=b1_rows[:].bitcast(F32), in_=bank[:])
+            nc.scalar.copy(out=b1_rows[:].bitcast(F32), in_=bank[:])
             give_back("b1")
 
-        def x_sort(run, copy=nc.vector.tensor_copy):
+        def x_sort(run):
             for b in run:
-                copy(
-                    out=x_sorted[b][:].rearrange("r (g u m) -> r g u m", g=b[2], u=2),
-                    in_=x_raw[b][:].bitcast(F32).rearrange("r (g m u) -> r g u m", g=b[2], u=2),
+                nc.vector.tensor_copy(
+                    out=x_sorted[b][:].rearrange("r (g u m) -> r g u m", g=2, u=2),
+                    in_=x_raw[b][:].bitcast(F32).rearrange("r (g m u) -> r g u m", g=2, u=2),
                 )
 
         def x_turn(run):
             for b in run:
-                for c in range(b[2] // 2):
-                    bank = take(("x", b))
-                    for j in range(4):
-                        words = x_sorted[b][:, GROUP * c + P * j : GROUP * c + P * (j + 1)]
-                        nc.tensor.transpose(bank[:, P * j : P * (j + 1)], words, ident[:])
-                    nc.scalar.copy(
-                        out=x_raw[b][:].bitcast(F32)[:, GROUP * c : GROUP * (c + 1)].rearrange("p (g r u) -> p g r u", g=2, u=2),
-                        in_=bank[:].rearrange("p (g u r) -> p g r u", g=2, u=2),
-                    )
-                    give_back(("x", b))
+                bank = take(("x", b))
+                for j in range(4):
+                    nc.tensor.transpose(bank[:, P * j : P * (j + 1)], x_sorted[b][:, P * j : P * (j + 1)], ident[:])
+                nc.scalar.copy(
+                    out=x_raw[b][:].bitcast(F32).rearrange("p (g r u) -> p g r u", g=2, u=2),
+                    in_=bank[:].rearrange("p (g u r) -> p g r u", g=2, u=2),
+                )
+                give_back(("x", b))
 
         def x_quant(run):
             for b in run:
                 nc.vector.quantize_mx(out=x_codes[b][:].bitcast(FP8X4), scales=x_scales[b][:], in_=x_raw[b][:])
 
-        def mm1(rt, h, g0, g1):
-            bank = take(("h", rt, h)) if g0 == 0 else bank_of(("h", rt, h))
-            for g in range(g0, g1):
-                b = [b for b in blocks if b[0] == rt and b[1] <= g < b[1] + b[2]][0]
-                cols = slice(P * (g - b[1]), P * (g - b[1] + 1))
-                nc.tensor.matmul_mx(
-                    out=bank[:],
-                    lhsT=x_codes[b][:, cols].bitcast(FP8X4),
-                    lhsT_scale=x_scales[b][:, cols],
-                    rhs=w1[h, g].bitcast(FP4X4),
-                    rhs_scale=s1[h, g],
-                    start=(g == 0),
-                    stop=(g == GROUPS - 1),
-                )
+        def mm1(rt, h, chunks):
+            for c in chunks:
+                bank = take(("h", rt, h)) if c == 0 else bank_of(("h", rt, h))
+                for j in range(2):
+                    g = 2 * c + j
+                    nc.tensor.matmul_mx(
+                        out=bank[:],
+                        lhsT=x_codes[rt, c][:, P * j : P * (j + 1)].bitcast(FP8X4),
+                        lhsT_scale=x_scales[rt, c][:, P * j : P * (j + 1)],
+                        rhs=w1[h, c][:, j, :].bitcast(FP4X4),
+                        rhs_scale=s1[h, g],
+                        start=(g == 0),
+                        stop=(g == GROUPS - 1),
+                    )
 
-        def h_add(rt, h, parts=1):
+        def h_add(rt, h, parts=(slice(0, 2),)):
             dst = h_biased[rt, h][:].rearrange("r (u m e) -> r u m e", u=2, e=2)
             src = bank_of(("h", rt, h))[:].rearrange("r (m u e) -> r u m e", u=2, e=2)
             bias = b1_rows[:, GROUP * h : GROUP * (h + 1)].rearrange("r (u m e) -> r u m e", u=2, e=2)
-            for u in [slice(0, 2)] if parts == 1 else [0, 1]:
+            for u in parts:
                 nc.vector.tensor_tensor(out=dst[:, u], in0=src[:, u], in1=bias[:, u], op=ALU.add)
             give_back(("h", rt, h))
 
@@ -228,36 +208,10 @@ def tile_box_head_region_features_h1_kernel(
                 in_=s2_raw[:, h, :].rearrange("p (g m t) -> p g t m", g=2, t=4),
             )
 
-        def stage2(rt, count, g, slices, engine=SCALAR):
-            bank = take(("z", rt, g, slices))
-            width = P * count
-            for j, t in enumerate(slices):
-                col = GROUP * g + P * t
-                for i in range(count):
-                    for h in range(2):
-                        nc.tensor.matmul_mx(
-                            out=bank[:, width * j + P * i : width * j + P * (i + 1)],
-                            lhsT=w2[:, h, 2 * col : 2 * (col + P)].bitcast(FP4X4),
-                            lhsT_scale=s2[:, h, col : col + P],
-                            rhs=h_codes[h][:, regions(rt + i)].bitcast(FP8X4),
-                            rhs_scale=h_scales[h][:, regions(rt + i)],
-                            start=(h == 0),
-                            stop=(h == 1),
-                        )
-            for j, t in enumerate(slices):
-                dst, src = a_t[g][:, t, regions(rt, count)], bank[:, width * j : width * (j + 1)]
-                bias = vec["b2"][:, g, t : t + 1]
-                if engine == SCALAR:
-                    nc.scalar.activation(out=dst, in_=src, func=ACT.Relu, bias=bias)
-                else:
-                    nc.vector.tensor_scalar(out=dst, in0=src, scalar1=bias, scalar2=0.0, op0=ALU.add, op1=ALU.max)
-            give_back(("z", rt, g, slices))
-
-        def z_pass(rt, g, t, h):
-            bank = take(("z", rt, g, t)) if h == 0 else bank_of(("z", rt, g, t))
+        def mm2(out, rt, g, t, h):
             col = GROUP * g + P * t
             nc.tensor.matmul_mx(
-                out=bank[:, 0:P],
+                out=out,
                 lhsT=w2[:, h, 2 * col : 2 * (col + P)].bitcast(FP4X4),
                 lhsT_scale=s2[:, h, col : col + P],
                 rhs=h_codes[h][:, regions(rt)].bitcast(FP8X4),
@@ -266,13 +220,31 @@ def tile_box_head_region_features_h1_kernel(
                 stop=(h == 1),
             )
 
-        def z_relu(rt, g, t, engine=SCALAR):
-            dst, src = a_t[g][:, t, regions(rt)], bank_of(("z", rt, g, t))[:, 0:P]
-            bias = vec["b2"][:, g, t : t + 1]
+        def a_relu(src, rt, count, g, t, engine):
+            dst, bias = a_t[g][:, t, regions(rt, count)], vec["b2"][:, g, t : t + 1]
             if engine == SCALAR:
                 nc.scalar.activation(out=dst, in_=src, func=ACT.Relu, bias=bias)
             else:
                 nc.vector.tensor_scalar(out=dst, in0=src, scalar1=bias, scalar2=0.0, op0=ALU.add, op1=ALU.max)
+
+        def stage2(rt, count, g, slices):
+            bank = take(("z", rt, g, slices))
+            width = P * count
+            for j, t in enumerate(slices):
+                for i in range(count):
+                    for h in range(2):
+                        mm2(bank[:, width * j + P * i : width * j + P * (i + 1)], rt + i, g, t, h)
+            for j, t in enumerate(slices):
+                a_relu(bank[:, width * j : width * (j + 1)], rt, count, g, t, SCALAR)
+            give_back(("z", rt, g, slices))
+
+        def slice_open(rt, g, t):
+            mm2(take(("z", rt, g, t))[:, 0:P], rt, g, t, 0)
+
+        def slice_close(rt, g, t, engine):
+            sums = bank_of(("z", rt, g, t))[:, 0:P]
+            mm2(sums, rt, g, t, 1)
+            a_relu(sums, rt, 1, g, t, engine)
             give_back(("z", rt, g, t))
 
         def y_affine(rt, count, g, slices):
@@ -299,139 +271,117 @@ def tile_box_head_region_features_h1_kernel(
                 in_=y_bf16[g][:, regions(rt, count), :].rearrange("p r t -> p (r t)"),
             )
 
-        def y_turn(rt, g, copy=nc.scalar.copy):
+        def y_turn(rt, g):
             bank = take(("y", rt, g))
             for t in range(4):
                 nc.tensor.transpose(bank[:, P * t : P * (t + 1)], y_t[g][:, t, regions(rt)], ident[:])
-            copy(
+            nc.scalar.copy(
                 out=y_rows[rt][:, GROUP * g : GROUP * (g + 1)].rearrange("r (p t) -> r p t", t=4),
                 in_=bank[:].rearrange("r (t p) -> r p t", t=4),
             )
             give_back(("y", rt, g))
 
-        def y_leave_halves(rt, g):
-            bank = take(("y", rt, g))
-            for t in range(4):
-                nc.tensor.transpose(bank[:, P * t : P * (t + 1)], y_t[g][:, t, regions(rt)], ident[:])
-            for j in range(2):
-                cols = slice(GROUP * g + 256 * j, GROUP * g + 256 * (j + 1))
-                nc.scalar.copy(
-                    out=y_rows[rt][:, cols].rearrange("r (p t) -> r p t", t=4),
-                    in_=bank[:].rearrange("r (t p) -> r p t", t=4)[:, 64 * j : 64 * (j + 1), :],
-                )
-                nc.sync.dma_start(out=out_0[regions(rt), cols], in_=y_rows[rt][:, cols])
-            give_back(("y", rt, g))
-
         def store_y(rt, g):
-            if rt in WHOLE:
-                if g == 1:
-                    nc.sync.dma_start(out=out_0[regions(rt), :], in_=y_rows[rt][:])
-                return
             cols = slice(GROUP * g, GROUP * (g + 1))
             nc.sync.dma_start(out=out_0[regions(rt), cols], in_=y_rows[rt][:, cols])
 
-        def y_leave(rt, g, copy=nc.scalar.copy):
-            y_turn(rt, g, copy)
+        def y_leave(rt, g):
+            y_turn(rt, g)
             store_y(rt, g)
 
-        def store_codes(rt, count, groups=slice(0, 2)):
+        def store_codes(rt, count):
             cols = regions(rt, count)
-            nc.sync.dma_start(out=codes_hbm[:, groups, cols], in_=y_codes[:, groups, cols].bitcast(I32))
+            nc.sync.dma_start(out=codes_hbm[:, :, cols], in_=y_codes[:, :, cols].bitcast(I32))
 
-        def store_scales(queue):
+        def store_scales():
             for r in range(4):
                 dst = scales_hbm[:, r:16:4, :].rearrange("g q n -> q g n")
-                queue.dma_start(out=dst, in_=y_scales[r:P:32].bitcast(I32))
+                nc.scalar.dma_start(out=dst, in_=y_scales[r:P:32].bitcast(I32))
 
+        first_rows, middle_rows, last_rows, second_half_rows = range(len(SCALE_PARTS))
         make_identity(nc, ident[:])
-        for plane in s1_parts[:-1]:
-            clear(plane)
-        for j in POOL:
-            load_s1(nc.gpsimd, j)
+        for part in (first_rows, middle_rows, last_rows):
+            clear(s1_parts[part])
+        load_s1(nc.gpsimd, middle_rows)
 
-        runs = [blocks[a:b] for a, b in zip((0,) + ENDS, ENDS)]
-        passes = [blocks[a:b] for a, b in zip((0,) + PASS_ENDS, PASS_ENDS)]
-
-        if B1_LOAD < 0:
-            load_vec(nc.sync, "b1", b1)
-        for i, b in enumerate(blocks):
-            load_x(b)
-            if i == B1_LOAD:
-                load_vec(nc.sync, "b1", b1)
-            for j, at in enumerate(W_AT):
-                if at == i:
-                    load_w1(*w1_parts[j])
-            for j, at in enumerate(S_AT):
-                if at == i and j not in POOL:
-                    load_s1(nc.sync, j)
-
-        def load_late():
-            for key in LATE.split():
-                if key == "s2":
-                    load_scale_rows(nc.sync, s2_raw, s2_hbm)
-                elif key == "s1":
-                    load_s1(nc.sync, len(PARTS) - 1)
-                elif key in "abcd":
-                    load_w1(1, *spans["abcd".index(key)])
-                else:
-                    load_w2("wv".index(key))
-            load_vec(nc.sync, "b2", b2)
-            load_vec(nc.sync, "shift", shift)
-            load_vec(nc.sync, "gain", gain)
-
-        if B1_AT < 0:
-            spread_b1()
-        for b, plane in zip(runs[0], [None, s1_parts[-1], s2_raw, None]):
-            x_sort([b])
-            if plane is not None:
-                clear(plane)
-        load_late()
-        for k, (run, todo) in enumerate(zip(runs, passes)):
-            nxt = runs[k + 1] if k + 1 < len(runs) else []
+        runs = [blocks[TILES * c : TILES * (c + 1)] for c in range(CHUNKS)]
+        load_vec("b1", b1)
+        for c, run in enumerate(runs):
             for b in run:
-                x_turn([b])
-                if B1_AT >= 0 and b == blocks[B1_AT]:
-                    spread_b1()
-            x_quant(todo)
-            x_sort(nxt)
-            for rt, g, n in todo:
-                mm1(rt, 0, g, g + n)
-        low, high = (0, 1), (2, 3)
-        pairs = [(g, slices) for g in range(2) for slices in (low, high)]
+                load_x(b)
+            load_w1(0, c)
+            if c == 0:
+                load_s1(nc.sync, first_rows)
+        load_s1(nc.sync, last_rows)
+
+        spread_b1()
+        x_sort(runs[0][:2])
+        clear(s1_parts[second_half_rows])
+        x_sort(runs[0][2:3])
+        clear(s2_raw)
+        x_sort(runs[0][3:])
+
+        load_w1(1, 0)
+        load_s1(nc.sync, second_half_rows)
+        load_w1(1, 1)
+        load_scale_rows(nc.sync, s2_raw, s2_hbm)
+        load_w1(1, 2)
+        load_w1(1, 3)
+        for h in range(2):
+            load_w2(h)
+        load_vec("b2", b2)
+        load_vec("shift", shift)
+        load_vec("gain", gain)
+
+        done = 0
+        for c, run in enumerate(runs):
+            last = c == CHUNKS - 1
+            x_turn(run)
+            ready = blocks[done : len(blocks) if last else TILES * (c + 1) - LAG]
+            done += len(ready)
+            x_quant(ready)
+            if not last:
+                x_sort(runs[c + 1])
+            for rt, chunk in ready:
+                mm1(rt, 0, [chunk])
+
         for rt in range(TILES):
             h_add(rt, 0)
-        for g in (0, 2):
+        for c in (0, 1):
             for rt in range(2):
-                mm1(rt, 1, g, g + 2)
+                mm1(rt, 1, [c])
         for rt in (0, 2):
             h_turn(rt, 2, 0)
         for rt in (0, 2):
             h_relu(rt, 2, 0, SCALAR)
         for h in range(2):
             w2_sort_scales(h)
-        for g in (4, 6):
+        for c in (2, 3):
             for rt in range(2):
-                mm1(rt, 1, g, g + 2)
+                mm1(rt, 1, [c])
         for h in range(2):
             w2_sort_words(h)
         h_quant(0, 2, 0)
+
         for rt in range(2):
             h_add(rt, 1)
-        mm1(2, 1, 0, 4)
+        mm1(2, 1, [0, 1])
         h_quant(2, 2, 0)
         for rt in range(2):
             h_turn(rt, 1, 1)
         h_relu(0, 1, 1, SCALAR)
         h_relu(1, 1, 1, VECTOR)
-        mm1(2, 1, 4, 8)
+        mm1(2, 1, [2, 3])
         h_quant(0, 2, 1)
-        mm1(3, 1, 0, 2)
+        mm1(3, 1, [0])
         h_add(2, 1)
 
+        low, high = (0, 1), (2, 3)
+        pairs = [(g, slices) for g in range(2) for slices in (low, high)]
         for g, slices in pairs:
             stage2(0, 2, g, slices)
             y_affine(0, 2, g, slices)
-        mm1(3, 1, 2, 4)
+        mm1(3, 1, [1])
         h_turn(2, 1, 1)
         h_relu(2, 1, 1, SCALAR)
         for rt, g in [(0, 0), (1, 0), (0, 1)]:
@@ -440,8 +390,8 @@ def tile_box_head_region_features_h1_kernel(
         h_quant(2, 1, 1)
         y_round(0, 2, 1)
         y_quant(0, 2, 0)
-        mm1(3, 1, 4, 8)
-        h_add(3, 1, 2)
+        mm1(3, 1, [2, 3])
+        h_add(3, 1, (0, 1))
         y_quant(0, 2, 1)
         store_codes(0, 2)
 
@@ -457,14 +407,13 @@ def tile_box_head_region_features_h1_kernel(
         y_affine(2, 1, 1, high)
         y_round(2, 1, 0)
 
-        order = [(g, t) for g in range(2) for t in range(4)]
-        for g, t in order[:OPEN]:
-            z_pass(3, g, t, 0)
-        for g, t in order:
-            if (g, t) not in order[:OPEN]:
-                z_pass(3, g, t, 0)
-            z_pass(3, g, t, 1)
-            z_relu(3, g, t, VECTOR if (g, t) in ON_V else SCALAR)
+        out_slices = [(g, t) for g in range(2) for t in range(4)]
+        for g, t in out_slices[:AHEAD]:
+            slice_open(3, g, t)
+        for i, (g, t) in enumerate(out_slices):
+            if i >= AHEAD:
+                slice_open(3, g, t)
+            slice_close(3, g, t, VECTOR if g == 0 and t % 2 == 1 else SCALAR)
         y_quant(2, 1, 0)
         y_round(2, 1, 1)
         y_affine(3, 1, 0, low + high)
@@ -480,4 +429,4 @@ def tile_box_head_region_features_h1_kernel(
             y_quant(3, 1, g)
         store_codes(3, 1)
         store_y(3, 1)
-        store_scales(nc.scalar)
+        store_scales()

@@ -305,13 +305,13 @@ def tile_box_head_region_features_h1_kernel(
         load_s1(nc.gpsimd, middle_rows)
 
         runs = [blocks[TILES * c : TILES * (c + 1)] for c in range(CHUNKS)]
-        load_vec("b1", b1)
+        nc.scalar.dma_start(out=vec["b1"][:], in_=b1.rearrange("(g p t) -> p g t", g=2, t=4))
         for c, run in enumerate(runs):
             for b in run:
                 load_x(b)
             load_w1(0, c)
             if c == 0:
-                load_s1(nc.sync, first_rows)
+                load_s1(nc.scalar, first_rows)
         load_s1(nc.sync, last_rows)
 
         spread_b1()

@@ -26,7 +26,7 @@ SCALAR, VECTOR = "scalar", "vector"
 
 LAG = 2
 AHEAD = 6
-SCALE_PARTS = [(0, 0, 2), (0, 2, 6), (0, 6, 8), (1, 0, 8)]
+SCALE_PARTS = [(0, 0, 2), (0, 2, 8), (1, 0, 8)]
 
 
 def tile_box_head_region_features_h1_kernel(
@@ -298,9 +298,9 @@ def tile_box_head_region_features_h1_kernel(
                 dst = scales_hbm[:, r:16:4, :].rearrange("g q n -> q g n")
                 nc.scalar.dma_start(out=dst, in_=y_scales[r:P:32].bitcast(I32))
 
-        first_rows, middle_rows, last_rows, second_half_rows = range(len(SCALE_PARTS))
+        first_rows, middle_rows, second_half_rows = range(len(SCALE_PARTS))
         make_identity(nc, ident[:])
-        for part in (first_rows, middle_rows, last_rows):
+        for part in (first_rows, middle_rows):
             clear(s1_parts[part])
         load_s1(nc.gpsimd, middle_rows)
 
@@ -312,7 +312,6 @@ def tile_box_head_region_features_h1_kernel(
             load_w1(0, c)
             if c == 0:
                 load_s1(nc.scalar, first_rows)
-        load_s1(nc.sync, last_rows)
 
         spread_b1()
         x_sort(runs[0][:2])
@@ -324,9 +323,9 @@ def tile_box_head_region_features_h1_kernel(
         load_w1(1, 0)
         load_s1(nc.sync, second_half_rows)
         load_w1(1, 1)
-        load_scale_rows(nc.sync, s2_raw, s2_hbm)
         load_w1(1, 2)
         load_w1(1, 3)
+        load_scale_rows(nc.sync, s2_raw, s2_hbm)
         for h in range(2):
             load_w2(h)
         load_vec("b2", b2)
@@ -350,31 +349,29 @@ def tile_box_head_region_features_h1_kernel(
         for c in (0, 1):
             for rt in range(2):
                 mm1(rt, 1, [c])
-        for rt in (0, 2):
-            h_turn(rt, 2, 0)
-        for rt in (0, 2):
-            h_relu(rt, 2, 0, SCALAR)
         for h in range(2):
             w2_sort_scales(h)
         for c in (2, 3):
             for rt in range(2):
                 mm1(rt, 1, [c])
-        for h in range(2):
-            w2_sort_words(h)
-        h_quant(0, 2, 0)
+        w2_sort_words(0)
 
         for rt in range(2):
             h_add(rt, 1)
-        mm1(2, 1, [0, 1])
-        h_quant(2, 2, 0)
-        for rt in range(2):
-            h_turn(rt, 1, 1)
-        h_relu(0, 1, 1, SCALAR)
-        h_relu(1, 1, 1, VECTOR)
-        mm1(2, 1, [2, 3])
+        w2_sort_words(1)
+        mm1(2, 1, [0])
+        h_turn(0, 2, 0)
+        h_relu(0, 2, 0, SCALAR)
+        h_turn(2, 2, 0)
+        h_turn(0, 2, 1)
+        h_relu(0, 2, 1, VECTOR)
+        h_relu(2, 2, 0, SCALAR)
+        mm1(2, 1, [1, 2, 3])
+        h_quant(0, 2, 0)
         h_quant(0, 2, 1)
         mm1(3, 1, [0])
         h_add(2, 1)
+        h_quant(2, 2, 0)
 
         low, high = (0, 1), (2, 3)
         pairs = [(g, slices) for g in range(2) for slices in (low, high)]
@@ -406,6 +403,7 @@ def tile_box_head_region_features_h1_kernel(
         h_quant(3, 1, 1)
         y_affine(2, 1, 1, high)
         y_round(2, 1, 0)
+        y_round(2, 1, 1)
 
         out_slices = [(g, t) for g in range(2) for t in range(4)]
         for g, t in out_slices[:AHEAD]:
@@ -415,10 +413,9 @@ def tile_box_head_region_features_h1_kernel(
                 slice_open(3, g, t)
             slice_close(3, g, t, VECTOR if g == 0 and t % 2 == 1 else SCALAR)
         y_quant(2, 1, 0)
-        y_round(2, 1, 1)
-        y_affine(3, 1, 0, low + high)
         y_quant(2, 1, 1)
         store_codes(2, 1)
+        y_affine(3, 1, 0, low + high)
         y_affine(3, 1, 1, low + high)
         y_leave(2, 1)
         y_leave(3, 0)

@@ -26,7 +26,7 @@ SCALAR, VECTOR = "scalar", "vector"
 
 LAG = 2
 AHEAD = 6
-SCALE_PARTS = [(0, 0, 2), (0, 2, 8), (1, 0, 8)]
+SCALE_PARTS = [(0, 0, 2), (0, 2, 6), (0, 6, 8), (1, 0, 8)]
 
 
 def tile_box_head_region_features_h1_kernel(
@@ -54,7 +54,13 @@ def tile_box_head_region_features_h1_kernel(
         vec = {key: tile("vec_" + key, [P, 2, 4], BF16) for key in ("b1", "b2", "shift", "gain")}
         b1_rows = tile("b1_rows", [P, F], BF16)
         blocks = [(rt, c) for c in range(CHUNKS) for rt in range(TILES)]
-        x_raw = {b: tile("x_raw%d_%d" % b, [P, 2 * GROUP], BF16) for b in blocks}
+        x_pair = {c: tile("x_pair%d" % c, [P, 4 * GROUP], BF16) for c in (1,)}
+        x_raw = {}
+        for rt, c in blocks:
+            if rt < 2 and c in x_pair:
+                x_raw[rt, c] = x_pair[c][:, 2 * GROUP * rt : 2 * GROUP * (rt + 1)]
+            else:
+                x_raw[rt, c] = tile("x_raw%d_%d" % (rt, c), [P, 2 * GROUP], BF16)
         x_sorted = {b: tile("x_sorted%d_%d" % b, [P, GROUP], F32) for b in blocks}
         x_codes = {b: tile("x_codes%d_%d" % b, [P, 2 * P], U32) for b in blocks}
         x_scales = {b: tile("x_scales%d_%d" % b, [P, 2 * P], U8) for b in blocks}
@@ -98,7 +104,12 @@ def tile_box_head_region_features_h1_kernel(
 
         def load_x(b):
             rt, c = b
-            nc.sync.dma_start(out=x_raw[b][:], in_=x[regions(rt), 2 * GROUP * c : 2 * GROUP * (c + 1)])
+            cols = slice(2 * GROUP * c, 2 * GROUP * (c + 1))
+            if rt >= 2 or c not in x_pair:
+                nc.sync.dma_start(out=x_raw[b][:], in_=x[regions(rt), cols])
+            elif rt == 0:
+                src = x[regions(0, 2), cols].rearrange("(a r) n -> r a n", a=2)
+                nc.sync.dma_start(out=x_pair[c][:].rearrange("r (a n) -> r a n", a=2), in_=src)
 
         def load_w1(h, c):
             src = w1_hbm[2 * c : 2 * c + 2, :, 256 * h : 256 * (h + 1)]
@@ -281,26 +292,26 @@ def tile_box_head_region_features_h1_kernel(
             )
             give_back(("y", rt, g))
 
-        def store_y(rt, g):
+        def store_y(rt, g, queue=nc.sync):
             cols = slice(GROUP * g, GROUP * (g + 1))
-            nc.sync.dma_start(out=out_0[regions(rt), cols], in_=y_rows[rt][:, cols])
+            queue.dma_start(out=out_0[regions(rt), cols], in_=y_rows[rt][:, cols])
 
         def y_leave(rt, g):
             y_turn(rt, g)
             store_y(rt, g)
 
-        def store_codes(rt, count):
+        def store_codes(rt, count, queue=nc.sync):
             cols = regions(rt, count)
-            nc.sync.dma_start(out=codes_hbm[:, :, cols], in_=y_codes[:, :, cols].bitcast(I32))
+            queue.dma_start(out=codes_hbm[:, :, cols], in_=y_codes[:, :, cols].bitcast(I32))
 
         def store_scales():
             for r in range(4):
                 dst = scales_hbm[:, r:16:4, :].rearrange("g q n -> q g n")
                 nc.scalar.dma_start(out=dst, in_=y_scales[r:P:32].bitcast(I32))
 
-        first_rows, middle_rows, second_half_rows = range(len(SCALE_PARTS))
+        first_rows, middle_rows, last_rows, second_half_rows = range(len(SCALE_PARTS))
         make_identity(nc, ident[:])
-        for part in (first_rows, middle_rows):
+        for part in (first_rows, middle_rows, last_rows):
             clear(s1_parts[part])
         load_s1(nc.gpsimd, middle_rows)
 
@@ -312,6 +323,7 @@ def tile_box_head_region_features_h1_kernel(
             load_w1(0, c)
             if c == 0:
                 load_s1(nc.scalar, first_rows)
+        load_s1(nc.sync, last_rows)
 
         spread_b1()
         x_sort(runs[0][:2])
@@ -324,8 +336,8 @@ def tile_box_head_region_features_h1_kernel(
         load_s1(nc.sync, second_half_rows)
         load_w1(1, 1)
         load_w1(1, 2)
-        load_w1(1, 3)
         load_scale_rows(nc.sync, s2_raw, s2_hbm)
+        load_w1(1, 3)
         for h in range(2):
             load_w2(h)
         load_vec("b2", b2)
@@ -354,11 +366,11 @@ def tile_box_head_region_features_h1_kernel(
         for c in (2, 3):
             for rt in range(2):
                 mm1(rt, 1, [c])
-        w2_sort_words(0)
 
         for rt in range(2):
             h_add(rt, 1)
-        w2_sort_words(1)
+        for h in range(2):
+            w2_sort_words(h)
         mm1(2, 1, [0])
         h_turn(0, 2, 0)
         h_relu(0, 2, 0, SCALAR)
@@ -424,6 +436,6 @@ def tile_box_head_region_features_h1_kernel(
         y_turn(3, 1)
         for g in range(2):
             y_quant(3, 1, g)
-        store_codes(3, 1)
         store_y(3, 1)
+        store_codes(3, 1, nc.scalar)
         store_scales()

@@ -23,10 +23,8 @@ TILES = R // P
 GROUPS = D // GROUP
 CHUNKS = GROUPS // 2
 SCALAR, VECTOR = "scalar", "vector"
-
-LAG = 2
-AHEAD = 6
-SCALE_PARTS = [(0, 0, 2), (0, 2, 6), (0, 6, 8), (1, 0, 8)]
+W1_PARTS = [(2 * c, 2 * c + 2, h, h + 1) for h in range(2) for c in range(CHUNKS)]
+S1_PARTS = [(0, 2, 0, 1), (2, 6, 0, 1), (6, 8, 0, 1), (0, 8, 1, 2)]
 
 
 def tile_box_head_region_features_h1_kernel(
@@ -48,25 +46,23 @@ def tile_box_head_region_features_h1_kernel(
             return sb.tile(shape, dtype, name=name, align_bytes=64)
 
         halves = [(rt, h) for rt in range(TILES) for h in range(2)]
-
+        blocks = [(rt, c) for rt in range(TILES) for c in range(CHUNKS)]
         banks = [ps.tile([P, GROUP], F32, name="bank%d" % i) for i in range(8)]
         ident = tile("ident", [P, P], F32)
         vec = {key: tile("vec_" + key, [P, 2, 4], BF16) for key in ("b1", "b2", "shift", "gain")}
         b1_rows = tile("b1_rows", [P, F], BF16)
-        blocks = [(rt, c) for c in range(CHUNKS) for rt in range(TILES)]
-        x_pair = {c: tile("x_pair%d" % c, [P, 4 * GROUP], BF16) for c in (1,)}
-        x_raw = {}
-        for rt, c in blocks:
-            if rt < 2 and c in x_pair:
-                x_raw[rt, c] = x_pair[c][:, 2 * GROUP * rt : 2 * GROUP * (rt + 1)]
-            else:
-                x_raw[rt, c] = tile("x_raw%d_%d" % (rt, c), [P, 2 * GROUP], BF16)
+        x_raw = {b: tile("x_raw%d_%d" % b, [P, 2 * GROUP], BF16) for b in blocks}
         x_sorted = {b: tile("x_sorted%d_%d" % b, [P, GROUP], F32) for b in blocks}
         x_codes = {b: tile("x_codes%d_%d" % b, [P, 2 * P], U32) for b in blocks}
         x_scales = {b: tile("x_scales%d_%d" % b, [P, 2 * P], U8) for b in blocks}
-        w1 = {(h, c): tile("w1_%d_%d" % (h, c), [P, 2, 2 * GROUP], U8) for h in range(2) for c in range(CHUNKS)}
-        s1_parts = [tile("s1_%d" % i, [P, g1 - g0, GROUP], U8) for i, (h, g0, g1) in enumerate(SCALE_PARTS)]
-        s1 = {(h, g): s1_parts[i][:, g - g0, :] for i, (h, g0, g1) in enumerate(SCALE_PARTS) for g in range(g0, g1)}
+        w1_tiles = [tile("w1_%d_%d" % (g0, h0), [P, g1 - g0, 2 * GROUP * (h1 - h0)], U8) for g0, g1, h0, h1 in W1_PARTS]
+        s1_tiles = [tile("s1_%d_%d" % (g0, h0), [P, g1 - g0, GROUP * (h1 - h0)], U8) for g0, g1, h0, h1 in S1_PARTS]
+        w1, s1 = {}, {}
+        for found, tiles, parts, width in ((w1, w1_tiles, W1_PARTS, 2 * GROUP), (s1, s1_tiles, S1_PARTS, GROUP)):
+            for part, (g0, g1, h0, h1) in zip(tiles, parts):
+                for g in range(g0, g1):
+                    for h in range(h0, h1):
+                        found[h, g] = part[:, g - g0, width * (h - h0) : width * (h - h0 + 1)]
         w2_raw = [tile("w2_raw%d" % h, [P, 2 * N], U8) for h in range(2)]
         s2_raw = tile("s2_raw", [P, 2, N], U8)
         w2 = tile("w2", [P, 2, 2 * N], U8)
@@ -99,21 +95,17 @@ def tile_box_head_region_features_h1_kernel(
         def regions(rt, count=1):
             return slice(P * rt, P * (rt + count))
 
-        def load_vec(key, src):
-            nc.sync.dma_start(out=vec[key][:], in_=src.rearrange("(g p t) -> p g t", g=2, t=4))
+        def load_vec(queue, key, src):
+            queue.dma_start(out=vec[key][:], in_=src.rearrange("(g p t) -> p g t", g=2, t=4))
 
         def load_x(b):
             rt, c = b
-            cols = slice(2 * GROUP * c, 2 * GROUP * (c + 1))
-            if rt >= 2 or c not in x_pair:
-                nc.sync.dma_start(out=x_raw[b][:], in_=x[regions(rt), cols])
-            elif rt == 0:
-                src = x[regions(0, 2), cols].rearrange("(a r) n -> r a n", a=2)
-                nc.sync.dma_start(out=x_pair[c][:].rearrange("r (a n) -> r a n", a=2), in_=src)
+            nc.sync.dma_start(out=x_raw[b][:], in_=x[regions(rt), 2 * GROUP * c : 2 * GROUP * (c + 1)])
 
-        def load_w1(h, c):
-            src = w1_hbm[2 * c : 2 * c + 2, :, 256 * h : 256 * (h + 1)]
-            nc.sync.dma_start(out=w1[h, c][:].bitcast(I32), in_=src.rearrange("g p n -> p g n"))
+        def load_w1(part):
+            g0, g1, h0, h1 = W1_PARTS[part]
+            src = w1_hbm[g0:g1, :, 256 * h0 : 256 * h1]
+            nc.sync.dma_start(out=w1_tiles[part][:].bitcast(I32), in_=src.rearrange("g p n -> p g n"))
 
         def load_w2(h):
             nc.sync.dma_start(out=w2_raw[h][:].bitcast(I32), in_=w2_hbm[h])
@@ -123,11 +115,11 @@ def tile_box_head_region_features_h1_kernel(
                 queue.dma_start(out=plane[r:P:32].bitcast(I32), in_=src[:, r:16:4, :].rearrange("g q n -> q g n"))
 
         def load_s1(queue, part):
-            h, g0, g1 = SCALE_PARTS[part]
-            load_scale_rows(queue, s1_parts[part], s1_hbm[g0:g1, :, 128 * h : 128 * (h + 1)])
+            g0, g1, h0, h1 = S1_PARTS[part]
+            load_scale_rows(queue, s1_tiles[part], s1_hbm[g0:g1, :, 128 * h0 : 128 * h1])
 
-        def clear(plane):
-            nc.vector.memset(plane[:].bitcast(I32), 0)
+        def clear(plane, engine=nc.vector):
+            engine.memset(plane[:].bitcast(I32), 0)
 
         def spread_b1():
             bank = take("b1")
@@ -137,42 +129,56 @@ def tile_box_head_region_features_h1_kernel(
             nc.scalar.copy(out=b1_rows[:].bitcast(F32), in_=bank[:])
             give_back("b1")
 
-        def x_sort(run):
+        def x_sort(*run):
             for b in run:
                 nc.vector.tensor_copy(
                     out=x_sorted[b][:].rearrange("r (g u m) -> r g u m", g=2, u=2),
                     in_=x_raw[b][:].bitcast(F32).rearrange("r (g m u) -> r g u m", g=2, u=2),
                 )
 
-        def x_turn(run):
+        def x_turn(*run):
             for b in run:
                 bank = take(("x", b))
                 for j in range(4):
                     nc.tensor.transpose(bank[:, P * j : P * (j + 1)], x_sorted[b][:, P * j : P * (j + 1)], ident[:])
-                nc.scalar.copy(
-                    out=x_raw[b][:].bitcast(F32).rearrange("p (g r u) -> p g r u", g=2, u=2),
-                    in_=bank[:].rearrange("p (g u r) -> p g r u", g=2, u=2),
-                )
-                give_back(("x", b))
+                x_copy(b)
 
-        def x_quant(run):
+        def x_turn_raw(*run):
+            for b in run:
+                bank = take(("x", b))
+                words = x_raw[b][:].bitcast(F32)
+                for j in range(4):
+                    start = 2 * P * (j // 2) + j % 2
+                    nc.tensor.transpose(bank[:, P * j : P * (j + 1)], words[:, start : 2 * P * (j // 2 + 1) : 2], ident[:])
+                x_copy(b)
+
+        def x_copy(b):
+            nc.scalar.copy(
+                out=x_raw[b][:].bitcast(F32).rearrange("p (g r u) -> p g r u", g=2, u=2),
+                in_=bank_of(("x", b))[:].rearrange("p (g u r) -> p g r u", g=2, u=2),
+            )
+            give_back(("x", b))
+
+        def x_quant(*run):
             for b in run:
                 nc.vector.quantize_mx(out=x_codes[b][:].bitcast(FP8X4), scales=x_scales[b][:], in_=x_raw[b][:])
 
-        def mm1(rt, h, chunks):
-            for c in chunks:
-                bank = take(("h", rt, h)) if c == 0 else bank_of(("h", rt, h))
-                for j in range(2):
-                    g = 2 * c + j
-                    nc.tensor.matmul_mx(
-                        out=bank[:],
-                        lhsT=x_codes[rt, c][:, P * j : P * (j + 1)].bitcast(FP8X4),
-                        lhsT_scale=x_scales[rt, c][:, P * j : P * (j + 1)],
-                        rhs=w1[h, c][:, j, :].bitcast(FP4X4),
-                        rhs_scale=s1[h, g],
-                        start=(g == 0),
-                        stop=(g == GROUPS - 1),
-                    )
+        def mm1(rt, h, g):
+            bank = take(("h", rt, h)) if g == 0 else bank_of(("h", rt, h))
+            c, j = divmod(g, 2)
+            nc.tensor.matmul_mx(
+                out=bank[:],
+                lhsT=x_codes[rt, c][:, P * j : P * (j + 1)].bitcast(FP8X4),
+                lhsT_scale=x_scales[rt, c][:, P * j : P * (j + 1)],
+                rhs=w1[h, g].bitcast(FP4X4),
+                rhs_scale=s1[h, g],
+                start=(g == 0),
+                stop=(g == GROUPS - 1),
+            )
+
+        def mm1_half(rt, h, groups=range(GROUPS)):
+            for g in groups:
+                mm1(rt, h, g)
 
         def h_add(rt, h, parts=(slice(0, 2),)):
             dst = h_biased[rt, h][:].rearrange("r (u m e) -> r u m e", u=2, e=2)
@@ -182,23 +188,26 @@ def tile_box_head_region_features_h1_kernel(
                 nc.vector.tensor_tensor(out=dst[:, u], in0=src[:, u], in1=bias[:, u], op=ALU.add)
             give_back(("h", rt, h))
 
-        def h_turn(rt, count, h):
-            bank = take(("ht", rt, h))
-            for j in range(count):
-                words = h_biased[rt + j, h][:].bitcast(F32)
+        def h_turn(*parts):
+            bank = take(("ht", parts))
+            for i, key in enumerate(parts):
+                words = h_biased[key][:].bitcast(F32)
                 for u in range(2):
-                    cols = slice(P * (count * u + j), P * (count * u + j + 1))
+                    cols = slice(P * (len(parts) * u + i), P * (len(parts) * u + i + 1))
                     nc.tensor.transpose(bank[:, cols], words[:, P * u : P * (u + 1)], ident[:])
 
         def h_relu(rt, count, h, engine):
-            src = bank_of(("ht", rt, h))[:, 0 : 2 * P * count].bitcast(BF16)
-            src = src.rearrange("p (u r e) -> p r u e", u=2, e=2)
+            use = ("ht", tuple((rt + i, h) for i in range(count)))
+            src = bank_of(use)[:, 0 : 2 * P * count].bitcast(BF16).rearrange("p (u r e) -> p r u e", u=2, e=2)
+            relu_words(src, rt, count, h, engine)
+            give_back(use)
+
+        def relu_words(src, rt, count, h, engine):
             dst = h_turned[h][:, GROUP * rt : GROUP * (rt + count)].rearrange("p (r u e) -> p r u e", u=2, e=2)
             if engine == SCALAR:
                 nc.scalar.activation(out=dst, in_=src, func=ACT.Relu)
             else:
                 nc.vector.tensor_scalar(out=dst, in0=src, scalar1=0.0, scalar2=None, op0=ALU.max)
-            give_back(("ht", rt, h))
 
         def h_quant(rt, count, h):
             nc.vector.quantize_mx(
@@ -207,8 +216,8 @@ def tile_box_head_region_features_h1_kernel(
                 in_=h_turned[h][:, GROUP * rt : GROUP * (rt + count)],
             )
 
-        def w2_sort_words(h):
-            nc.vector.tensor_copy(
+        def w2_sort_words(h, copy):
+            copy(
                 out=w2[:, h, :].bitcast(U16).rearrange("p (g t m) -> p g t m", g=2, t=4),
                 in_=w2_raw[h][:].bitcast(U16).rearrange("p (g m t) -> p g t m", g=2, t=4),
             )
@@ -219,44 +228,37 @@ def tile_box_head_region_features_h1_kernel(
                 in_=s2_raw[:, h, :].rearrange("p (g m t) -> p g t m", g=2, t=4),
             )
 
-        def mm2(out, rt, g, t, h):
+        def mm2(out, rt, count, g, t, h, start, stop):
             col = GROUP * g + P * t
             nc.tensor.matmul_mx(
                 out=out,
                 lhsT=w2[:, h, 2 * col : 2 * (col + P)].bitcast(FP4X4),
                 lhsT_scale=s2[:, h, col : col + P],
-                rhs=h_codes[h][:, regions(rt)].bitcast(FP8X4),
-                rhs_scale=h_scales[h][:, regions(rt)],
-                start=(h == 0),
-                stop=(h == 1),
+                rhs=h_codes[h][:, regions(rt, count)].bitcast(FP8X4),
+                rhs_scale=h_scales[h][:, regions(rt, count)],
+                start=start,
+                stop=stop,
             )
 
-        def a_relu(src, rt, count, g, t, engine):
-            dst, bias = a_t[g][:, t, regions(rt, count)], vec["b2"][:, g, t : t + 1]
-            if engine == SCALAR:
-                nc.scalar.activation(out=dst, in_=src, func=ACT.Relu, bias=bias)
-            else:
-                nc.vector.tensor_scalar(out=dst, in0=src, scalar1=bias, scalar2=0.0, op0=ALU.add, op1=ALU.max)
-
-        def stage2(rt, count, g, slices):
-            bank = take(("z", rt, g, slices))
+        def z_passes(rt, count, g, slices, h):
+            use = ("z", rt, g, slices)
+            bank = take(use) if h == 0 else bank_of(use)
             width = P * count
             for j, t in enumerate(slices):
-                for i in range(count):
-                    for h in range(2):
-                        mm2(bank[:, width * j + P * i : width * j + P * (i + 1)], rt + i, g, t, h)
+                first, last = (h, j) == (0, 0), (h, j) == (1, len(slices) - 1)
+                mm2(bank[:, width * j : width * (j + 1)], rt, count, g, t, h, first, last)
+
+        def a_relu(rt, count, g, slices, engine):
+            use = ("z", rt, g, slices)
+            width = P * count
             for j, t in enumerate(slices):
-                a_relu(bank[:, width * j : width * (j + 1)], rt, count, g, t, SCALAR)
-            give_back(("z", rt, g, slices))
-
-        def slice_open(rt, g, t):
-            mm2(take(("z", rt, g, t))[:, 0:P], rt, g, t, 0)
-
-        def slice_close(rt, g, t, engine):
-            sums = bank_of(("z", rt, g, t))[:, 0:P]
-            mm2(sums, rt, g, t, 1)
-            a_relu(sums, rt, 1, g, t, engine)
-            give_back(("z", rt, g, t))
+                src = bank_of(use)[:, width * j : width * (j + 1)]
+                dst, bias = a_t[g][:, t, regions(rt, count)], vec["b2"][:, g, t : t + 1]
+                if engine == SCALAR:
+                    nc.scalar.activation(out=dst, in_=src, func=ACT.Relu, bias=bias)
+                else:
+                    nc.vector.tensor_scalar(out=dst, in0=src, scalar1=bias, scalar2=0.0, op0=ALU.add, op1=ALU.max)
+            give_back(use)
 
         def y_affine(rt, count, g, slices):
             for t in slices:
@@ -286,9 +288,11 @@ def tile_box_head_region_features_h1_kernel(
             bank = take(("y", rt, g))
             for t in range(4):
                 nc.tensor.transpose(bank[:, P * t : P * (t + 1)], y_t[g][:, t, regions(rt)], ident[:])
-            nc.scalar.copy(
+
+        def y_copy(rt, g, copy=nc.scalar.copy):
+            copy(
                 out=y_rows[rt][:, GROUP * g : GROUP * (g + 1)].rearrange("r (p t) -> r p t", t=4),
-                in_=bank[:].rearrange("r (t p) -> r p t", t=4),
+                in_=bank_of(("y", rt, g))[:].rearrange("r (t p) -> r p t", t=4),
             )
             give_back(("y", rt, g))
 
@@ -298,100 +302,112 @@ def tile_box_head_region_features_h1_kernel(
 
         def y_leave(rt, g):
             y_turn(rt, g)
+            y_copy(rt, g)
             store_y(rt, g)
 
-        def store_codes(rt, count, queue=nc.sync):
+        def store_codes(rt, count, queue):
             cols = regions(rt, count)
             queue.dma_start(out=codes_hbm[:, :, cols], in_=y_codes[:, :, cols].bitcast(I32))
 
-        def store_scales():
+        def store_scales(rt, count, queue):
+            words = slice(32 * rt, 32 * (rt + count))
             for r in range(4):
-                dst = scales_hbm[:, r:16:4, :].rearrange("g q n -> q g n")
-                nc.scalar.dma_start(out=dst, in_=y_scales[r:P:32].bitcast(I32))
-
-        first_rows, middle_rows, last_rows, second_half_rows = range(len(SCALE_PARTS))
-        make_identity(nc, ident[:])
-        for part in (first_rows, middle_rows, last_rows):
-            clear(s1_parts[part])
-        load_s1(nc.gpsimd, middle_rows)
-
-        runs = [blocks[TILES * c : TILES * (c + 1)] for c in range(CHUNKS)]
-        nc.scalar.dma_start(out=vec["b1"][:], in_=b1.rearrange("(g p t) -> p g t", g=2, t=4))
-        for c, run in enumerate(runs):
-            for b in run:
-                load_x(b)
-            load_w1(0, c)
-            if c == 0:
-                load_s1(nc.scalar, first_rows)
-        load_s1(nc.sync, last_rows)
-
-        spread_b1()
-        x_sort(runs[0][:2])
-        clear(s1_parts[second_half_rows])
-        x_sort(runs[0][2:3])
-        clear(s2_raw)
-        x_sort(runs[0][3:])
-
-        load_w1(1, 0)
-        load_s1(nc.sync, second_half_rows)
-        load_w1(1, 1)
-        load_w1(1, 2)
-        load_scale_rows(nc.sync, s2_raw, s2_hbm)
-        load_w1(1, 3)
-        for h in range(2):
-            load_w2(h)
-        load_vec("b2", b2)
-        load_vec("shift", shift)
-        load_vec("gain", gain)
-
-        done = 0
-        for c, run in enumerate(runs):
-            last = c == CHUNKS - 1
-            x_turn(run)
-            ready = blocks[done : len(blocks) if last else TILES * (c + 1) - LAG]
-            done += len(ready)
-            x_quant(ready)
-            if not last:
-                x_sort(runs[c + 1])
-            for rt, chunk in ready:
-                mm1(rt, 0, [chunk])
-
-        for rt in range(TILES):
-            h_add(rt, 0)
-        for c in (0, 1):
-            for rt in range(2):
-                mm1(rt, 1, [c])
-        for h in range(2):
-            w2_sort_scales(h)
-        for c in (2, 3):
-            for rt in range(2):
-                mm1(rt, 1, [c])
-
-        for rt in range(2):
-            h_add(rt, 1)
-        for h in range(2):
-            w2_sort_words(h)
-        mm1(2, 1, [0])
-        h_turn(0, 2, 0)
-        h_relu(0, 2, 0, SCALAR)
-        h_turn(2, 2, 0)
-        h_turn(0, 2, 1)
-        h_relu(0, 2, 1, VECTOR)
-        h_relu(2, 2, 0, SCALAR)
-        mm1(2, 1, [1, 2, 3])
-        h_quant(0, 2, 0)
-        h_quant(0, 2, 1)
-        mm1(3, 1, [0])
-        h_add(2, 1)
-        h_quant(2, 2, 0)
+                dst = scales_hbm[:, r:16:4, words].rearrange("g q n -> q g n")
+                queue.dma_start(out=dst, in_=y_scales[r:P:32].bitcast(I32)[:, :, words])
 
         low, high = (0, 1), (2, 3)
         pairs = [(g, slices) for g in range(2) for slices in (low, high)]
+
+        order = [(rt, c) for c in range(CHUNKS) for rt in range(TILES)]
+        clear(s1_tiles[0])
+        clear(s1_tiles[1])
+        clear(s1_tiles[2])
+        make_identity(nc, ident[:])
+        load_vec(nc.scalar, "b1", b1)
+        load_s1(nc.gpsimd, 1)
+        load_x((0, 0))
+        load_x((1, 0))
+        load_x((2, 0))
+        load_w1(0)
+        load_s1(nc.sync, 0)
+        load_x((3, 0))
+        for b in order[4:11]:
+            load_x(b)
+        load_w1(1)
+        for b in order[11:]:
+            load_x(b)
+        load_w1(2)
+        load_w1(3)
+        load_s1(nc.sync, 2)
+        load_w1(4)
+        clear(s1_tiles[3])
+        clear(s2_raw)
+        load_s1(nc.sync, 3)
+        load_w1(5)
+        load_w1(6)
+        load_scale_rows(nc.sync, s2_raw, s2_hbm)
+        load_w1(7)
+        for h in range(2):
+            load_w2(h)
+        load_vec(nc.sync, "b2", b2)
+        load_vec(nc.sync, "shift", shift)
+        load_vec(nc.sync, "gain", gain)
+
+        def passes(run):
+            for rt, c in run:
+                mm1_half(rt, 0, [2 * c, 2 * c + 1])
+
+        x_turn_raw(*order[0:2])
+        spread_b1()
+        x_turn_raw(order[2])
+        x_quant(*order[0:3])
+        passes(order[0:2])
+        x_sort(*order[3:7])
+        x_turn(*order[3:7])
+        x_quant(order[3])
+        passes(order[2:4])
+        x_sort(*order[7:11])
+        x_turn(*order[7:11])
+        x_quant(*order[4:8])
+        passes(order[4:8])
+        x_sort(*order[11:])
+        x_turn(*order[11:])
+        x_quant(*order[8:])
+        passes(order[8:])
+        mm1_half(0, 1, [0, 1])
+        for rt in range(TILES):
+            h_add(rt, 0)
+        mm1_half(1, 1, [0, 1])
+        for c in range(1, CHUNKS):
+            for rt in range(2):
+                mm1_half(rt, 1, [2 * c, 2 * c + 1])
+        for h in range(2):
+            w2_sort_scales(h)
+        for h in range(2):
+            w2_sort_words(h, nc.scalar.copy)
+        for rt in range(2):
+            h_add(rt, 1)
+        mm1_half(2, 1, [0, 1])
+        h_turn((0, 0), (1, 0))
+        h_relu(0, 2, 0, SCALAR)
+        h_turn((2, 0), (3, 0))
+        h_turn((0, 1), (1, 1))
+        h_relu(0, 2, 1, VECTOR)
+        h_relu(2, 2, 0, SCALAR)
+        mm1_half(2, 1, range(2, 8))
+        h_quant(0, 2, 0)
+        h_quant(0, 2, 1)
+        mm1_half(3, 1, range(0, 2))
+        h_add(2, 1)
+        h_quant(2, 2, 0)
+        for i, (g, slices) in enumerate(pairs):
+            for h in range(2):
+                z_passes(0, 2, g, slices, h)
+            a_relu(0, 2, g, slices, VECTOR if i == 1 else SCALAR)
         for g, slices in pairs:
-            stage2(0, 2, g, slices)
             y_affine(0, 2, g, slices)
-        mm1(3, 1, [1])
-        h_turn(2, 1, 1)
+        mm1_half(3, 1, range(2, 4))
+        h_turn((2, 1))
         h_relu(2, 1, 1, SCALAR)
         for rt, g in [(0, 0), (1, 0), (0, 1)]:
             y_leave(rt, g)
@@ -399,15 +415,16 @@ def tile_box_head_region_features_h1_kernel(
         h_quant(2, 1, 1)
         y_round(0, 2, 1)
         y_quant(0, 2, 0)
-        mm1(3, 1, [2, 3])
+        mm1_half(3, 1, range(4, 8))
         h_add(3, 1, (0, 1))
         y_quant(0, 2, 1)
-        store_codes(0, 2)
-
+        store_codes(0, 2, nc.sync)
         for g, slices in pairs:
-            stage2(2, 1, g, slices)
+            for h in range(2):
+                z_passes(2, 1, g, slices, h)
+            a_relu(2, 1, g, slices, SCALAR)
         y_affine(2, 1, 0, low + high)
-        h_turn(3, 1, 1)
+        h_turn((3, 1))
         h_relu(3, 1, 1, VECTOR)
         y_leave(1, 1)
         y_leave(2, 0)
@@ -416,17 +433,14 @@ def tile_box_head_region_features_h1_kernel(
         y_affine(2, 1, 1, high)
         y_round(2, 1, 0)
         y_round(2, 1, 1)
-
-        out_slices = [(g, t) for g in range(2) for t in range(4)]
-        for g, t in out_slices[:AHEAD]:
-            slice_open(3, g, t)
-        for i, (g, t) in enumerate(out_slices):
-            if i >= AHEAD:
-                slice_open(3, g, t)
-            slice_close(3, g, t, VECTOR if g == 0 and t % 2 == 1 else SCALAR)
+        for g, slices in pairs:
+            z_passes(3, 1, g, slices, 0)
+        for i, (g, slices) in enumerate(pairs):
+            z_passes(3, 1, g, slices, 1)
+            a_relu(3, 1, g, slices, VECTOR if i == 1 else SCALAR)
         y_quant(2, 1, 0)
         y_quant(2, 1, 1)
-        store_codes(2, 1)
+        store_codes(2, 1, nc.sync)
         y_affine(3, 1, 0, low + high)
         y_affine(3, 1, 1, low + high)
         y_leave(2, 1)
@@ -434,8 +448,9 @@ def tile_box_head_region_features_h1_kernel(
         for g in range(2):
             y_round(3, 1, g)
         y_turn(3, 1)
+        y_copy(3, 1)
         for g in range(2):
             y_quant(3, 1, g)
         store_y(3, 1)
         store_codes(3, 1, nc.scalar)
-        store_scales()
+        store_scales(0, 4, nc.scalar)

@@ -143,15 +143,6 @@ def tile_box_head_region_features_h1_kernel(
                     nc.tensor.transpose(bank[:, P * j : P * (j + 1)], x_sorted[b][:, P * j : P * (j + 1)], ident[:])
                 x_copy(b)
 
-        def x_turn_raw(*run):
-            for b in run:
-                bank = take(("x", b))
-                words = x_raw[b][:].bitcast(F32)
-                for j in range(4):
-                    start = 2 * P * (j // 2) + j % 2
-                    nc.tensor.transpose(bank[:, P * j : P * (j + 1)], words[:, start : 2 * P * (j // 2 + 1) : 2], ident[:])
-                x_copy(b)
-
         def x_copy(b):
             nc.scalar.copy(
                 out=x_raw[b][:].bitcast(F32).rearrange("p (g r u) -> p g r u", g=2, u=2),
@@ -357,12 +348,14 @@ def tile_box_head_region_features_h1_kernel(
             for rt, c in run:
                 mm1_half(rt, 0, [2 * c, 2 * c + 1])
 
-        x_turn_raw(*order[0:2])
         spread_b1()
-        x_turn_raw(order[2])
-        x_quant(*order[0:3])
+        x_sort(*order[0:3])
+        x_turn(*order[0:3])
+        x_quant(*order[0:2])
         passes(order[0:2])
-        x_sort(*order[3:7])
+        x_sort(order[3])
+        x_quant(order[2])
+        x_sort(*order[4:7])
         x_turn(*order[3:7])
         x_quant(order[3])
         passes(order[2:4])

@@ -300,9 +300,9 @@ def tile_box_head_region_features_h1_kernel(
             cols = regions(rt, count)
             queue.dma_start(out=codes_hbm[:, :, cols], in_=y_codes[:, :, cols].bitcast(I32))
 
-        def store_scales(rt, count, queue):
+        def store_scales(rt, count, queue, rows=range(4)):
             words = slice(32 * rt, 32 * (rt + count))
-            for r in range(4):
+            for r in rows:
                 dst = scales_hbm[:, r:16:4, words].rearrange("g q n -> q g n")
                 queue.dma_start(out=dst, in_=y_scales[r:P:32].bitcast(I32)[:, :, words])
 
@@ -376,10 +376,10 @@ def tile_box_head_region_features_h1_kernel(
                 mm1_half(rt, 1, [2 * c, 2 * c + 1])
         for h in range(2):
             w2_sort_scales(h)
-        for h in range(2):
-            w2_sort_words(h, nc.scalar.copy)
         for rt in range(2):
             h_add(rt, 1)
+        for h in range(2):
+            w2_sort_words(h, nc.vector.tensor_copy)
         mm1_half(2, 1, [0, 1])
         h_turn((0, 0), (1, 0))
         h_relu(0, 2, 0, SCALAR)

@@ -24,7 +24,7 @@ GROUPS = D // GROUP
 CHUNKS = GROUPS // 2
 SCALAR, VECTOR = "scalar", "vector"
 W1_PARTS = [(2 * c, 2 * c + 2, h, h + 1) for h in range(2) for c in range(CHUNKS)]
-S1_PARTS = [(0, 2, 0, 1), (2, 6, 0, 1), (6, 8, 0, 1), (0, 8, 1, 2)]
+S1_PARTS = [(0, 2, 0, 1), (4, 8, 0, 1), (2, 4, 0, 1), (0, 8, 1, 2)]
 
 
 def tile_box_head_region_features_h1_kernel(
@@ -49,7 +49,8 @@ def tile_box_head_region_features_h1_kernel(
         blocks = [(rt, c) for rt in range(TILES) for c in range(CHUNKS)]
         banks = [ps.tile([P, GROUP], F32, name="bank%d" % i) for i in range(8)]
         ident = tile("ident", [P, P], F32)
-        vec = {key: tile("vec_" + key, [P, 2, 4], BF16) for key in ("b1", "b2", "shift", "gain")}
+        vec = {key: tile("vec_" + key, [P, 2, 4], BF16) for key in ("b2", "shift", "gain")}
+        b1_cols = tile("b1_cols", [P, 8], BF16)
         b1_rows = tile("b1_rows", [P, F], BF16)
         x_raw = {b: tile("x_raw%d_%d" % b, [P, 2 * GROUP], BF16) for b in blocks}
         x_sorted = {b: tile("x_sorted%d_%d" % b, [P, GROUP], F32) for b in blocks}
@@ -98,6 +99,9 @@ def tile_box_head_region_features_h1_kernel(
         def load_vec(queue, key, src):
             queue.dma_start(out=vec[key][:], in_=src.rearrange("(g p t) -> p g t", g=2, t=4))
 
+        def load_b1():
+            nc.scalar.dma_start(out=b1_cols[:], in_=b1.rearrange("(p j) -> p j", j=8))
+
         def load_x(b):
             rt, c = b
             nc.sync.dma_start(out=x_raw[b][:], in_=x[regions(rt), 2 * GROUP * c : 2 * GROUP * (c + 1)])
@@ -123,10 +127,13 @@ def tile_box_head_region_features_h1_kernel(
 
         def spread_b1():
             bank = take("b1")
-            words = vec["b1"][:].rearrange("p g t -> p (g t)").bitcast(F32)
+            words = b1_cols[:].bitcast(F32)
             for j in range(4):
                 nc.tensor.transpose(bank[:, P * j : P * (j + 1)], words[:, j : j + 1].to_broadcast([P, P]), ident[:])
-            nc.scalar.copy(out=b1_rows[:].bitcast(F32), in_=bank[:])
+            nc.scalar.copy(
+                out=b1_rows[:].bitcast(F32).rearrange("r (h u a b) -> r h u a b", h=2, u=2, b=2),
+                in_=bank[:].rearrange("r (b u h a) -> r h u a b", b=2, u=2, h=2),
+            )
             give_back("b1")
 
         def x_sort(*run):
@@ -310,29 +317,39 @@ def tile_box_head_region_features_h1_kernel(
         pairs = [(g, slices) for g in range(2) for slices in (low, high)]
 
         order = [(rt, c) for c in range(CHUNKS) for rt in range(TILES)]
+        make_identity(nc, ident[:])
         clear(s1_tiles[0])
         clear(s1_tiles[1])
         clear(s1_tiles[2])
-        make_identity(nc, ident[:])
-        load_vec(nc.scalar, "b1", b1)
         load_s1(nc.gpsimd, 1)
-        load_x((0, 0))
-        load_x((1, 0))
-        load_x((2, 0))
+        load_b1()
+        for b in order[:4]:
+            load_x(b)
         load_w1(0)
         load_s1(nc.sync, 0)
-        load_x((3, 0))
-        for b in order[4:11]:
+        for b in order[4:10]:
             load_x(b)
         load_w1(1)
-        for b in order[11:]:
+        load_s1(nc.sync, 2)
+        for b in order[10:14]:
             load_x(b)
         load_w1(2)
+        for b in order[14:]:
+            load_x(b)
         load_w1(3)
-        load_s1(nc.sync, 2)
-        load_w1(4)
-        clear(s1_tiles[3])
+
+        def passes(run):
+            for rt, c in run:
+                mm1_half(rt, 0, [2 * c, 2 * c + 1])
+
+        spread_b1()
+        x_sort(order[0])
+        x_sort(order[1])
         clear(s2_raw)
+        x_sort(order[2])
+        clear(s1_tiles[3])
+        x_sort(order[3])
+        load_w1(4)
         load_s1(nc.sync, 3)
         load_w1(5)
         load_w1(6)
@@ -343,31 +360,26 @@ def tile_box_head_region_features_h1_kernel(
         load_vec(nc.sync, "b2", b2)
         load_vec(nc.sync, "shift", shift)
         load_vec(nc.sync, "gain", gain)
-
-        def passes(run):
-            for rt, c in run:
-                mm1_half(rt, 0, [2 * c, 2 * c + 1])
-
-        spread_b1()
-        x_sort(*order[0:3])
-        x_turn(*order[0:3])
+        x_turn(*order[0:4])
         x_quant(*order[0:2])
         passes(order[0:2])
-        x_sort(order[3])
         x_quant(order[2])
-        x_sort(*order[4:7])
-        x_turn(*order[3:7])
+        x_sort(order[4])
         x_quant(order[3])
+        x_sort(order[5])
+        x_turn(*order[4:6])
         passes(order[2:4])
-        x_sort(*order[7:11])
-        x_turn(*order[7:11])
-        x_quant(*order[4:8])
-        passes(order[4:8])
-        x_sort(*order[11:])
-        x_turn(*order[11:])
-        x_quant(*order[8:])
-        passes(order[8:])
+        for start in (6, 10):
+            x_sort(*order[start : start + 4])
+            x_turn(*order[start : start + 4])
+            x_quant(*order[start - 2 : start + 2])
+            passes(order[start - 2 : start + 2])
+        x_sort(*order[14:])
+        x_turn(*order[14:])
+        x_quant(*order[12:])
+        passes(order[12:14])
         mm1_half(0, 1, [0, 1])
+        passes(order[14:])
         for rt in range(TILES):
             h_add(rt, 0)
         mm1_half(1, 1, [0, 1])

@@ -25,6 +25,7 @@ CHUNKS = GROUPS // 2
 SCALAR, VECTOR = "scalar", "vector"
 W1_PARTS = [(2 * c, 2 * c + 2, h, h + 1) for h in range(2) for c in range(CHUNKS)]
 S1_PARTS = [(0, 2, 0, 1), (4, 8, 0, 1), (2, 4, 0, 1), (0, 8, 1, 2)]
+PAIRED = [(2, 1), (3, 1), (0, 2), (1, 2), (2, 2), (3, 2), (0, 3), (1, 3), (2, 3), (3, 3)]
 
 
 def tile_box_head_region_features_h1_kernel(
@@ -52,7 +53,10 @@ def tile_box_head_region_features_h1_kernel(
         vec = {key: tile("vec_" + key, [P, 2, 4], BF16) for key in ("b2", "shift", "gain")}
         b1_cols = tile("b1_cols", [P, 8], BF16)
         b1_rows = tile("b1_rows", [P, F], BF16)
-        x_raw = {b: tile("x_raw%d_%d" % b, [P, 2 * GROUP], BF16) for b in blocks}
+        x_raw = {b: tile("x_raw%d_%d" % b, [P, 2 * GROUP], BF16) for b in blocks if b not in PAIRED}
+        x_pairs = {b: tile("x_pair%d_%d" % b, [P, 4 * GROUP], BF16) for b in PAIRED[::2]}
+        for (rt, c), pair in x_pairs.items():
+            x_raw[rt, c], x_raw[rt + 1, c] = pair[:, 0 : 2 * GROUP], pair[:, 2 * GROUP : 4 * GROUP]
         x_sorted = {b: tile("x_sorted%d_%d" % b, [P, GROUP], F32) for b in blocks}
         x_codes = {b: tile("x_codes%d_%d" % b, [P, 2 * P], U32) for b in blocks}
         x_scales = {b: tile("x_scales%d_%d" % b, [P, 2 * P], U8) for b in blocks}
@@ -104,7 +108,12 @@ def tile_box_head_region_features_h1_kernel(
 
         def load_x(b):
             rt, c = b
-            nc.sync.dma_start(out=x_raw[b][:], in_=x[regions(rt), 2 * GROUP * c : 2 * GROUP * (c + 1)])
+            cols = slice(2 * GROUP * c, 2 * GROUP * (c + 1))
+            if b in x_pairs:
+                src = x[regions(rt, 2), cols].rearrange("(a r) k -> r a k", a=2)
+                nc.sync.dma_start(out=x_pairs[b][:].rearrange("r (a k) -> r a k", a=2), in_=src)
+            elif b not in PAIRED:
+                nc.sync.dma_start(out=x_raw[b][:], in_=x[regions(rt), cols])
 
         def load_w1(part):
             g0, g1, h0, h1 = W1_PARTS[part]
@@ -246,10 +255,11 @@ def tile_box_head_region_features_h1_kernel(
                 first, last = (h, j) == (0, 0), (h, j) == (1, len(slices) - 1)
                 mm2(bank[:, width * j : width * (j + 1)], rt, count, g, t, h, first, last)
 
-        def a_relu(rt, count, g, slices, engine):
+        def a_relu(rt, count, g, slices, *engines):
             use = ("z", rt, g, slices)
             width = P * count
             for j, t in enumerate(slices):
+                engine = engines[j % len(engines)]
                 src = bank_of(use)[:, width * j : width * (j + 1)]
                 dst, bias = a_t[g][:, t, regions(rt, count)], vec["b2"][:, g, t : t + 1]
                 if engine == SCALAR:
@@ -347,8 +357,15 @@ def tile_box_head_region_features_h1_kernel(
         x_sort(order[1])
         clear(s2_raw)
         x_sort(order[2])
-        clear(s1_tiles[3])
         x_sort(order[3])
+        x_turn(*order[0:4])
+        x_quant(*order[0:2])
+        passes(order[0:2])
+        x_quant(order[2])
+        x_sort(order[4])
+        x_quant(order[3])
+        x_sort(order[5])
+        clear(s1_tiles[3])
         load_w1(4)
         load_s1(nc.sync, 3)
         load_w1(5)
@@ -360,13 +377,6 @@ def tile_box_head_region_features_h1_kernel(
         load_vec(nc.sync, "b2", b2)
         load_vec(nc.sync, "shift", shift)
         load_vec(nc.sync, "gain", gain)
-        x_turn(*order[0:4])
-        x_quant(*order[0:2])
-        passes(order[0:2])
-        x_quant(order[2])
-        x_sort(order[4])
-        x_quant(order[3])
-        x_sort(order[5])
         x_turn(*order[4:6])
         passes(order[2:4])
         for start in (6, 10):
@@ -402,7 +412,7 @@ def tile_box_head_region_features_h1_kernel(
         mm1_half(2, 1, range(2, 8))
         h_quant(0, 2, 0)
         h_quant(0, 2, 1)
-        mm1_half(3, 1, range(0, 2))
+        mm1_half(3, 1, range(0, 1))
         h_add(2, 1)
         h_quant(2, 2, 0)
         for i, (g, slices) in enumerate(pairs):
@@ -411,7 +421,7 @@ def tile_box_head_region_features_h1_kernel(
             a_relu(0, 2, g, slices, VECTOR if i == 1 else SCALAR)
         for g, slices in pairs:
             y_affine(0, 2, g, slices)
-        mm1_half(3, 1, range(2, 4))
+        mm1_half(3, 1, range(1, 4))
         h_turn((2, 1))
         h_relu(2, 1, 1, SCALAR)
         for rt, g in [(0, 0), (1, 0), (0, 1)]:

@@ -80,7 +80,7 @@ def tile_box_head_region_features_h1_kernel(
         y_t = [tile("y_t%d" % g, [P, 4, R], F32) for g in range(2)]
         y_bf16 = [tile("y_bf16_%d" % g, [P, R, 4], BF16) for g in range(2)]
         y_codes = tile("y_codes", [P, 2, R], U32)
-        y_scales = tile("y_scales", [P, 2, R], U8)
+        y_scales = tile("y_scales", [P, R], U8)
         y_rows = [tile("y_rows%d" % rt, [P, N], F32) for rt in range(TILES)]
 
         free_banks = list(range(len(banks)))
@@ -281,14 +281,14 @@ def tile_box_head_region_features_h1_kernel(
 
         def y_round(rt, count, g):
             nc.vector.tensor_copy(
-                out=y_bf16[g][:, regions(rt, count), :],
-                in_=y_t[g][:, :, regions(rt, count)].rearrange("p t r -> p r t"),
+                out=y_bf16[g][:, regions(rt, count), :].rearrange("p (c i) t -> p c t i", i=4),
+                in_=y_t[g][:, :, regions(rt, count)].rearrange("p t (c i) -> p c t i", i=4),
             )
 
         def y_quant(rt, count, g):
             nc.vector.quantize_mx(
                 out=y_codes[:, g, regions(rt, count)].bitcast(FP8X4),
-                scales=y_scales[:, g, regions(rt, count)],
+                scales=y_scales[4 * g : P, regions(rt, count)],
                 in_=y_bf16[g][:, regions(rt, count), :].rearrange("p r t -> p (r t)"),
             )
 
@@ -317,11 +317,9 @@ def tile_box_head_region_features_h1_kernel(
             cols = regions(rt, count)
             queue.dma_start(out=codes_hbm[:, :, cols], in_=y_codes[:, :, cols].bitcast(I32))
 
-        def store_scales(rt, count, queue, rows=range(4)):
-            words = slice(32 * rt, 32 * (rt + count))
-            for r in rows:
-                dst = scales_hbm[:, r:16:4, words].rearrange("g q n -> q g n")
-                queue.dma_start(out=dst, in_=y_scales[r:P:32].bitcast(I32)[:, :, words])
+        def store_scales(rt, count, queue):
+            for q in range(4):
+                queue.dma_start(out=scales_hbm[:, 4 * q : 4 * q + 4, :], in_=y_scales[32 * q : 32 * q + 8].bitcast(I32))
 
         low, high = (0, 1), (2, 3)
         pairs = [(g, slices) for g in range(2) for slices in (low, high)]
@@ -448,12 +446,12 @@ def tile_box_head_region_features_h1_kernel(
         y_affine(2, 1, 1, high)
         y_round(2, 1, 0)
         y_round(2, 1, 1)
+        y_quant(2, 1, 0)
         for g, slices in pairs:
             z_passes(3, 1, g, slices, 0)
         for i, (g, slices) in enumerate(pairs):
             z_passes(3, 1, g, slices, 1)
             a_relu(3, 1, g, slices, VECTOR if i == 1 else SCALAR)
-        y_quant(2, 1, 0)
         y_quant(2, 1, 1)
         store_codes(2, 1, nc.sync)
         y_affine(3, 1, 0, low + high)

from contextlib import ExitStack

import concourse.mybir as mybir
from concourse.masks import make_identity

R, D, F, N = 512, 4096, 1024, 1024
FLOPS = 2 * R * D * F + 2 * R * F * N

F32 = mybir.dt.float32
BF16 = mybir.dt.bfloat16
U32 = mybir.dt.uint32
I32 = mybir.dt.int32
U16 = mybir.dt.uint16
U8 = mybir.dt.uint8
FP8X4 = mybir.dt.float8_e4m3fn_x4
FP4X4 = mybir.dt.float4_e2m1fn_x4
ALU = mybir.AluOpType
ACT = mybir.ActivationFunctionType

P = 128
GROUP = 512
TILES = R // P
GROUPS = D // GROUP
CHUNKS = GROUPS // 2
SCALAR, VECTOR = "scalar", "vector"
W1_PARTS = [(2 * c, 2 * c + 2, h, h + 1) for h in range(2) for c in range(CHUNKS)]
S1_PARTS = [(0, 2, 0, 1), (4, 8, 0, 1), (2, 4, 0, 1), (0, 8, 1, 2)]
PAIRED = [(2, 1), (3, 1), (0, 2), (1, 2), (2, 2), (3, 2), (0, 3), (1, 3), (2, 3), (3, 3)]


def tile_box_head_region_features_h1_kernel(
    tc, roi, w1_words, w1_scales, b1, w2_words, w2_scales, b2, shift, gain, out_0, out_1, out_2
):
    nc = tc.nc
    x = roi.rearrange("r c a b -> r (c a b)")
    w1_hbm, s1_hbm = w1_words.bitcast(I32), w1_scales.bitcast(I32)
    w2_hbm, s2_hbm = w2_words.bitcast(I32), w2_scales.bitcast(I32)
    codes_hbm = out_1.rearrange("g p m t -> p g (m t)").bitcast(I32)
    scales_hbm = out_2.bitcast(I32)

    with ExitStack() as ctx:
        sb = ctx.enter_context(tc.tile_pool(name="sb", bufs=1))
        ps = ctx.enter_context(tc.psum_pool(name="ps", bufs=1))
        ctx.enter_context(tc.manual_schedule())

        def tile(name, shape, dtype):
            return sb.tile(shape, dtype, name=name, align_bytes=64)

        halves = [(rt, h) for rt in range(TILES) for h in range(2)]
        blocks = [(rt, c) for rt in range(TILES) for c in range(CHUNKS)]
        banks = [ps.tile([P, GROUP], F32, name="bank%d" % i) for i in range(8)]
        ident = tile("ident", [P, P], F32)
        vec = {key: tile("vec_" + key, [P, 2, 4], BF16) for key in ("b2", "shift", "gain")}
        b1_cols = tile("b1_cols", [P, 8], BF16)
        b1_rows = tile("b1_rows", [P, F], BF16)
        x_raw = {b: tile("x_raw%d_%d" % b, [P, 2 * GROUP], BF16) for b in blocks if b not in PAIRED}
        x_pairs = {b: tile("x_pair%d_%d" % b, [P, 4 * GROUP], BF16) for b in PAIRED[::2]}
        for (rt, c), pair in x_pairs.items():
            x_raw[rt, c], x_raw[rt + 1, c] = pair[:, 0 : 2 * GROUP], pair[:, 2 * GROUP : 4 * GROUP]
        x_sorted = {b: tile("x_sorted%d_%d" % b, [P, GROUP], F32) for b in blocks}
        x_codes = {b: tile("x_codes%d_%d" % b, [P, 2 * P], U32) for b in blocks}
        x_scales = {b: tile("x_scales%d_%d" % b, [P, 2 * P], U8) for b in blocks}
        w1_tiles = [tile("w1_%d_%d" % (g0, h0), [P, g1 - g0, 2 * GROUP * (h1 - h0)], U8) for g0, g1, h0, h1 in W1_PARTS]
        s1_tiles = [tile("s1_%d_%d" % (g0, h0), [P, g1 - g0, GROUP * (h1 - h0)], U8) for g0, g1, h0, h1 in S1_PARTS]
        w1, s1 = {}, {}
        for found, tiles, parts, width in ((w1, w1_tiles, W1_PARTS, 2 * GROUP), (s1, s1_tiles, S1_PARTS, GROUP)):
            for part, (g0, g1, h0, h1) in zip(tiles, parts):
                for g in range(g0, g1):
                    for h in range(h0, h1):
                        found[h, g] = part[:, g - g0, width * (h - h0) : width * (h - h0 + 1)]
        w2_raw = [tile("w2_raw%d" % h, [P, 2 * N], U8) for h in range(2)]
        s2_raw = tile("s2_raw", [P, 2, N], U8)
        w2 = tile("w2", [P, 2, 2 * N], U8)
        s2 = tile("s2", [P, 2, N], U8)
        h_biased = {key: tile("h_biased%d_%d" % key, [P, GROUP], BF16) for key in halves}
        h_turned = [tile("h_turned%d" % h, [P, TILES * GROUP], BF16) for h in range(2)]
        h_codes = [tile("h_codes%d" % h, [P, R], U32) for h in range(2)]
        h_scales = [tile("h_scales%d" % h, [P, R], U8) for h in range(2)]
        a_t = [tile("a_t%d" % g, [P, 4, R], F32) for g in range(2)]
        y_t = [tile("y_t%d" % g, [P, 4, R], F32) for g in range(2)]
        y_bf16 = [tile("y_bf16_%d" % g, [P, R, 4], BF16) for g in range(2)]
        y_codes = tile("y_codes", [P, 2, R], U32)
        y_scales = tile("y_scales", [P, R], U8)
        y_rows = [tile("y_rows%d" % rt, [P, N], F32) for rt in range(TILES)]

        free_banks = list(range(len(banks)))
        held = {}

        def take(use):
            held[use] = free_banks[0]
            free_banks.remove(held[use])
            return banks[held[use]]

        def bank_of(use):
            return banks[held[use]]

        def give_back(use):
            free_banks.append(held[use])

        def regions(rt, count=1):
            return slice(P * rt, P * (rt + count))

        def load_vec(queue, key, src):
            queue.dma_start(out=vec[key][:], in_=src.rearrange("(g p t) -> p g t", g=2, t=4))

        def load_b1():
            nc.scalar.dma_start(out=b1_cols[:], in_=b1.rearrange("(p j) -> p j", j=8))

        def load_x(b):
            rt, c = b
            cols = slice(2 * GROUP * c, 2 * GROUP * (c + 1))
            if b in x_pairs:
                src = x[regions(rt, 2), cols].rearrange("(a r) k -> r a k", a=2)
                nc.sync.dma_start(out=x_pairs[b][:].rearrange("r (a k) -> r a k", a=2), in_=src)
            elif b not in PAIRED:
                nc.sync.dma_start(out=x_raw[b][:], in_=x[regions(rt), cols])

        def load_w1(part):
            g0, g1, h0, h1 = W1_PARTS[part]
            src = w1_hbm[g0:g1, :, 256 * h0 : 256 * h1]
            nc.sync.dma_start(out=w1_tiles[part][:].bitcast(I32), in_=src.rearrange("g p n -> p g n"))

        def load_w2(h):
            nc.sync.dma_start(out=w2_raw[h][:].bitcast(I32), in_=w2_hbm[h])

        def load_scale_rows(queue, plane, src):
            for r in range(4):
                queue.dma_start(out=plane[r:P:32].bitcast(I32), in_=src[:, r:16:4, :].rearrange("g q n -> q g n"))

        def load_s1(queue, part):
            g0, g1, h0, h1 = S1_PARTS[part]
            load_scale_rows(queue, s1_tiles[part], s1_hbm[g0:g1, :, 128 * h0 : 128 * h1])

        def clear(plane, engine=nc.vector):
            engine.memset(plane[:].bitcast(I32), 0)

        def spread_b1():
            bank = take("b1")
            words = b1_cols[:].bitcast(F32)
            for j in range(4):
                nc.tensor.transpose(bank[:, P * j : P * (j + 1)], words[:, j : j + 1].to_broadcast([P, P]), ident[:])
            nc.scalar.copy(
                out=b1_rows[:].bitcast(F32).rearrange("r (h u a b) -> r h u a b", h=2, u=2, b=2),
                in_=bank[:].rearrange("r (b u h a) -> r h u a b", b=2, u=2, h=2),
            )
            give_back("b1")

        def x_sort(*run):
            for b in run:
                nc.vector.tensor_copy(
                    out=x_sorted[b][:].rearrange("r (g u m) -> r g u m", g=2, u=2),
                    in_=x_raw[b][:].bitcast(F32).rearrange("r (g m u) -> r g u m", g=2, u=2),
                )

        def x_turn(*run):
            for b in run:
                bank = take(("x", b))
                for j in range(4):
                    nc.tensor.transpose(bank[:, P * j : P * (j + 1)], x_sorted[b][:, P * j : P * (j + 1)], ident[:])
                x_copy(b)

        def x_copy(b):
            nc.scalar.copy(
                out=x_raw[b][:].bitcast(F32).rearrange("p (g r u) -> p g r u", g=2, u=2),
                in_=bank_of(("x", b))[:].rearrange("p (g u r) -> p g r u", g=2, u=2),
            )
            give_back(("x", b))

        def x_quant(*run):
            for b in run:
                nc.vector.quantize_mx(out=x_codes[b][:].bitcast(FP8X4), scales=x_scales[b][:], in_=x_raw[b][:])

        def mm1(rt, h, g):
            bank = take(("h", rt, h)) if g == 0 else bank_of(("h", rt, h))
            c, j = divmod(g, 2)
            nc.tensor.matmul_mx(
                out=bank[:],
                lhsT=x_codes[rt, c][:, P * j : P * (j + 1)].bitcast(FP8X4),
                lhsT_scale=x_scales[rt, c][:, P * j : P * (j + 1)],
                rhs=w1[h, g].bitcast(FP4X4),
                rhs_scale=s1[h, g],
                start=(g == 0),
                stop=(g == GROUPS - 1),
            )

        def mm1_half(rt, h, groups=range(GROUPS)):
            for g in groups:
                mm1(rt, h, g)

        def h_add(rt, h, parts=(slice(0, 2),)):
            dst = h_biased[rt, h][:].rearrange("r (u m e) -> r u m e", u=2, e=2)
            src = bank_of(("h", rt, h))[:].rearrange("r (m u e) -> r u m e", u=2, e=2)
            bias = b1_rows[:, GROUP * h : GROUP * (h + 1)].rearrange("r (u m e) -> r u m e", u=2, e=2)
            for u in parts:
                nc.vector.tensor_tensor(out=dst[:, u], in0=src[:, u], in1=bias[:, u], op=ALU.add)
            give_back(("h", rt, h))

        def h_turn(*parts):
            bank = take(("ht", parts))
            for i, key in enumerate(parts):
                words = h_biased[key][:].bitcast(F32)
                for u in range(2):
                    cols = slice(P * (len(parts) * u + i), P * (len(parts) * u + i + 1))
                    nc.tensor.transpose(bank[:, cols], words[:, P * u : P * (u + 1)], ident[:])

        def h_relu(rt, count, h, engine):
            use = ("ht", tuple((rt + i, h) for i in range(count)))
            src = bank_of(use)[:, 0 : 2 * P * count].bitcast(BF16).rearrange("p (u r e) -> p r u e", u=2, e=2)
            relu_words(src, rt, count, h, engine)
            give_back(use)

        def relu_words(src, rt, count, h, engine):
            dst = h_turned[h][:, GROUP * rt : GROUP * (rt + count)].rearrange("p (r u e) -> p r u e", u=2, e=2)
            if engine == SCALAR:
                nc.scalar.activation(out=dst, in_=src, func=ACT.Relu)
            else:
                nc.vector.tensor_scalar(out=dst, in0=src, scalar1=0.0, scalar2=None, op0=ALU.max)

        def h_quant(rt, count, h):
            nc.vector.quantize_mx(
                out=h_codes[h][:, regions(rt, count)].bitcast(FP8X4),
                scales=h_scales[h][:, regions(rt, count)],
                in_=h_turned[h][:, GROUP * rt : GROUP * (rt + count)],
            )

        def w2_sort_words(h, copy):
            copy(
                out=w2[:, h, :].bitcast(U16).rearrange("p (g t m) -> p g t m", g=2, t=4),
                in_=w2_raw[h][:].bitcast(U16).rearrange("p (g m t) -> p g t m", g=2, t=4),
            )

        def w2_sort_scales(h):
            nc.vector.tensor_copy(
                out=s2[:, h, :].rearrange("p (g t m) -> p g t m", g=2, t=4),
                in_=s2_raw[:, h, :].rearrange("p (g m t) -> p g t m", g=2, t=4),
            )

        def mm2(out, rt, count, g, t, h, start, stop):
            col = GROUP * g + P * t
            nc.tensor.matmul_mx(
                out=out,
                lhsT=w2[:, h, 2 * col : 2 * (col + P)].bitcast(FP4X4),
                lhsT_scale=s2[:, h, col : col + P],
                rhs=h_codes[h][:, regions(rt, count)].bitcast(FP8X4),
                rhs_scale=h_scales[h][:, regions(rt, count)],
                start=start,
                stop=stop,
            )

        def z_passes(rt, count, g, slices, h):
            use = ("z", rt, g, slices)
            bank = take(use) if h == 0 else bank_of(use)
            width = P * count
            for j, t in enumerate(slices):
                first, last = (h, j) == (0, 0), (h, j) == (1, len(slices) - 1)
                mm2(bank[:, width * j : width * (j + 1)], rt, count, g, t, h, first, last)

        def a_relu(rt, count, g, slices, *engines):
            use = ("z", rt, g, slices)
            width = P * count
            for j, t in enumerate(slices):
                engine = engines[j % len(engines)]
                src = bank_of(use)[:, width * j : width * (j + 1)]
                dst, bias = a_t[g][:, t, regions(rt, count)], vec["b2"][:, g, t : t + 1]
                if engine == SCALAR:
                    nc.scalar.activation(out=dst, in_=src, func=ACT.Relu, bias=bias)
                else:
                    nc.vector.tensor_scalar(out=dst, in0=src, scalar1=bias, scalar2=0.0, op0=ALU.add, op1=ALU.max)
            give_back(use)

        def y_affine(rt, count, g, slices):
            for t in slices:
                nc.vector.tensor_scalar(
                    out=y_t[g][:, t, regions(rt, count)],
                    in0=a_t[g][:, t, regions(rt, count)],
                    scalar1=vec["shift"][:, g, t : t + 1],
                    scalar2=vec["gain"][:, g, t : t + 1],
                    op0=ALU.add,
                    op1=ALU.mult,
                )

        def y_round(rt, count, g):
            nc.vector.tensor_copy(
                out=y_bf16[g][:, regions(rt, count), :].rearrange("p (c i) t -> p c t i", i=4),
                in_=y_t[g][:, :, regions(rt, count)].rearrange("p t (c i) -> p c t i", i=4),
            )

        def y_quant(rt, count, g):
            nc.vector.quantize_mx(
                out=y_codes[:, g, regions(rt, count)].bitcast(FP8X4),
                scales=y_scales[4 * g : P, regions(rt, count)],
                in_=y_bf16[g][:, regions(rt, count), :].rearrange("p r t -> p (r t)"),
            )

        def y_turn(rt, g):
            bank = take(("y", rt, g))
            for t in range(4):
                nc.tensor.transpose(bank[:, P * t : P * (t + 1)], y_t[g][:, t, regions(rt)], ident[:])

        def y_copy(rt, g, copy=nc.scalar.copy):
            copy(
                out=y_rows[rt][:, GROUP * g : GROUP * (g + 1)].rearrange("r (p t) -> r p t", t=4),
                in_=bank_of(("y", rt, g))[:].rearrange("r (t p) -> r p t", t=4),
            )
            give_back(("y", rt, g))

        def store_y(rt, g, queue=nc.sync):
            cols = slice(GROUP * g, GROUP * (g + 1))
            queue.dma_start(out=out_0[regions(rt), cols], in_=y_rows[rt][:, cols])

        def y_leave(rt, g):
            y_turn(rt, g)
            y_copy(rt, g)
            store_y(rt, g)

        def store_codes(rt, count, queue):
            cols = regions(rt, count)
            queue.dma_start(out=codes_hbm[:, :, cols], in_=y_codes[:, :, cols].bitcast(I32))

        def store_scales(rt, count, queue):
            for q in range(4):
                queue.dma_start(out=scales_hbm[:, 4 * q : 4 * q + 4, :], in_=y_scales[32 * q : 32 * q + 8].bitcast(I32))

        low, high = (0, 1), (2, 3)
        pairs = [(g, slices) for g in range(2) for slices in (low, high)]

        order = [(rt, c) for c in range(CHUNKS) for rt in range(TILES)]
        make_identity(nc, ident[:])
        clear(s1_tiles[0])
        clear(s1_tiles[1])
        clear(s1_tiles[2])
        load_s1(nc.gpsimd, 1)
        load_b1()
        for b in order[:4]:
            load_x(b)
        load_w1(0)
        load_s1(nc.sync, 0)
        for b in order[4:10]:
            load_x(b)
        load_w1(1)
        load_s1(nc.sync, 2)
        for b in order[10:14]:
            load_x(b)
        load_w1(2)
        for b in order[14:]:
            load_x(b)
        load_w1(3)

        def passes(run):
            for rt, c in run:
                mm1_half(rt, 0, [2 * c, 2 * c + 1])

        spread_b1()
        x_sort(order[0])
        x_sort(order[1])
        clear(s2_raw)
        x_sort(order[2])
        x_sort(order[3])
        x_turn(*order[0:4])
        x_quant(*order[0:2])
        passes(order[0:2])
        x_quant(order[2])
        x_sort(order[4])
        x_quant(order[3])
        x_sort(order[5])
        clear(s1_tiles[3])
        load_w1(4)
        load_s1(nc.sync, 3)
        load_w1(5)
        load_w1(6)
        load_scale_rows(nc.sync, s2_raw, s2_hbm)
        load_w1(7)
        for h in range(2):
            load_w2(h)
        load_vec(nc.sync, "b2", b2)
        load_vec(nc.sync, "shift", shift)
        load_vec(nc.sync, "gain", gain)
        x_turn(*order[4:6])
        passes(order[2:4])
        for start in (6, 10):
            x_sort(*order[start : start + 4])
            x_turn(*order[start : start + 4])
            x_quant(*order[start - 2 : start + 2])
            passes(order[start - 2 : start + 2])
        x_sort(*order[14:])
        x_turn(*order[14:])
        x_quant(*order[12:])
        passes(order[12:14])
        mm1_half(0, 1, [0, 1])
        passes(order[14:])
        for rt in range(TILES):
            h_add(rt, 0)
        mm1_half(1, 1, [0, 1])
        for c in range(1, CHUNKS):
            for rt in range(2):
                mm1_half(rt, 1, [2 * c, 2 * c + 1])
        for h in range(2):
            w2_sort_scales(h)
        for rt in range(2):
            h_add(rt, 1)
        for h in range(2):
            w2_sort_words(h, nc.vector.tensor_copy)
        mm1_half(2, 1, [0, 1])
        h_turn((0, 0), (1, 0))
        h_relu(0, 2, 0, SCALAR)
        h_turn((2, 0), (3, 0))
        h_turn((0, 1), (1, 1))
        h_relu(0, 2, 1, VECTOR)
        h_relu(2, 2, 0, SCALAR)
        mm1_half(2, 1, range(2, 8))
        h_quant(0, 2, 0)
        h_quant(0, 2, 1)
        mm1_half(3, 1, range(0, 1))
        h_add(2, 1)
        h_quant(2, 2, 0)
        for i, (g, slices) in enumerate(pairs):
            for h in range(2):
                z_passes(0, 2, g, slices, h)
            a_relu(0, 2, g, slices, VECTOR if i == 1 else SCALAR)
        for g, slices in pairs:
            y_affine(0, 2, g, slices)
        mm1_half(3, 1, range(1, 4))
        h_turn((2, 1))
        h_relu(2, 1, 1, SCALAR)
        for rt, g in [(0, 0), (1, 0), (0, 1)]:
            y_leave(rt, g)
        y_round(0, 2, 0)
        h_quant(2, 1, 1)
        y_round(0, 2, 1)
        y_quant(0, 2, 0)
        mm1_half(3, 1, range(4, 8))
        h_add(3, 1, (0, 1))
        y_quant(0, 2, 1)
        store_codes(0, 2, nc.sync)
        for g, slices in pairs:
            for h in range(2):
                z_passes(2, 1, g, slices, h)
            a_relu(2, 1, g, slices, SCALAR)
        y_affine(2, 1, 0, low + high)
        h_turn((3, 1))
        h_relu(3, 1, 1, VECTOR)
        y_leave(1, 1)
        y_leave(2, 0)
        y_affine(2, 1, 1, low)
        h_quant(3, 1, 1)
        y_affine(2, 1, 1, high)
        y_round(2, 1, 0)
        y_round(2, 1, 1)
        y_quant(2, 1, 0)
        for g, slices in pairs:
            z_passes(3, 1, g, slices, 0)
        for i, (g, slices) in enumerate(pairs):
            z_passes(3, 1, g, slices, 1)
            a_relu(3, 1, g, slices, VECTOR if i == 1 else SCALAR)
        y_quant(2, 1, 1)
        store_codes(2, 1, nc.sync)
        y_affine(3, 1, 0, low + high)
        y_affine(3, 1, 1, low + high)
        y_leave(2, 1)
        y_leave(3, 0)
        for g in range(2):
            y_round(3, 1, g)
        y_turn(3, 1)
        y_copy(3, 1)
        for g in range(2):
            y_quant(3, 1, g)
        store_y(3, 1)
        store_codes(3, 1, nc.scalar)
        store_scales(0, 4, nc.scalar)
